import numpy as np
import ml_dtypes


def mxq(x, axis, fmt="e4m3"):
    dtype, down = {"e4m3": (ml_dtypes.float8_e4m3fn, 7), "e5m2": (ml_dtypes.float8_e5m2, 14)}[fmt]
    v = np.moveaxis(np.asarray(x, np.float32).astype(ml_dtypes.bfloat16).astype(np.float64), axis, -1)
    blocks = v.reshape(v.shape[:-1] + (-1, 32))
    amax = np.abs(blocks).max(-1, keepdims=True)
    byte = np.maximum(np.where(amax > 0, np.frexp(amax)[1] - 1 + 127, 0) - down, 1)
    scale = np.exp2(byte - 127.0)
    codes = (blocks / scale).astype(np.float32).astype(dtype).astype(np.float64)
    return np.moveaxis((codes * scale).reshape(v.shape), -1, axis)


WIDE = False


def mx_kscale(k):
    if not WIDE:
        return np.ones(k)
    levels = np.array([10, -10, 5, -5, 0])
    if k % 512:
        return np.exp2(np.random.permutation(np.resize(levels, k // 32))).repeat(32)
    a = np.empty((k // 512, 16))
    for p in range(k // 512):
        a[p, :8] = np.random.permutation(np.resize(levels, 8))
        for g in range(8):
            far = levels[np.abs(levels - a[p, g]) >= 10]
            a[p, g + 8] = far[np.random.randint(len(far))]
    return np.exp2(a.ravel()).repeat(32)


def f64(x):
    return np.asarray(x).astype(np.float64)


def striped(idx):
    return np.tile(np.asarray(idx).reshape(-1, 16).T, (8, 1)).astype(np.uint16)


def unstriped(offs):
    return offs[:16].T.reshape(-1).astype(np.int64)


B, N, T, D, DV, NQ = 1, 1024, 4096, 512, 256, 128


def setup_inputs():
    n = np.random.standard_normal
    idx = np.sort(np.random.permutation(T)[:B * N].reshape(B, N), axis=1).reshape(-1)
    s = mx_kscale(D)[:, None]
    u = np.ones(T)
    u[idx] = mx_kscale(B * N)
    r = np.random.uniform(0.5, 2.0, T)
    k = n((D, T)) / s
    v = n((DV, T)) / (u * r)
    when = np.zeros(T)
    when[idx] = np.sort(np.random.permutation(2 * N)[:B * N])
    return {
        "qT": (n((B, D, NQ)) * s * (0.60 / np.sqrt(D))).astype(np.float32),
        "kT": k.astype(np.float32),
        "vT": v.astype(np.float32),
        "vs": np.tile(u * r, (128, 1)).astype(np.float32),
        "pos": np.tile(when, (128, 1)).astype(np.float32),
        "slope": np.exp2(-np.random.randint(8, 13, (B, NQ, 1))).astype(np.float32),
        "og": n((B, NQ, DV)).astype(np.float32),
        "offs": striped(idx),
    }


def reference(qT, kT, vT, vs, pos, slope, og, offs):
    idx = unstriped(offs)
    k = f64(kT)
    v = f64(vT)
    pick = lambda x: x[:, idx].reshape(x.shape[0], B, N).transpose(1, 0, 2)
    q = f64(qT)
    score = mxq(q, 1, "e4m3").transpose(0, 2, 1) @ mxq(pick(k), 1, "e4m3")
    score = score + f64(slope) * pick(f64(pos))[:, :1, :]
    m = score.max(-1, keepdims=True)
    p = np.exp(score - m)
    total = p.sum(-1, keepdims=True)
    w = p * pick(f64(vs))[:, :1, :]
    y = mxq(w, 2, "e4m3") @ mxq(pick(v).transpose(0, 2, 1), 1, "e4m3")
    y = y / total
    y = y / (1.0 + np.exp(-f64(og)))
    return y

@@ -1,0 +1,229 @@
+from contextlib import ExitStack
+
+import concourse.mybir as mybir
+from concourse.masks import make_identity
+
+F32 = mybir.dt.float32
+BF16 = mybir.dt.bfloat16
+U32 = mybir.dt.uint32
+U16 = mybir.dt.uint16
+U8 = mybir.dt.uint8
+FP8X4 = mybir.dt.float8_e4m3fn_x4
+ACT = mybir.ActivationFunctionType
+ALU = mybir.AluOpType
+AX = mybir.AxisListType
+
+P = 128
+D = 512
+DV = 256
+T = 4096
+N = 1024
+HALF = 512
+FIRST = T - HALF
+FLOPS = 2 * N * D * P + 2 * N * P * DV
+BYTES = 4 * (D * P + D * T + DV * T + 2 * T + P + 2 * P * DV) + 2 * P * (N // 16)
+
+
+def tile_attend_x_alibi_gate_srt_kernel(tc, qT, kT, vT, vs, pos, slope, og, offs, out):
+    nc = tc.nc
+    with ExitStack() as ctx:
+        keep = ctx.enter_context(tc.tile_pool(name="keep", bufs=1))
+        banks = ctx.enter_context(tc.psum_pool(name="banks", bufs=1))
+
+        offsets = keep.tile([P, N // 16], U16, name="offsets")
+        nc.sync.dma_start(offsets[:], offs)
+
+        pos_row = keep.tile([P, T], F32, name="pos_row")
+        vs_row = keep.tile([P, T], F32, name="vs_row")
+        kp = [keep.tile([P, T], F32, name=f"k_plane{t}") for t in range(4)]
+        vp = [keep.tile([P, T], F32, name=f"v_plane{e}") for e in range(2)]
+        k_planes = kT.rearrange("(p t) n -> p t n", t=4)
+
+        nc.vector.memset(pos_row[:], 0.0)
+        nc.gpsimd.memset(vs_row[:], 0.0)
+        nc.vector.memset(kp[0][:, T // 2 : T // 2 + 8], 0.0)
+        for plane in (kp[1], kp[2], kp[3], vp[0], vp[1]):
+            nc.gpsimd.memset(plane[:, 0:8], 0.0)
+        ident = keep.tile([P, P], F32, name="ident")
+        make_identity(nc, ident[:])
+        ident_b = keep.tile([P, P], BF16, name="ident_b")
+        make_identity(nc, ident_b[:])
+
+        q_raw = keep.tile([P, 4, P], F32, name="q_raw")
+        nc.scalar.dma_start(q_raw[:], qT[0].rearrange("(p t) q -> p t q", t=4))
+        og_sb = keep.tile([P, DV], F32, name="og_sb")
+        nc.scalar.dma_start(og_sb[:], og[0])
+        slope_sb = keep.tile([P, 1], F32, name="slope_sb")
+        nc.scalar.dma_start(slope_sb[:], slope[0])
+        nc.sync.dma_start(kp[0][:, : T // 2], k_planes[:, 0, : T // 2])
+        nc.sync.dma_start(pos_row[0:1, :], pos[0:1, :])
+        nc.sync.dma_start(kp[0][:, T // 2 :], k_planes[:, 0, T // 2 :])
+        nc.sync.dma_start(vs_row[0:1, :], vs[0:1, :])
+        for t in range(1, 4):
+            if t < 3:
+                nc.sync.dma_start(kp[t][:], k_planes[:, t, :])
+            else:
+                nc.sync.dma_start(kp[t][:, :FIRST], k_planes[:, t, :FIRST])
+                nc.sync.dma_start(kp[t][:, FIRST:], k_planes[:, t, FIRST:])
+        nc.sync.dma_start(vp[0][:], vT[0:P, :])
+        nc.sync.dma_start(vp[1][:, :FIRST], vT[P : 2 * P, :FIRST])
+        nc.sync.dma_start(vp[1][:, FIRST:], vT[P : 2 * P, FIRST:])
+
+        gate = keep.tile([P, DV], F32, name="gate")
+        nc.scalar.activation(gate[:], og_sb[:], ACT.Sigmoid)
+        warm = keep.tile([P, 1], F32, name="warm")
+        nc.scalar.activation(warm[:], slope_sb[:], ACT.Exp)
+
+        q_grp = keep.tile([P, P, 4], BF16, name="q_grp", align_bytes=64)
+        nc.scalar.copy(q_grp[:], q_raw[:].rearrange("p t q -> p q t"))
+        q_codes = keep.tile([P, P], U32, name="q_codes", align_bytes=64)
+        q_scales = keep.tile([P, P], U8, name="q_scales", align_bytes=64)
+        nc.vector.quantize_mx(
+            out=q_codes[:].bitcast(FP8X4),
+            scales=q_scales[:],
+            in_=q_grp[:].rearrange("p q t -> p (q t)"),
+        )
+
+        pos_g = keep.tile([P, N], F32, name="pos_g")
+        nc.vector.tensor_copy(pos_g[:], pos_row[:].indirect(offsets[:]))
+        vs_g = keep.tile([P, N], F32, name="vs_g")
+        nc.vector.tensor_copy(vs_g[:], vs_row[:].indirect(offsets[:]))
+
+        cols = {}
+        for what, src in (("pos", pos_g), ("vs", vs_g)):
+            col = keep.tile([P, 2, 1, 4], F32, name=f"{what}_col")
+            for g in range(2):
+                turned = banks.tile([P, 4, P], F32, name="turned", tag="head", bufs=2)
+                for t in range(4):
+                    nc.tensor.transpose(turned[:, t, :], src[:, g * HALF + t : (g + 1) * HALF : 4], ident[:])
+                nc.vector.tensor_copy(col[:, g, 0, :], turned[:, :, 0])
+            cols[what] = col
+        bias = keep.tile([P, 2, 4, P], F32, name="bias")
+        for g in range(2):
+            spread = banks.tile([P, 4, P], F32, name="spread", tag="head", bufs=2)
+            for t in range(4):
+                nc.tensor.transpose(
+                    spread[:, t, :], cols["pos"][:, g, 0, t : t + 1].to_broadcast([P, P]), ident[:]
+                )
+            nc.scalar.activation(bias[:, g], spread[:], ACT.Copy, scale=slope_sb[:])
+
+        k_grp = keep.tile([P, N, 4], BF16, name="k_grp", align_bytes=64)
+        k_pair = keep.tile([P, 2, N], F32, name="k_pair")
+        for t in range(2):
+            nc.vector.tensor_copy(k_pair[:, t, :], kp[t][:].indirect(offsets[:]))
+        for h in range(2):
+            c = slice(h * HALF, (h + 1) * HALF)
+            nc.scalar.activation(k_grp[:, c, 0:2], k_pair[:, :, c].rearrange("p t n -> p n t"), ACT.Copy)
+        nc.vector.tensor_copy(k_grp[:, :, 2], kp[2][:].indirect(offsets[:]))
+        for h in range(2):
+            nc.vector.tensor_copy(
+                k_grp[:, h * HALF : (h + 1) * HALF, 3],
+                kp[3][:, : (FIRST, T)[h]].indirect(offsets[:, h * 32 : (h + 1) * 32]),
+            )
+        k_codes = keep.tile([P, N], U32, name="k_codes", align_bytes=64)
+        k_scales = keep.tile([P, N], U8, name="k_scales", align_bytes=64)
+        score = []
+        for h in range(2):
+            c = slice(h * HALF, (h + 1) * HALF)
+            nc.vector.quantize_mx(
+                out=k_codes[:, c].bitcast(FP8X4),
+                scales=k_scales[:, c],
+                in_=k_grp[:, c, :].rearrange("p n t -> p (n t)"),
+            )
+            s_ps = banks.tile([P, HALF], F32, name=f"s_ps{h}")
+            nc.tensor.matmul_mx(
+                out=s_ps[:],
+                lhsT=q_codes[:].bitcast(FP8X4),
+                lhsT_scale=q_scales[:],
+                rhs=k_codes[:, c].bitcast(FP8X4),
+                rhs_scale=k_scales[:, c],
+                start=True,
+                stop=True,
+            )
+            score.append(s_ps)
+
+        s_sb = keep.tile([P, 2, 4, P], F32, name="s_sb")
+        for h in range(2):
+            nc.vector.tensor_tensor(
+                s_sb[:, h], score[h][:].rearrange("q (p t) -> q t p", t=4), bias[:, h], ALU.add
+            )
+        neg_max = keep.tile([P, 1], F32, name="neg_max")
+        nc.vector.tensor_reduce(
+            neg_max[:], s_sb[:].rearrange("q h t p -> q (h t p)"), AX.X, ALU.max, negate=True
+        )
+        prob = keep.tile([P, 2, 4, P], F32, name="prob")
+        sums = keep.tile([P, 2], F32, name="sums")
+        for h in range(2):
+            nc.scalar.activation(
+                prob[:, h], s_sb[:, h], ACT.Exp, bias=neg_max[:], accum_out=sums[:, h : h + 1]
+            )
+
+        w_codes = keep.tile([P, 2, P], U32, name="w_codes", align_bytes=64)
+        w_scales = keep.tile([P, 2, P], U8, name="w_scales", align_bytes=64)
+        v_codes = [keep.tile([P, 2, P], U32, name=f"v_codes{e}", align_bytes=64) for e in range(2)]
+        v_scales = [keep.tile([P, 2, P], U8, name=f"v_scales{e}", align_bytes=64) for e in range(2)]
+        v_g = [keep.tile([P, 2, 4, P], BF16, name=f"v_g{e}") for e in range(2)]
+        v_grp = [keep.tile([P, 2, P, 4], BF16, name=f"v_grp{e}", align_bytes=64) for e in range(2)]
+        w_grp = keep.tile([P, 2, P, 4], BF16, name="w_grp", align_bytes=64)
+
+        def gather_values(e, g):
+            nc.vector.tensor_copy(
+                v_g[e][:, g].rearrange("p t m -> p m t"),
+                vp[e][:, : (FIRST, T)[g]].indirect(offsets[:, g * 32 : (g + 1) * 32]),
+            )
+
+        def turn_values(e, g):
+            v_ps = banks.tile([P, 4, P], BF16, name="v_ps", tag="turn", bufs=4)
+            for t in range(4):
+                nc.tensor.transpose(v_ps[:, t, :], v_g[e][:, g, t, :], ident_b[:])
+            nc.scalar.copy(v_grp[e][:, g], v_ps[:].rearrange("p t e -> p e t"))
+
+        def quantise(codes, scales, grouped):
+            nc.vector.quantize_mx(out=codes.bitcast(FP8X4), scales=scales, in_=grouped)
+
+        gather_values(0, 0)
+        gather_values(0, 1)
+        total = keep.tile([P, 1], F32, name="total")
+        nc.vector.tensor_tensor(total[:], sums[:, 0:1], sums[:, 1:2], ALU.add)
+        inv = keep.tile([P, 1], F32, name="inv")
+        nc.vector.reciprocal(inv[:], total[:])
+        for g in range(2):
+            p_ps = banks.tile([P, 4, P], F32, name="p_ps", tag="turn", bufs=4)
+            for t in range(4):
+                nc.tensor.transpose(p_ps[:, t, :], prob[:, g, t, :], ident[:])
+            nc.vector.tensor_tensor(
+                w_grp[:, g],
+                p_ps[:].rearrange("p t q -> p q t"),
+                cols["vs"][:, g].to_broadcast([P, P, 4]),
+                ALU.mult,
+            )
+        turn_values(0, 0)
+        turn_values(0, 1)
+        for g in range(2):
+            quantise(w_codes[:, g], w_scales[:, g], w_grp[:, g].rearrange("p q t -> p (q t)"))
+        gather_values(1, 0)
+        gather_values(1, 1)
+        quantise(
+            v_codes[0][:].rearrange("p g e -> p (g e)"),
+            v_scales[0][:].rearrange("p g e -> p (g e)"),
+            v_grp[0][:].rearrange("p g e t -> p (g e t)"),
+        )
+        for g in range(2):
+            turn_values(1, g)
+            quantise(v_codes[1][:, g], v_scales[1][:, g], v_grp[1][:, g].rearrange("p e t -> p (e t)"))
+
+        y_sb = keep.tile([P, DV], F32, name="y_sb")
+        y_ps = banks.tile([P, DV], F32, name="y_ps", tag="head", bufs=2)
+        for e in range(2):
+            for g in range(2):
+                nc.tensor.matmul_mx(
+                    out=y_ps[:, e * P : (e + 1) * P],
+                    lhsT=w_codes[:, g].bitcast(FP8X4),
+                    lhsT_scale=w_scales[:, g],
+                    rhs=v_codes[e][:, g].bitcast(FP8X4),
+                    rhs_scale=v_scales[e][:, g],
+                    start=(g == 0),
+                    stop=(g == 1),
+                )
+        nc.vector.scalar_tensor_tensor(y_sb[:], y_ps[:], inv[:], gate[:], ALU.mult, ALU.mult)
+        nc.sync.dma_start(out[0], y_sb[:])

@@ -7,6 +7,7 @@ F32 = mybir.dt.float32
 BF16 = mybir.dt.bfloat16
 U32 = mybir.dt.uint32
 U16 = mybir.dt.uint16
+I32 = mybir.dt.int32
 U8 = mybir.dt.uint8
 FP8X4 = mybir.dt.float8_e4m3fn_x4
 ACT = mybir.ActivationFunctionType
@@ -33,17 +34,17 @@ def tile_attend_x_alibi_gate_srt_kernel(tc, qT, kT, vT, vs, pos, slope, og, offs
         offsets = keep.tile([P, N // 16], U16, name="offsets")
         nc.sync.dma_start(offsets[:], offs)
 
-        pos_row = keep.tile([P, T], F32, name="pos_row")
-        vs_row = keep.tile([P, T], F32, name="vs_row")
-        kp = [keep.tile([P, T], F32, name=f"k_plane{t}") for t in range(4)]
-        vp = [keep.tile([P, T], F32, name=f"v_plane{e}") for e in range(2)]
-        k_planes = kT.rearrange("(p t) n -> p t n", t=4)
+        def buffer(b, name, shape=(P, T), dtype=F32):
+            return keep.tile(list(shape), dtype, name=name, tag=f"buffer{b}", bufs=1, align_bytes=64)
 
-        nc.vector.memset(pos_row[:], 0.0)
-        nc.gpsimd.memset(vs_row[:], 0.0)
-        nc.vector.memset(kp[0][:, T // 2 : T // 2 + 8], 0.0)
-        for plane in (kp[1], kp[2], kp[3], vp[0], vp[1]):
-            nc.gpsimd.memset(plane[:, 0:8], 0.0)
+        pos_row = buffer(0, "pos_row")
+        vs_row = buffer(1, "vs_row")
+        k_planes = kT.rearrange("(p t) n -> p t n", t=4)
+        kp = [buffer(2, "k_plane0")]
+        q_grp = buffer(3, "q_grp", (P, P, 4), BF16)
+
+        nc.vector.memset(pos_row[:].bitcast(I32), 0)
+        nc.vector.memset(vs_row[:].bitcast(I32), 0)
         ident = keep.tile([P, P], F32, name="ident")
         make_identity(nc, ident[:])
         ident_b = keep.tile([P, P], BF16, name="ident_b")
@@ -55,26 +56,18 @@ def tile_attend_x_alibi_gate_srt_kernel(tc, qT, kT, vT, vs, pos, slope, og, offs
         nc.scalar.dma_start(og_sb[:], og[0])
         slope_sb = keep.tile([P, 1], F32, name="slope_sb")
         nc.scalar.dma_start(slope_sb[:], slope[0])
-        nc.sync.dma_start(kp[0][:, : T // 2], k_planes[:, 0, : T // 2])
-        nc.sync.dma_start(pos_row[0:1, :], pos[0:1, :])
-        nc.sync.dma_start(kp[0][:, T // 2 :], k_planes[:, 0, T // 2 :])
-        nc.sync.dma_start(vs_row[0:1, :], vs[0:1, :])
-        for t in range(1, 4):
-            if t < 3:
-                nc.sync.dma_start(kp[t][:], k_planes[:, t, :])
-            else:
-                nc.sync.dma_start(kp[t][:, :FIRST], k_planes[:, t, :FIRST])
-                nc.sync.dma_start(kp[t][:, FIRST:], k_planes[:, t, FIRST:])
-        nc.sync.dma_start(vp[0][:], vT[0:P, :])
-        nc.sync.dma_start(vp[1][:, :FIRST], vT[P : 2 * P, :FIRST])
-        nc.sync.dma_start(vp[1][:, FIRST:], vT[P : 2 * P, FIRST:])
+        nc.sync.dma_start(kp[0][:], k_planes[:, 0, :])
+        for row, src, first in ((pos_row, pos, 0), (vs_row, vs, 4)):
+            for u in range(2):
+                c = slice(u * T // 2, (u + 1) * T // 2)
+                at = first + 64 * u
+                nc.sync.dma_start(row[at : at + 1, c], src[0:1, c])
 
         gate = keep.tile([P, DV], F32, name="gate")
         nc.scalar.activation(gate[:], og_sb[:], ACT.Sigmoid)
         warm = keep.tile([P, 1], F32, name="warm")
         nc.scalar.activation(warm[:], slope_sb[:], ACT.Exp)
 
-        q_grp = keep.tile([P, P, 4], BF16, name="q_grp", align_bytes=64)
         nc.scalar.copy(q_grp[:], q_raw[:].rearrange("p t q -> p q t"))
         q_codes = keep.tile([P, P], U32, name="q_codes", align_bytes=64)
         q_scales = keep.tile([P, P], U8, name="q_scales", align_bytes=64)
@@ -84,19 +77,40 @@ def tile_attend_x_alibi_gate_srt_kernel(tc, qT, kT, vT, vs, pos, slope, og, offs
             in_=q_grp[:].rearrange("p q t -> p (q t)"),
         )
 
+        def load(tile, src, cut):
+            if cut:
+                nc.sync.dma_start(tile[:, :FIRST], src[:, :FIRST])
+                nc.sync.dma_start(tile[:, FIRST:], src[:, FIRST:])
+            else:
+                nc.sync.dma_start(tile[:], src)
+
+        kp.append(buffer(3, "k_plane1"))
+        load(kp[1], k_planes[:, 1, :], False)
+        k_pair = keep.tile([P, 2, N], F32, name="k_pair")
+        nc.vector.tensor_copy(k_pair[:, 0, :], kp[0][:].indirect(offsets[:]))
+        kp.append(buffer(2, "k_plane2"))
+        load(kp[2], k_planes[:, 2, :], False)
+
         pos_g = keep.tile([P, N], F32, name="pos_g")
         nc.vector.tensor_copy(pos_g[:], pos_row[:].indirect(offsets[:]))
+        kp.append(buffer(0, "k_plane3"))
+        load(kp[3], k_planes[:, 3, :], True)
         vs_g = keep.tile([P, N], F32, name="vs_g")
         nc.vector.tensor_copy(vs_g[:], vs_row[:].indirect(offsets[:]))
+        vp = [buffer(1, "v_plane0")]
+        load(vp[0], vT[0:P, :], False)
+        nc.vector.tensor_copy(k_pair[:, 1, :], kp[1][:].indirect(offsets[:]))
+        vp.append(buffer(3, "v_plane1"))
+        load(vp[1], vT[P : 2 * P, :], True)
 
         cols = {}
-        for what, src in (("pos", pos_g), ("vs", vs_g)):
+        for what, src, first in (("pos", pos_g, 0), ("vs", vs_g, 4)):
             col = keep.tile([P, 2, 1, 4], F32, name=f"{what}_col")
             for g in range(2):
                 turned = banks.tile([P, 4, P], F32, name="turned", tag="head", bufs=2)
                 for t in range(4):
                     nc.tensor.transpose(turned[:, t, :], src[:, g * HALF + t : (g + 1) * HALF : 4], ident[:])
-                nc.vector.tensor_copy(col[:, g, 0, :], turned[:, :, 0])
+                nc.vector.tensor_reduce(col[:, g, 0, :], turned[:, :, first : P : 64], AX.X, ALU.add)
             cols[what] = col
         bias = keep.tile([P, 2, 4, P], F32, name="bias")
         for g in range(2):
@@ -108,9 +122,6 @@ def tile_attend_x_alibi_gate_srt_kernel(tc, qT, kT, vT, vs, pos, slope, og, offs
             nc.scalar.activation(bias[:, g], spread[:], ACT.Copy, scale=slope_sb[:])
 
         k_grp = keep.tile([P, N, 4], BF16, name="k_grp", align_bytes=64)
-        k_pair = keep.tile([P, 2, N], F32, name="k_pair")
-        for t in range(2):
-            nc.vector.tensor_copy(k_pair[:, t, :], kp[t][:].indirect(offsets[:]))
         for h in range(2):
             c = slice(h * HALF, (h + 1) * HALF)
             nc.scalar.activation(k_grp[:, c, 0:2], k_pair[:, :, c].rearrange("p t n -> p n t"), ACT.Copy)

@@ -7,7 +7,6 @@ F32 = mybir.dt.float32
 BF16 = mybir.dt.bfloat16
 U32 = mybir.dt.uint32
 U16 = mybir.dt.uint16
-I32 = mybir.dt.int32
 U8 = mybir.dt.uint8
 FP8X4 = mybir.dt.float8_e4m3fn_x4
 ACT = mybir.ActivationFunctionType
@@ -21,6 +20,7 @@ T = 4096
 N = 1024
 HALF = 512
 FIRST = T - HALF
+CHUNKS = [slice(0, 1024), slice(1024, 2048), slice(2048, 3072), slice(3072, FIRST), slice(FIRST, T)]
 FLOPS = 2 * N * D * P + 2 * N * P * DV
 BYTES = 4 * (D * P + D * T + DV * T + 2 * T + P + 2 * P * DV) + 2 * P * (N // 16)
 
@@ -34,8 +34,10 @@ def tile_attend_x_alibi_gate_srt_kernel(tc, qT, kT, vT, vs, pos, slope, og, offs
         offsets = keep.tile([P, N // 16], U16, name="offsets")
         nc.sync.dma_start(offsets[:], offs)
 
-        def buffer(b, name, shape=(P, T), dtype=F32):
-            return keep.tile(list(shape), dtype, name=name, tag=f"buffer{b}", bufs=1, align_bytes=64)
+        planes = ctx.enter_context(tc.tile_pool(name="planes", bufs=1))
+
+        def buffer(b, name, shape=(P, T), dtype=F32, at=0):
+            return planes.tile(list(shape), dtype, name=name, align_bytes=64, offset=4 * T * b + at)
 
         pos_row = buffer(0, "pos_row")
         vs_row = buffer(1, "vs_row")
@@ -43,12 +45,11 @@ def tile_attend_x_alibi_gate_srt_kernel(tc, qT, kT, vT, vs, pos, slope, og, offs
         kp = [buffer(2, "k_plane0")]
         q_grp = buffer(3, "q_grp", (P, P, 4), BF16)
 
-        nc.vector.memset(pos_row[:].bitcast(I32), 0)
-        nc.vector.memset(vs_row[:].bitcast(I32), 0)
+        nc.gpsimd.memset(vs_row[:], 0.0)
+        nc.vector.memset(pos_row[:, : T - 1], 0.0)
+        nc.vector.memset(pos_row[:, T - 1 :], 0.0)
         ident = keep.tile([P, P], F32, name="ident")
         make_identity(nc, ident[:])
-        ident_b = keep.tile([P, P], BF16, name="ident_b")
-        make_identity(nc, ident_b[:])
 
         q_raw = keep.tile([P, 4, P], F32, name="q_raw")
         nc.scalar.dma_start(q_raw[:], qT[0].rearrange("(p t) q -> p t q", t=4))
@@ -57,11 +58,11 @@ def tile_attend_x_alibi_gate_srt_kernel(tc, qT, kT, vT, vs, pos, slope, og, offs
         slope_sb = keep.tile([P, 1], F32, name="slope_sb")
         nc.scalar.dma_start(slope_sb[:], slope[0])
         nc.sync.dma_start(kp[0][:], k_planes[:, 0, :])
-        for row, src, first in ((pos_row, pos, 0), (vs_row, vs, 4)):
+        for row, src, first, queue in ((pos_row, pos, 0, nc.sync), (vs_row, vs, 4, nc.scalar)):
             for u in range(2):
                 c = slice(u * T // 2, (u + 1) * T // 2)
                 at = first + 64 * u
-                nc.sync.dma_start(row[at : at + 1, c], src[0:1, c])
+                queue.dma_start(row[at : at + 1, c], src[0:1, c])
 
         gate = keep.tile([P, DV], F32, name="gate")
         nc.scalar.activation(gate[:], og_sb[:], ACT.Sigmoid)
@@ -98,7 +99,9 @@ def tile_attend_x_alibi_gate_srt_kernel(tc, qT, kT, vT, vs, pos, slope, og, offs
         vs_g = keep.tile([P, N], F32, name="vs_g")
         nc.vector.tensor_copy(vs_g[:], vs_row[:].indirect(offsets[:]))
         vp = [buffer(1, "v_plane0")]
-        load(vp[0], vT[0:P, :], False)
+        v_cast = keep.tile([P, T], BF16, name="v_cast")
+        for c in CHUNKS:
+            nc.sync.dma_start(vp[0][:, c], vT[0:P, c])
         nc.vector.tensor_copy(k_pair[:, 1, :], kp[1][:].indirect(offsets[:]))
         vp.append(buffer(3, "v_plane1"))
         load(vp[1], vT[P : 2 * P, :], True)
@@ -153,7 +156,10 @@ def tile_attend_x_alibi_gate_srt_kernel(tc, qT, kT, vT, vs, pos, slope, og, offs
             )
             score.append(s_ps)
 
-        s_sb = keep.tile([P, 2, 4, P], F32, name="s_sb")
+        for c in CHUNKS:
+            nc.scalar.activation(v_cast[:, c], vp[0][:, c], ACT.Copy)
+
+        s_sb = keep.tile([P, 2, 4, P], F32, name="s_sb", tag="scores")
         for h in range(2):
             nc.vector.tensor_tensor(
                 s_sb[:, h], score[h][:].rearrange("q (p t) -> q t p", t=4), bias[:, h], ALU.add
@@ -171,30 +177,36 @@ def tile_attend_x_alibi_gate_srt_kernel(tc, qT, kT, vT, vs, pos, slope, og, offs
 
         w_codes = keep.tile([P, 2, P], U32, name="w_codes", align_bytes=64)
         w_scales = keep.tile([P, 2, P], U8, name="w_scales", align_bytes=64)
-        v_codes = [keep.tile([P, 2, P], U32, name=f"v_codes{e}", align_bytes=64) for e in range(2)]
         v_scales = [keep.tile([P, 2, P], U8, name=f"v_scales{e}", align_bytes=64) for e in range(2)]
-        v_g = [keep.tile([P, 2, 4, P], BF16, name=f"v_g{e}") for e in range(2)]
+        v_g = [[keep.tile([P, 2, P, 2], BF16, name=f"v_g{e}{g}", tag="scores" if (e, g) == (0, 1) else f"v_g{e}{g}") for g in range(2)] for e in range(2)]
         v_grp = [keep.tile([P, 2, P, 4], BF16, name=f"v_grp{e}", align_bytes=64) for e in range(2)]
-        w_grp = keep.tile([P, 2, P, 4], BF16, name="w_grp", align_bytes=64)
 
         def gather_values(e, g):
-            nc.vector.tensor_copy(
-                v_g[e][:, g].rearrange("p t m -> p m t"),
-                vp[e][:, : (FIRST, T)[g]].indirect(offsets[:, g * 32 : (g + 1) * 32]),
-            )
+            dealt = v_g[e][g][:].rearrange("p u m i -> p m u i")
+            listed = offsets[:, g * 32 : (g + 1) * 32]
+            if e == 0:
+                nc.scalar.activation(dealt, v_cast[:, : (FIRST, T)[g]].indirect(listed), ACT.Copy)
+            else:
+                nc.vector.tensor_copy(dealt, vp[e][:, : (FIRST, T)[g]].indirect(listed))
 
         def turn_values(e, g):
-            v_ps = banks.tile([P, 4, P], BF16, name="v_ps", tag="turn", bufs=4)
-            for t in range(4):
-                nc.tensor.transpose(v_ps[:, t, :], v_g[e][:, g, t, :], ident_b[:])
-            nc.scalar.copy(v_grp[e][:, g], v_ps[:].rearrange("p t e -> p e t"))
+            v_ps = banks.tile([P, 2, P], F32, name="v_ps", tag="turn", bufs=4)
+            for u in range(2):
+                words = v_g[e][g][:, u].rearrange("p m i -> p (m i)").bitcast(F32)
+                nc.tensor.transpose(v_ps[:, u, :], words, ident[:])
+            grouped = v_grp[e][:, g].rearrange("p e t -> p (e t)").bitcast(F32)
+            nc.scalar.copy(grouped.rearrange("p (e u) -> p e u", u=2), v_ps[:].rearrange("p u e -> p e u"))
 
         def quantise(codes, scales, grouped):
             nc.vector.quantize_mx(out=codes.bitcast(FP8X4), scales=scales, in_=grouped)
 
         gather_values(0, 0)
         gather_values(0, 1)
-        total = keep.tile([P, 1], F32, name="total")
+        gather_values(1, 0)
+        gather_values(1, 1)
+        w_grp = buffer(3, "w_grp", (P, 2, P, 4), BF16)
+        v_codes = [buffer(3, f"v_codes{e}", (P, 2, P), U32, at=2048 + 1024 * e) for e in range(2)]
+        total = buffer(3, "total", (P, 1), F32, at=4096)
         nc.vector.tensor_tensor(total[:], sums[:, 0:1], sums[:, 1:2], ALU.add)
         inv = keep.tile([P, 1], F32, name="inv")
         nc.vector.reciprocal(inv[:], total[:])
@@ -212,8 +224,6 @@ def tile_attend_x_alibi_gate_srt_kernel(tc, qT, kT, vT, vs, pos, slope, og, offs
         turn_values(0, 1)
         for g in range(2):
             quantise(w_codes[:, g], w_scales[:, g], w_grp[:, g].rearrange("p q t -> p (q t)"))
-        gather_values(1, 0)
-        gather_values(1, 1)
         quantise(
             v_codes[0][:].rearrange("p g e -> p (g e)"),
             v_scales[0][:].rearrange("p g e -> p (g e)"),

@@ -20,7 +20,10 @@ T = 4096
 N = 1024
 HALF = 512
 FIRST = T - HALF
-CHUNKS = [slice(0, 1024), slice(1024, 2048), slice(2048, 3072), slice(3072, FIRST), slice(FIRST, T)]
+V_CASTS = [slice(0, 1024), slice(1024, 2048), slice(2048, 3072), slice(3072, FIRST)]
+V_LOADS = V_CASTS + [slice(FIRST, T)]
+K_CHUNKS = [slice(0, T // 2), slice(T // 2, T)]
+SPARE = 256
 FLOPS = 2 * N * D * P + 2 * N * P * DV
 BYTES = 4 * (D * P + D * T + DV * T + 2 * T + P + 2 * P * DV) + 2 * P * (N // 16)
 
@@ -37,13 +40,13 @@ def tile_attend_x_alibi_gate_srt_kernel(tc, qT, kT, vT, vs, pos, slope, og, offs
         planes = ctx.enter_context(tc.tile_pool(name="planes", bufs=1))
 
         def buffer(b, name, shape=(P, T), dtype=F32, at=0):
-            return planes.tile(list(shape), dtype, name=name, align_bytes=64, offset=4 * T * b + at)
+            return planes.tile(list(shape), dtype, name=name, align_bytes=64, offset=(4 * T + SPARE) * b + at)
 
         pos_row = buffer(0, "pos_row")
         vs_row = buffer(1, "vs_row")
         k_planes = kT.rearrange("(p t) n -> p t n", t=4)
         kp = [buffer(2, "k_plane0")]
-        q_grp = buffer(3, "q_grp", (P, P, 4), BF16)
+        q_grp = buffer(4, "q_grp", (P, P, 4), BF16, at=-4 * P)
 
         nc.gpsimd.memset(vs_row[:], 0.0)
         nc.vector.memset(pos_row[:, : T - 1], 0.0)
@@ -55,9 +58,8 @@ def tile_attend_x_alibi_gate_srt_kernel(tc, qT, kT, vT, vs, pos, slope, og, offs
         nc.scalar.dma_start(q_raw[:], qT[0].rearrange("(p t) q -> p t q", t=4))
         og_sb = keep.tile([P, DV], F32, name="og_sb")
         nc.scalar.dma_start(og_sb[:], og[0])
-        slope_sb = keep.tile([P, 1], F32, name="slope_sb")
-        nc.scalar.dma_start(slope_sb[:], slope[0])
-        nc.sync.dma_start(kp[0][:], k_planes[:, 0, :])
+        for c in K_CHUNKS:
+            nc.sync.dma_start(kp[0][:, c], k_planes[:, 0, c])
         for row, src, first, queue in ((pos_row, pos, 0, nc.sync), (vs_row, vs, 4, nc.scalar)):
             for u in range(2):
                 c = slice(u * T // 2, (u + 1) * T // 2)
@@ -67,7 +69,7 @@ def tile_attend_x_alibi_gate_srt_kernel(tc, qT, kT, vT, vs, pos, slope, og, offs
         gate = keep.tile([P, DV], F32, name="gate")
         nc.scalar.activation(gate[:], og_sb[:], ACT.Sigmoid)
         warm = keep.tile([P, 1], F32, name="warm")
-        nc.scalar.activation(warm[:], slope_sb[:], ACT.Exp)
+        nc.scalar.activation(warm[:], gate[:, 0:1], ACT.Exp)
 
         nc.scalar.copy(q_grp[:], q_raw[:].rearrange("p t q -> p q t"))
         q_codes = keep.tile([P, P], U32, name="q_codes", align_bytes=64)
@@ -87,10 +89,15 @@ def tile_attend_x_alibi_gate_srt_kernel(tc, qT, kT, vT, vs, pos, slope, og, offs
 
         kp.append(buffer(3, "k_plane1"))
         load(kp[1], k_planes[:, 1, :], False)
-        k_pair = keep.tile([P, 2, N], F32, name="k_pair")
-        nc.vector.tensor_copy(k_pair[:, 0, :], kp[0][:].indirect(offsets[:]))
-        kp.append(buffer(2, "k_plane2"))
+        k_pair = keep.tile([P, 2 * N], BF16, name="k_pair")
+        k_cast = keep.tile([P, T], BF16, name="k_cast", tag="cast")
+        for c in K_CHUNKS:
+            nc.scalar.activation(k_cast[:, c], kp[0][:, c], ACT.Copy)
+        nc.scalar.activation(k_pair[:, :N], k_cast[:].indirect(offsets[:]), ACT.Copy)
+        kp.append(buffer(4, "k_plane2"))
         load(kp[2], k_planes[:, 2, :], False)
+        slope_sb = buffer(4, "slope_sb", (P, 1), at=-128)
+        nc.sync.dma_start(slope_sb[:], slope[0])
 
         pos_g = keep.tile([P, N], F32, name="pos_g")
         nc.vector.tensor_copy(pos_g[:], pos_row[:].indirect(offsets[:]))
@@ -98,43 +105,48 @@ def tile_attend_x_alibi_gate_srt_kernel(tc, qT, kT, vT, vs, pos, slope, og, offs
         load(kp[3], k_planes[:, 3, :], True)
         vs_g = keep.tile([P, N], F32, name="vs_g")
         nc.vector.tensor_copy(vs_g[:], vs_row[:].indirect(offsets[:]))
-        vp = [buffer(1, "v_plane0")]
-        v_cast = keep.tile([P, T], BF16, name="v_cast")
-        for c in CHUNKS:
+        nc.vector.tensor_copy(k_pair[:, N:], kp[1][:].indirect(offsets[:]))
+        vp = [buffer(3, "v_plane0", at=128)]
+        v_cast = keep.tile([P, FIRST], BF16, name="v_cast", tag="cast")
+        for c in V_LOADS:
             nc.sync.dma_start(vp[0][:, c], vT[0:P, c])
-        nc.vector.tensor_copy(k_pair[:, 1, :], kp[1][:].indirect(offsets[:]))
-        vp.append(buffer(3, "v_plane1"))
-        load(vp[1], vT[P : 2 * P, :], True)
 
-        cols = {}
-        for what, src, first in (("pos", pos_g, 0), ("vs", vs_g, 4)):
-            col = keep.tile([P, 2, 1, 4], F32, name=f"{what}_col")
-            for g in range(2):
-                turned = banks.tile([P, 4, P], F32, name="turned", tag="head", bufs=2)
-                for t in range(4):
-                    nc.tensor.transpose(turned[:, t, :], src[:, g * HALF + t : (g + 1) * HALF : 4], ident[:])
-                nc.vector.tensor_reduce(col[:, g, 0, :], turned[:, :, first : P : 64], AX.X, ALU.add)
-            cols[what] = col
+        k_grp = [keep.tile([P, HALF, 4], BF16, name=f"k_grp{h}", align_bytes=64) for h in range(2)]
+        for h in range(2):
+            c = slice(h * HALF, (h + 1) * HALF)
+            nc.scalar.copy(k_grp[h][:, :, 0:2], k_pair[:].rearrange("p (t n) -> p n t", t=2)[:, c, :])
+
+        pos_col = buffer(3, "pos_col", (P, 2, 4))
+        vs_col = buffer(3, "vs_col", (P, 2, 1, 4), at=64)
+        for g in range(2):
+            turned = banks.tile([P, 4, P], F32, name="turned", tag="turn", bufs=4)
+            for j in range(4):
+                at = g * HALF + j * P
+                nc.tensor.transpose(turned[:, j, :], pos_g[:, at : at + P], ident[:])
+            nc.vector.tensor_reduce(pos_col[:, g, :], turned[:, :, 0:P:64], AX.X, ALU.add)
         bias = keep.tile([P, 2, 4, P], F32, name="bias")
         for g in range(2):
             spread = banks.tile([P, 4, P], F32, name="spread", tag="head", bufs=2)
+            for j in range(4):
+                nc.tensor.transpose(spread[:, j, :], pos_col[:, g, j : j + 1].to_broadcast([P, P]), ident[:])
+            dealt = spread[:].rearrange("q j n -> q (j n)").rearrange("q (p t) -> q t p", t=4)
+            nc.scalar.activation(bias[:, g], dealt, ACT.Copy, scale=slope_sb[:])
+        for g in range(2):
+            turned = banks.tile([P, 4, P], F32, name="turned", tag="turn", bufs=4)
             for t in range(4):
-                nc.tensor.transpose(
-                    spread[:, t, :], cols["pos"][:, g, 0, t : t + 1].to_broadcast([P, P]), ident[:]
-                )
-            nc.scalar.activation(bias[:, g], spread[:], ACT.Copy, scale=slope_sb[:])
+                nc.tensor.transpose(turned[:, t, :], vs_g[:, g * HALF + t : (g + 1) * HALF : 4], ident[:])
+            nc.vector.tensor_reduce(vs_col[:, g, 0, :], turned[:, :, 4:P:64], AX.X, ALU.add)
 
-        k_grp = keep.tile([P, N, 4], BF16, name="k_grp", align_bytes=64)
         for h in range(2):
-            c = slice(h * HALF, (h + 1) * HALF)
-            nc.scalar.activation(k_grp[:, c, 0:2], k_pair[:, :, c].rearrange("p t n -> p n t"), ACT.Copy)
-        nc.vector.tensor_copy(k_grp[:, :, 2], kp[2][:].indirect(offsets[:]))
+            nc.vector.tensor_copy(k_grp[h][:, :, 2], kp[2][:].indirect(offsets[:, h * 32 : (h + 1) * 32]))
+        vp.append(buffer(4, "v_plane1"))
+        load(vp[1], vT[P : 2 * P, :], True)
         for h in range(2):
             nc.vector.tensor_copy(
-                k_grp[:, h * HALF : (h + 1) * HALF, 3],
+                k_grp[h][:, :, 3],
                 kp[3][:, : (FIRST, T)[h]].indirect(offsets[:, h * 32 : (h + 1) * 32]),
             )
-        k_codes = keep.tile([P, N], U32, name="k_codes", align_bytes=64)
+        k_codes = buffer(0, "k_codes", (P, N), U32)
         k_scales = keep.tile([P, N], U8, name="k_scales", align_bytes=64)
         score = []
         for h in range(2):
@@ -142,7 +154,7 @@ def tile_attend_x_alibi_gate_srt_kernel(tc, qT, kT, vT, vs, pos, slope, og, offs
             nc.vector.quantize_mx(
                 out=k_codes[:, c].bitcast(FP8X4),
                 scales=k_scales[:, c],
-                in_=k_grp[:, c, :].rearrange("p n t -> p (n t)"),
+                in_=k_grp[h][:].rearrange("p n t -> p (n t)"),
             )
             s_ps = banks.tile([P, HALF], F32, name=f"s_ps{h}")
             nc.tensor.matmul_mx(
@@ -156,8 +168,32 @@ def tile_attend_x_alibi_gate_srt_kernel(tc, qT, kT, vT, vs, pos, slope, og, offs
             )
             score.append(s_ps)
 
-        for c in CHUNKS:
+        for c in V_CASTS:
             nc.scalar.activation(v_cast[:, c], vp[0][:, c], ACT.Copy)
+
+        v_g = [[None, None], [None, None]]
+
+        def gather_values(e, g, tag):
+            v_g[e][g] = keep.tile([P, 2, P, 2], BF16, name=f"v_g{e}{g}", tag=tag)
+            dealt = v_g[e][g][:].rearrange("p u m i -> p m u i")
+            listed = offsets[:, g * 32 : (g + 1) * 32]
+            if (e, g) == (0, 0):
+                nc.scalar.activation(dealt, v_cast[:].indirect(listed), ACT.Copy)
+            else:
+                nc.vector.tensor_copy(dealt, vp[e][:, : (FIRST, T)[g]].indirect(listed))
+
+        v_grp = [buffer(1, f"v_grp{g}", (P, DV * 4), BF16, at=2048 * g) for g in range(2)]
+
+        def turn_values(e, g):
+            v_ps = banks.tile([P, 2, P], F32, name="v_ps", tag="turn", bufs=4)
+            for u in range(2):
+                words = v_g[e][g][:, u].rearrange("p m i -> p (m i)").bitcast(F32)
+                nc.tensor.transpose(v_ps[:, u, :], words, ident[:])
+            grouped = v_grp[g][:, e * 4 * P : (e + 1) * 4 * P].bitcast(F32)
+            nc.scalar.copy(grouped.rearrange("p (e u) -> p e u", u=2), v_ps[:].rearrange("p u e -> p e u"))
+
+        def quantise(codes, scales, grouped):
+            nc.vector.quantize_mx(out=codes.bitcast(FP8X4), scales=scales, in_=grouped)
 
         s_sb = keep.tile([P, 2, 4, P], F32, name="s_sb", tag="scores")
         for h in range(2):
@@ -168,83 +204,59 @@ def tile_attend_x_alibi_gate_srt_kernel(tc, qT, kT, vT, vs, pos, slope, og, offs
         nc.vector.tensor_reduce(
             neg_max[:], s_sb[:].rearrange("q h t p -> q (h t p)"), AX.X, ALU.max, negate=True
         )
+        gather_values(0, 0, "sums")
+        turn_values(0, 0)
         prob = keep.tile([P, 2, 4, P], F32, name="prob")
-        sums = keep.tile([P, 2], F32, name="sums")
+        sums = keep.tile([P, 2], F32, name="sums", tag="sums")
         for h in range(2):
             nc.scalar.activation(
                 prob[:, h], s_sb[:, h], ACT.Exp, bias=neg_max[:], accum_out=sums[:, h : h + 1]
             )
+        gather_values(0, 1, "bias")
+        gather_values(1, 0, "v_g10")
+        gather_values(1, 1, "v_g11")
 
-        w_codes = keep.tile([P, 2, P], U32, name="w_codes", align_bytes=64)
+        w_grp = [keep.tile([P, P, 4], BF16, name="w_first", align_bytes=64), buffer(4, "w_second", (P, P, 4), BF16)]
+        v_codes = buffer(4, "v_codes", (P, 2, DV), U32, at=2048)
+        total = keep.tile([P, 1], F32, name="total")
+        w_codes = buffer(4, "w_codes", (P, 2, P), U32, at=4096)
         w_scales = keep.tile([P, 2, P], U8, name="w_scales", align_bytes=64)
-        v_scales = [keep.tile([P, 2, P], U8, name=f"v_scales{e}", align_bytes=64) for e in range(2)]
-        v_g = [[keep.tile([P, 2, P, 2], BF16, name=f"v_g{e}{g}", tag="scores" if (e, g) == (0, 1) else f"v_g{e}{g}") for g in range(2)] for e in range(2)]
-        v_grp = [keep.tile([P, 2, P, 4], BF16, name=f"v_grp{e}", align_bytes=64) for e in range(2)]
-
-        def gather_values(e, g):
-            dealt = v_g[e][g][:].rearrange("p u m i -> p m u i")
-            listed = offsets[:, g * 32 : (g + 1) * 32]
-            if e == 0:
-                nc.scalar.activation(dealt, v_cast[:, : (FIRST, T)[g]].indirect(listed), ACT.Copy)
-            else:
-                nc.vector.tensor_copy(dealt, vp[e][:, : (FIRST, T)[g]].indirect(listed))
-
-        def turn_values(e, g):
-            v_ps = banks.tile([P, 2, P], F32, name="v_ps", tag="turn", bufs=4)
-            for u in range(2):
-                words = v_g[e][g][:, u].rearrange("p m i -> p (m i)").bitcast(F32)
-                nc.tensor.transpose(v_ps[:, u, :], words, ident[:])
-            grouped = v_grp[e][:, g].rearrange("p e t -> p (e t)").bitcast(F32)
-            nc.scalar.copy(grouped.rearrange("p (e u) -> p e u", u=2), v_ps[:].rearrange("p u e -> p e u"))
-
-        def quantise(codes, scales, grouped):
-            nc.vector.quantize_mx(out=codes.bitcast(FP8X4), scales=scales, in_=grouped)
-
-        gather_values(0, 0)
-        gather_values(0, 1)
-        gather_values(1, 0)
-        gather_values(1, 1)
-        w_grp = buffer(3, "w_grp", (P, 2, P, 4), BF16)
-        v_codes = [buffer(3, f"v_codes{e}", (P, 2, P), U32, at=2048 + 1024 * e) for e in range(2)]
-        total = buffer(3, "total", (P, 1), F32, at=4096)
-        nc.vector.tensor_tensor(total[:], sums[:, 0:1], sums[:, 1:2], ALU.add)
-        inv = keep.tile([P, 1], F32, name="inv")
-        nc.vector.reciprocal(inv[:], total[:])
+        v_scales = keep.tile([P, 2, DV], U8, name="v_scales", align_bytes=64)
+        turned_p = []
         for g in range(2):
             p_ps = banks.tile([P, 4, P], F32, name="p_ps", tag="turn", bufs=4)
             for t in range(4):
                 nc.tensor.transpose(p_ps[:, t, :], prob[:, g, t, :], ident[:])
-            nc.vector.tensor_tensor(
-                w_grp[:, g],
-                p_ps[:].rearrange("p t q -> p q t"),
-                cols["vs"][:, g].to_broadcast([P, P, 4]),
-                ALU.mult,
-            )
-        turn_values(0, 0)
+            turned_p.append(p_ps)
         turn_values(0, 1)
-        for g in range(2):
-            quantise(w_codes[:, g], w_scales[:, g], w_grp[:, g].rearrange("p q t -> p (q t)"))
-        quantise(
-            v_codes[0][:].rearrange("p g e -> p (g e)"),
-            v_scales[0][:].rearrange("p g e -> p (g e)"),
-            v_grp[0][:].rearrange("p g e t -> p (g e t)"),
+        for t in range(4):
+            nc.scalar.activation(w_grp[0][:, :, t], turned_p[0][:, t, :], ACT.Copy, scale=vs_col[:, 0, 0, t : t + 1])
+        turn_values(1, 0)
+        turn_values(1, 1)
+        nc.vector.tensor_tensor(
+            w_grp[1][:],
+            turned_p[1][:].rearrange("p t q -> p q t"),
+            vs_col[:, 1].to_broadcast([P, P, 4]),
+            ALU.mult,
         )
-        for g in range(2):
-            turn_values(1, g)
-            quantise(v_codes[1][:, g], v_scales[1][:, g], v_grp[1][:, g].rearrange("p e t -> p (e t)"))
-
-        y_sb = keep.tile([P, DV], F32, name="y_sb")
+        nc.scalar.activation(total[:], sums[:, 0:1], ACT.Identity, bias=sums[:, 1:2])
         y_ps = banks.tile([P, DV], F32, name="y_ps", tag="head", bufs=2)
-        for e in range(2):
-            for g in range(2):
-                nc.tensor.matmul_mx(
-                    out=y_ps[:, e * P : (e + 1) * P],
-                    lhsT=w_codes[:, g].bitcast(FP8X4),
-                    lhsT_scale=w_scales[:, g],
-                    rhs=v_codes[e][:, g].bitcast(FP8X4),
-                    rhs_scale=v_scales[e][:, g],
-                    start=(g == 0),
-                    stop=(g == 1),
-                )
+        quantise(w_codes[:, 0], w_scales[:, 0], w_grp[0][:].rearrange("p q t -> p (q t)"))
+        quantise(v_codes[:, 0], v_scales[:, 0], v_grp[0][:])
+        quantise(w_codes[:, 1], w_scales[:, 1], w_grp[1][:].rearrange("p q t -> p (q t)"))
+        quantise(v_codes[:, 1], v_scales[:, 1], v_grp[1][:])
+        inv = buffer(1, "inv", (P, 1), F32, at=2048)
+        nc.vector.reciprocal(inv[:], total[:])
+        for g in range(2):
+            nc.tensor.matmul_mx(
+                out=y_ps[:],
+                lhsT=w_codes[:, g].bitcast(FP8X4),
+                lhsT_scale=w_scales[:, g],
+                rhs=v_codes[:, g].bitcast(FP8X4),
+                rhs_scale=v_scales[:, g],
+                start=(g == 0),
+                stop=(g == 1),
+            )
+        y_sb = keep.tile([P, DV], F32, name="y_sb")
         nc.vector.scalar_tensor_tensor(y_sb[:], y_ps[:], inv[:], gate[:], ALU.mult, ALU.mult)
         nc.sync.dma_start(out[0], y_sb[:])

@@ -23,7 +23,7 @@ FIRST = T - HALF
 V_CASTS = [slice(0, 1024), slice(1024, 2048), slice(2048, 3072), slice(3072, FIRST)]
 V_LOADS = V_CASTS + [slice(FIRST, T)]
 K_CHUNKS = [slice(0, T // 2), slice(T // 2, T)]
-SPARE = 256
+SPARE = 768
 FLOPS = 2 * N * D * P + 2 * N * P * DV
 BYTES = 4 * (D * P + D * T + DV * T + 2 * T + P + 2 * P * DV) + 2 * P * (N // 16)
 
@@ -46,13 +46,11 @@ def tile_attend_x_alibi_gate_srt_kernel(tc, qT, kT, vT, vs, pos, slope, og, offs
         vs_row = buffer(1, "vs_row")
         k_planes = kT.rearrange("(p t) n -> p t n", t=4)
         kp = [buffer(2, "k_plane0")]
-        q_grp = buffer(4, "q_grp", (P, P, 4), BF16, at=-4 * P)
+        q_grp = buffer(4, "q_grp", (P, P, 4), BF16, at=-SPARE - 128)
 
         nc.gpsimd.memset(vs_row[:], 0.0)
         nc.vector.memset(pos_row[:, : T - 1], 0.0)
         nc.vector.memset(pos_row[:, T - 1 :], 0.0)
-        ident = keep.tile([P, P], F32, name="ident")
-        make_identity(nc, ident[:])
 
         q_raw = keep.tile([P, 4, P], F32, name="q_raw")
         nc.scalar.dma_start(q_raw[:], qT[0].rearrange("(p t) q -> p t q", t=4))
@@ -67,9 +65,9 @@ def tile_attend_x_alibi_gate_srt_kernel(tc, qT, kT, vT, vs, pos, slope, og, offs
                 queue.dma_start(row[at : at + 1, c], src[0:1, c])
 
         gate = keep.tile([P, DV], F32, name="gate")
-        nc.scalar.activation(gate[:], og_sb[:], ACT.Sigmoid)
-        warm = keep.tile([P, 1], F32, name="warm")
-        nc.scalar.activation(warm[:], gate[:, 0:1], ACT.Exp)
+        half_tanh = keep.tile([P, DV], F32, name="half_tanh")
+        nc.scalar.activation(half_tanh[:], og_sb[:], ACT.Tanh, scale=0.5)
+        nc.scalar.activation(gate[:], half_tanh[:], ACT.Identity, scale=0.5, bias=0.5)
 
         nc.scalar.copy(q_grp[:], q_raw[:].rearrange("p t q -> p q t"))
         q_codes = keep.tile([P, P], U32, name="q_codes", align_bytes=64)
@@ -79,6 +77,9 @@ def tile_attend_x_alibi_gate_srt_kernel(tc, qT, kT, vT, vs, pos, slope, og, offs
             scales=q_scales[:],
             in_=q_grp[:].rearrange("p q t -> p (q t)"),
         )
+
+        ident = buffer(3, "ident", (P, P), at=4 * T + 192)
+        make_identity(nc, ident[:])
 
         def load(tile, src, cut):
             if cut:
@@ -96,7 +97,7 @@ def tile_attend_x_alibi_gate_srt_kernel(tc, qT, kT, vT, vs, pos, slope, og, offs
         nc.scalar.activation(k_pair[:, :N], k_cast[:].indirect(offsets[:]), ACT.Copy)
         kp.append(buffer(4, "k_plane2"))
         load(kp[2], k_planes[:, 2, :], False)
-        slope_sb = buffer(4, "slope_sb", (P, 1), at=-128)
+        slope_sb = buffer(3, "slope_sb", (P, 1), at=4 * T + 128)
         nc.sync.dma_start(slope_sb[:], slope[0])
 
         pos_g = keep.tile([P, N], F32, name="pos_g")

@@ -20,8 +20,8 @@ T = 4096
 N = 1024
 HALF = 512
 FIRST = T - HALF
-V_CASTS = [slice(0, 1024), slice(1024, 2048), slice(2048, 3072), slice(3072, FIRST)]
-V_LOADS = V_CASTS + [slice(FIRST, T)]
+LAST_CASTS = [slice(0, 1024), slice(1024, 2048), slice(2048, 3072), slice(3072, FIRST)]
+LAST_LOADS = LAST_CASTS + [slice(FIRST, T)]
 K_CHUNKS = [slice(0, T // 2), slice(T // 2, T)]
 SPARE = 768
 FLOPS = 2 * N * D * P + 2 * N * P * DV
@@ -78,7 +78,7 @@ def tile_attend_x_alibi_gate_srt_kernel(tc, qT, kT, vT, vs, pos, slope, og, offs
             in_=q_grp[:].rearrange("p q t -> p (q t)"),
         )
 
-        ident = buffer(3, "ident", (P, P), at=4 * T + 192)
+        ident = buffer(3, "ident", (P, P), at=4 * T + 64)
         make_identity(nc, ident[:])
 
         def load(tile, src, cut):
@@ -89,36 +89,27 @@ def tile_attend_x_alibi_gate_srt_kernel(tc, qT, kT, vT, vs, pos, slope, og, offs
                 nc.sync.dma_start(tile[:], src)
 
         kp.append(buffer(3, "k_plane1"))
-        load(kp[1], k_planes[:, 1, :], False)
-        k_pair = keep.tile([P, 2 * N], BF16, name="k_pair")
-        k_cast = keep.tile([P, T], BF16, name="k_cast", tag="cast")
+        load(kp[1], k_planes[:, 2, :], False)
+        k_grp = [keep.tile([P, HALF, 4], BF16, name=f"k_grp{h}", align_bytes=64) for h in range(2)]
+        listed = [offsets[:, h * 32 : (h + 1) * 32] for h in range(2)]
+        k_cast = buffer(4, "k_cast", (P, T), BF16, at=4 * T)
         for c in K_CHUNKS:
             nc.scalar.activation(k_cast[:, c], kp[0][:, c], ACT.Copy)
-        nc.scalar.activation(k_pair[:, :N], k_cast[:].indirect(offsets[:]), ACT.Copy)
+        for h in range(2):
+            nc.scalar.activation(k_grp[h][:, :, 0], k_cast[:].indirect(listed[h]), ACT.Copy)
         kp.append(buffer(4, "k_plane2"))
-        load(kp[2], k_planes[:, 2, :], False)
-        slope_sb = buffer(3, "slope_sb", (P, 1), at=4 * T + 128)
+        load(kp[2], k_planes[:, 3, :], False)
+        slope_sb = buffer(3, "slope_sb", (P, 1), at=4 * T)
         nc.sync.dma_start(slope_sb[:], slope[0])
 
         pos_g = keep.tile([P, N], F32, name="pos_g")
         nc.vector.tensor_copy(pos_g[:], pos_row[:].indirect(offsets[:]))
-        kp.append(buffer(0, "k_plane3"))
-        load(kp[3], k_planes[:, 3, :], True)
-        vs_g = keep.tile([P, N], F32, name="vs_g")
+        kp.append(buffer(5, "k_plane3"))
+        for c in LAST_LOADS:
+            nc.sync.dma_start(kp[3][:, c], k_planes[:, 1, c])
+        vs_g = buffer(0, "vs_g", (P, N))
         nc.vector.tensor_copy(vs_g[:], vs_row[:].indirect(offsets[:]))
-        nc.vector.tensor_copy(k_pair[:, N:], kp[1][:].indirect(offsets[:]))
-        vp = [buffer(3, "v_plane0", at=128)]
-        v_cast = keep.tile([P, FIRST], BF16, name="v_cast", tag="cast")
-        for c in V_LOADS:
-            nc.sync.dma_start(vp[0][:, c], vT[0:P, c])
-
-        k_grp = [keep.tile([P, HALF, 4], BF16, name=f"k_grp{h}", align_bytes=64) for h in range(2)]
-        for h in range(2):
-            c = slice(h * HALF, (h + 1) * HALF)
-            nc.scalar.copy(k_grp[h][:, :, 0:2], k_pair[:].rearrange("p (t n) -> p n t", t=2)[:, c, :])
-
-        pos_col = buffer(3, "pos_col", (P, 2, 4))
-        vs_col = buffer(3, "vs_col", (P, 2, 1, 4), at=64)
+        pos_col = keep.tile([P, 2, 4], F32, name="pos_col")
         for g in range(2):
             turned = banks.tile([P, 4, P], F32, name="turned", tag="turn", bufs=4)
             for j in range(4):
@@ -126,31 +117,39 @@ def tile_attend_x_alibi_gate_srt_kernel(tc, qT, kT, vT, vs, pos, slope, og, offs
                 nc.tensor.transpose(turned[:, j, :], pos_g[:, at : at + P], ident[:])
             nc.vector.tensor_reduce(pos_col[:, g, :], turned[:, :, 0:P:64], AX.X, ALU.add)
         bias = keep.tile([P, 2, 4, P], F32, name="bias")
-        for g in range(2):
+        for g in (1, 0):
             spread = banks.tile([P, 4, P], F32, name="spread", tag="head", bufs=2)
             for j in range(4):
                 nc.tensor.transpose(spread[:, j, :], pos_col[:, g, j : j + 1].to_broadcast([P, P]), ident[:])
             dealt = spread[:].rearrange("q j n -> q (j n)").rearrange("q (p t) -> q t p", t=4)
             nc.scalar.activation(bias[:, g], dealt, ACT.Copy, scale=slope_sb[:])
+        for h in range(2):
+            nc.vector.tensor_copy(k_grp[h][:, :, 2], kp[1][:].indirect(listed[h]))
+        vp = [buffer(3, "v_plane0")]
+        load(vp[0], vT[0:P, :], True)
+
+        for h in range(2):
+            nc.vector.tensor_copy(k_grp[h][:, :, 3], kp[2][:].indirect(listed[h]))
+        vp.append(buffer(4, "v_plane1", at=-64))
+        load(vp[1], vT[P : 2 * P, :], True)
+        last_cast = keep.tile([P, FIRST], BF16, name="last_cast")
+        for c in LAST_CASTS[:-1]:
+            nc.scalar.activation(last_cast[:, c], kp[3][:, c], ACT.Copy)
+        nc.vector.tensor_copy(last_cast[:, LAST_CASTS[-1]], kp[3][:, LAST_CASTS[-1]])
+        nc.scalar.activation(k_grp[0][:, :, 1], last_cast[:].indirect(listed[0]), ACT.Copy)
+        cols = buffer(4, "cols", (P, 32), at=4 * T - 64)
+        vs_col = cols[:, 16:24].rearrange("p (g o t) -> p g o t", g=2, o=1)
         for g in range(2):
             turned = banks.tile([P, 4, P], F32, name="turned", tag="turn", bufs=4)
             for t in range(4):
                 nc.tensor.transpose(turned[:, t, :], vs_g[:, g * HALF + t : (g + 1) * HALF : 4], ident[:])
             nc.vector.tensor_reduce(vs_col[:, g, 0, :], turned[:, :, 4:P:64], AX.X, ALU.add)
 
-        for h in range(2):
-            nc.vector.tensor_copy(k_grp[h][:, :, 2], kp[2][:].indirect(offsets[:, h * 32 : (h + 1) * 32]))
-        vp.append(buffer(4, "v_plane1"))
-        load(vp[1], vT[P : 2 * P, :], True)
-        for h in range(2):
-            nc.vector.tensor_copy(
-                k_grp[h][:, :, 3],
-                kp[3][:, : (FIRST, T)[h]].indirect(offsets[:, h * 32 : (h + 1) * 32]),
-            )
-        k_codes = buffer(0, "k_codes", (P, N), U32)
+        nc.vector.tensor_copy(k_grp[1][:, :, 1], kp[3][:].indirect(listed[1]))
+        k_codes = buffer(5, "k_codes", (P, N), U32)
         k_scales = keep.tile([P, N], U8, name="k_scales", align_bytes=64)
-        score = []
-        for h in range(2):
+        score = {}
+        for h in (1, 0):
             c = slice(h * HALF, (h + 1) * HALF)
             nc.vector.quantize_mx(
                 out=k_codes[:, c].bitcast(FP8X4),
@@ -167,37 +166,34 @@ def tile_attend_x_alibi_gate_srt_kernel(tc, qT, kT, vT, vs, pos, slope, og, offs
                 start=True,
                 stop=True,
             )
-            score.append(s_ps)
-
-        for c in V_CASTS:
-            nc.scalar.activation(v_cast[:, c], vp[0][:, c], ACT.Copy)
+            score[h] = s_ps
 
         v_g = [[None, None], [None, None]]
 
         def gather_values(e, g, tag):
             v_g[e][g] = keep.tile([P, 2, P, 2], BF16, name=f"v_g{e}{g}", tag=tag)
             dealt = v_g[e][g][:].rearrange("p u m i -> p m u i")
-            listed = offsets[:, g * 32 : (g + 1) * 32]
-            if (e, g) == (0, 0):
-                nc.scalar.activation(dealt, v_cast[:].indirect(listed), ACT.Copy)
-            else:
-                nc.vector.tensor_copy(dealt, vp[e][:, : (FIRST, T)[g]].indirect(listed))
+            nc.vector.tensor_copy(dealt, vp[e][:, : (FIRST, T)[g]].indirect(listed[g]))
 
-        v_grp = [buffer(1, f"v_grp{g}", (P, DV * 4), BF16, at=2048 * g) for g in range(2)]
+        v_both = [buffer(1, f"v_both{e}", (P, 2 * P * 4), BF16, at=2048 * e) for e in range(2)]
+        v_grp = [[v_both[e][:, g * 4 * P : (g + 1) * 4 * P] for g in range(2)] for e in range(2)]
 
         def turn_values(e, g):
-            v_ps = banks.tile([P, 2, P], F32, name="v_ps", tag="turn", bufs=4)
+            if e == 0:
+                v_ps = banks.tile([P, 2, P], F32, name="v_ps", tag="turn", bufs=4)
+            else:
+                v_ps = banks.tile([P, 2, P], F32, name="v_ps", tag=f"s_ps{g}")
             for u in range(2):
                 words = v_g[e][g][:, u].rearrange("p m i -> p (m i)").bitcast(F32)
                 nc.tensor.transpose(v_ps[:, u, :], words, ident[:])
-            grouped = v_grp[g][:, e * 4 * P : (e + 1) * 4 * P].bitcast(F32)
+            grouped = v_grp[e][g].bitcast(F32)
             nc.scalar.copy(grouped.rearrange("p (e u) -> p e u", u=2), v_ps[:].rearrange("p u e -> p e u"))
 
         def quantise(codes, scales, grouped):
             nc.vector.quantize_mx(out=codes.bitcast(FP8X4), scales=scales, in_=grouped)
 
         s_sb = keep.tile([P, 2, 4, P], F32, name="s_sb", tag="scores")
-        for h in range(2):
+        for h in (1, 0):
             nc.vector.tensor_tensor(
                 s_sb[:, h], score[h][:].rearrange("q (p t) -> q t p", t=4), bias[:, h], ALU.add
             )
@@ -205,33 +201,37 @@ def tile_attend_x_alibi_gate_srt_kernel(tc, qT, kT, vT, vs, pos, slope, og, offs
         nc.vector.tensor_reduce(
             neg_max[:], s_sb[:].rearrange("q h t p -> q (h t p)"), AX.X, ALU.max, negate=True
         )
-        gather_values(0, 0, "sums")
-        turn_values(0, 0)
         prob = keep.tile([P, 2, 4, P], F32, name="prob")
         sums = keep.tile([P, 2], F32, name="sums", tag="sums")
-        for h in range(2):
+        for h in (1, 0):
             nc.scalar.activation(
                 prob[:, h], s_sb[:, h], ACT.Exp, bias=neg_max[:], accum_out=sums[:, h : h + 1]
             )
-        gather_values(0, 1, "bias")
-        gather_values(1, 0, "v_g10")
-        gather_values(1, 1, "v_g11")
+        gather_values(0, 0, "bias")
+        gather_values(0, 1, "v_g01")
 
-        w_grp = [keep.tile([P, P, 4], BF16, name="w_first", align_bytes=64), buffer(4, "w_second", (P, P, 4), BF16)]
-        v_codes = buffer(4, "v_codes", (P, 2, DV), U32, at=2048)
         total = keep.tile([P, 1], F32, name="total")
-        w_codes = buffer(4, "w_codes", (P, 2, P), U32, at=4096)
-        w_scales = keep.tile([P, 2, P], U8, name="w_scales", align_bytes=64)
-        v_scales = keep.tile([P, 2, DV], U8, name="v_scales", align_bytes=64)
-        turned_p = []
-        for g in range(2):
+        nc.scalar.activation(total[:], sums[:, 0:1], ACT.Identity, bias=sums[:, 1:2])
+        inv = keep.tile([P, 1], F32, name="inv")
+        nc.vector.reciprocal(inv[:], total[:])
+        w_first = keep.tile([P, P, 4], BF16, name="w_first", align_bytes=64)
+        w_grp = [w_first, buffer(4, "w_second", (P, P, 4), BF16, at=2048)]
+        w_codes = [buffer(4, f"w_codes{g}", (P, P), U32, at=512 * g) for g in range(2)]
+        w_scales = [keep.tile([P, P], U8, name=f"w_scales{g}", align_bytes=64) for g in range(2)]
+        v_codes = [buffer(4, "v_codes0", (P, 2, P), U32, at=1024), buffer(4, "v_codes1", (P, 2, P), U32, at=4096)]
+        v_scales = [keep.tile([P, 2, P], U8, name=f"v_scales{e}", align_bytes=64) for e in range(2)]
+        turned_p = {}
+        for g in (1, 0):
             p_ps = banks.tile([P, 4, P], F32, name="p_ps", tag="turn", bufs=4)
             for t in range(4):
                 nc.tensor.transpose(p_ps[:, t, :], prob[:, g, t, :], ident[:])
-            turned_p.append(p_ps)
-        turn_values(0, 1)
+            turned_p[g] = p_ps
+        turn_values(0, 0)
         for t in range(4):
             nc.scalar.activation(w_grp[0][:, :, t], turned_p[0][:, t, :], ACT.Copy, scale=vs_col[:, 0, 0, t : t + 1])
+        turn_values(0, 1)
+        gather_values(1, 0, "v_g10")
+        gather_values(1, 1, "v_g11")
         turn_values(1, 0)
         turn_values(1, 1)
         nc.vector.tensor_tensor(
@@ -240,24 +240,27 @@ def tile_attend_x_alibi_gate_srt_kernel(tc, qT, kT, vT, vs, pos, slope, og, offs
             vs_col[:, 1].to_broadcast([P, P, 4]),
             ALU.mult,
         )
-        nc.scalar.activation(total[:], sums[:, 0:1], ACT.Identity, bias=sums[:, 1:2])
-        y_ps = banks.tile([P, DV], F32, name="y_ps", tag="head", bufs=2)
-        quantise(w_codes[:, 0], w_scales[:, 0], w_grp[0][:].rearrange("p q t -> p (q t)"))
-        quantise(v_codes[:, 0], v_scales[:, 0], v_grp[0][:])
-        quantise(w_codes[:, 1], w_scales[:, 1], w_grp[1][:].rearrange("p q t -> p (q t)"))
-        quantise(v_codes[:, 1], v_scales[:, 1], v_grp[1][:])
-        inv = buffer(1, "inv", (P, 1), F32, at=2048)
-        nc.vector.reciprocal(inv[:], total[:])
-        for g in range(2):
-            nc.tensor.matmul_mx(
-                out=y_ps[:],
-                lhsT=w_codes[:, g].bitcast(FP8X4),
-                lhsT_scale=w_scales[:, g],
-                rhs=v_codes[:, g].bitcast(FP8X4),
-                rhs_scale=v_scales[:, g],
-                start=(g == 0),
-                stop=(g == 1),
-            )
-        y_sb = keep.tile([P, DV], F32, name="y_sb")
-        nc.vector.scalar_tensor_tensor(y_sb[:], y_ps[:], inv[:], gate[:], ALU.mult, ALU.mult)
-        nc.sync.dma_start(out[0], y_sb[:])
+        quantise(w_codes[0][:], w_scales[0][:], w_grp[0][:].rearrange("p q t -> p (q t)"))
+        quantise(
+            v_codes[0][:].rearrange("p g e -> p (g e)"), v_scales[0][:].rearrange("p g e -> p (g e)"), v_both[0][:]
+        )
+        quantise(w_codes[1][:], w_scales[1][:], w_grp[1][:].rearrange("p q t -> p (q t)"))
+        quantise(v_codes[1][:, 0], v_scales[1][:, 0], v_grp[1][0])
+        quantise(v_codes[1][:, 1], v_scales[1][:, 1], v_grp[1][1])
+
+        for e in range(2):
+            y_ps = banks.tile([P, P], F32, name="y_ps", tag="head", bufs=2)
+            for g in range(2):
+                nc.tensor.matmul_mx(
+                    out=y_ps[:],
+                    lhsT=w_codes[g][:].bitcast(FP8X4),
+                    lhsT_scale=w_scales[g][:],
+                    rhs=v_codes[e][:, g].bitcast(FP8X4),
+                    rhs_scale=v_scales[e][:, g],
+                    start=(g == 0),
+                    stop=(g == 1),
+                )
+            c = slice(e * P, (e + 1) * P)
+            y_sb = keep.tile([P, P], F32, name=f"y_sb{e}")
+            nc.vector.scalar_tensor_tensor(y_sb[:], y_ps[:], inv[:], gate[:, c], ALU.mult, ALU.mult)
+            nc.sync.dma_start(out[0][:, c], y_sb[:])

@@ -20,7 +20,7 @@ T = 4096
 N = 1024
 HALF = 512
 FIRST = T - HALF
-LAST_CASTS = [slice(0, 1024), slice(1024, 2048), slice(2048, 3072), slice(3072, FIRST)]
+LAST_CASTS = [slice(0, 1280), slice(1280, 2560), slice(2560, FIRST)]
 LAST_LOADS = LAST_CASTS + [slice(FIRST, T)]
 K_CHUNKS = [slice(0, T // 2), slice(T // 2, T)]
 SPARE = 768
@@ -126,7 +126,7 @@ def tile_attend_x_alibi_gate_srt_kernel(tc, qT, kT, vT, vs, pos, slope, og, offs
         for h in range(2):
             nc.vector.tensor_copy(k_grp[h][:, :, 2], kp[1][:].indirect(listed[h]))
         vp = [buffer(3, "v_plane0")]
-        load(vp[0], vT[0:P, :], True)
+        load(vp[0], vT[0:P, :], False)
 
         for h in range(2):
             nc.vector.tensor_copy(k_grp[h][:, :, 3], kp[2][:].indirect(listed[h]))
@@ -212,8 +212,6 @@ def tile_attend_x_alibi_gate_srt_kernel(tc, qT, kT, vT, vs, pos, slope, og, offs
 
         total = keep.tile([P, 1], F32, name="total")
         nc.scalar.activation(total[:], sums[:, 0:1], ACT.Identity, bias=sums[:, 1:2])
-        inv = keep.tile([P, 1], F32, name="inv")
-        nc.vector.reciprocal(inv[:], total[:])
         w_first = keep.tile([P, P, 4], BF16, name="w_first", align_bytes=64)
         w_grp = [w_first, buffer(4, "w_second", (P, P, 4), BF16, at=2048)]
         w_codes = [buffer(4, f"w_codes{g}", (P, P), U32, at=512 * g) for g in range(2)]
@@ -245,6 +243,8 @@ def tile_attend_x_alibi_gate_srt_kernel(tc, qT, kT, vT, vs, pos, slope, og, offs
             v_codes[0][:].rearrange("p g e -> p (g e)"), v_scales[0][:].rearrange("p g e -> p (g e)"), v_both[0][:]
         )
         quantise(w_codes[1][:], w_scales[1][:], w_grp[1][:].rearrange("p q t -> p (q t)"))
+        inv = buffer(4, "inv", (P, 1), at=6144)
+        nc.vector.reciprocal(inv[:], total[:])
         quantise(v_codes[1][:, 0], v_scales[1][:, 0], v_grp[1][0])
         quantise(v_codes[1][:, 1], v_scales[1][:, 1], v_grp[1][1])
 

@@ -46,7 +46,7 @@ def tile_attend_x_alibi_gate_srt_kernel(tc, qT, kT, vT, vs, pos, slope, og, offs
         vs_row = buffer(1, "vs_row")
         k_planes = kT.rearrange("(p t) n -> p t n", t=4)
         kp = [buffer(2, "k_plane0")]
-        q_grp = buffer(4, "q_grp", (P, P, 4), BF16, at=-SPARE - 128)
+        q_grp = buffer(7, "q_grp", (P, P, 4), BF16, at=-SPARE - 128)
 
         nc.gpsimd.memset(vs_row[:], 0.0)
         nc.vector.memset(pos_row[:, : T - 1], 0.0)
@@ -78,7 +78,7 @@ def tile_attend_x_alibi_gate_srt_kernel(tc, qT, kT, vT, vs, pos, slope, og, offs
             in_=q_grp[:].rearrange("p q t -> p (q t)"),
         )
 
-        ident = buffer(3, "ident", (P, P), at=4 * T + 64)
+        ident = buffer(6, "ident", (P, P), at=4 * T + 128)
         make_identity(nc, ident[:])
 
         def load(tile, src, cut):
@@ -88,18 +88,18 @@ def tile_attend_x_alibi_gate_srt_kernel(tc, qT, kT, vT, vs, pos, slope, og, offs
             else:
                 nc.sync.dma_start(tile[:], src)
 
-        kp.append(buffer(3, "k_plane1"))
+        kp.append(buffer(6, "k_plane1"))
         load(kp[1], k_planes[:, 2, :], False)
         k_grp = [keep.tile([P, HALF, 4], BF16, name=f"k_grp{h}", align_bytes=64) for h in range(2)]
         listed = [offsets[:, h * 32 : (h + 1) * 32] for h in range(2)]
-        k_cast = buffer(4, "k_cast", (P, T), BF16, at=4 * T)
+        k_cast = buffer(6, "k_cast", (P, T), BF16, at=-2 * T)
         for c in K_CHUNKS:
             nc.scalar.activation(k_cast[:, c], kp[0][:, c], ACT.Copy)
         for h in range(2):
             nc.scalar.activation(k_grp[h][:, :, 0], k_cast[:].indirect(listed[h]), ACT.Copy)
-        kp.append(buffer(4, "k_plane2"))
-        load(kp[2], k_planes[:, 3, :], False)
-        slope_sb = buffer(3, "slope_sb", (P, 1), at=4 * T)
+        kp.append(buffer(7, "k_plane2"))
+        load(kp[2], k_planes[:, 3, :], True)
+        slope_sb = buffer(6, "slope_sb", (P, 1), at=4 * T + 64)
         nc.sync.dma_start(slope_sb[:], slope[0])
 
         pos_g = keep.tile([P, N], F32, name="pos_g")
@@ -125,19 +125,7 @@ def tile_attend_x_alibi_gate_srt_kernel(tc, qT, kT, vT, vs, pos, slope, og, offs
             nc.scalar.activation(bias[:, g], dealt, ACT.Copy, scale=slope_sb[:])
         for h in range(2):
             nc.vector.tensor_copy(k_grp[h][:, :, 2], kp[1][:].indirect(listed[h]))
-        vp = [buffer(3, "v_plane0")]
-        load(vp[0], vT[0:P, :], False)
-
-        for h in range(2):
-            nc.vector.tensor_copy(k_grp[h][:, :, 3], kp[2][:].indirect(listed[h]))
-        vp.append(buffer(4, "v_plane1", at=-64))
-        load(vp[1], vT[P : 2 * P, :], True)
-        last_cast = keep.tile([P, FIRST], BF16, name="last_cast")
-        for c in LAST_CASTS[:-1]:
-            nc.scalar.activation(last_cast[:, c], kp[3][:, c], ACT.Copy)
-        nc.vector.tensor_copy(last_cast[:, LAST_CASTS[-1]], kp[3][:, LAST_CASTS[-1]])
-        nc.scalar.activation(k_grp[0][:, :, 1], last_cast[:].indirect(listed[0]), ACT.Copy)
-        cols = buffer(4, "cols", (P, 32), at=4 * T - 64)
+        cols = buffer(6, "cols", (P, 32), at=-64)
         vs_col = cols[:, 16:24].rearrange("p (g o t) -> p g o t", g=2, o=1)
         for g in range(2):
             turned = banks.tile([P, 4, P], F32, name="turned", tag="turn", bufs=4)
@@ -145,6 +133,18 @@ def tile_attend_x_alibi_gate_srt_kernel(tc, qT, kT, vT, vs, pos, slope, og, offs
                 nc.tensor.transpose(turned[:, t, :], vs_g[:, g * HALF + t : (g + 1) * HALF : 4], ident[:])
             nc.vector.tensor_reduce(vs_col[:, g, 0, :], turned[:, :, 4:P:64], AX.X, ALU.add)
 
+        vp = [buffer(6, "v_plane0", at=64)]
+        load(vp[0], vT[0:P, :], False)
+
+        for h in range(2):
+            nc.vector.tensor_copy(k_grp[h][:, :, 3], kp[2][:, : (FIRST, T)[h]].indirect(listed[h]))
+        vp.append(buffer(7, "v_plane1"))
+        load(vp[1], vT[P : 2 * P, :], True)
+        last_cast = keep.tile([P, FIRST], BF16, name="last_cast")
+        for c in LAST_CASTS[:-1]:
+            nc.scalar.activation(last_cast[:, c], kp[3][:, c], ACT.Copy)
+        nc.vector.tensor_copy(last_cast[:, LAST_CASTS[-1]], kp[3][:, LAST_CASTS[-1]])
+        nc.scalar.activation(k_grp[0][:, :, 1], last_cast[:].indirect(listed[0]), ACT.Copy)
         nc.vector.tensor_copy(k_grp[1][:, :, 1], kp[3][:].indirect(listed[1]))
         k_codes = buffer(5, "k_codes", (P, N), U32)
         k_scales = keep.tile([P, N], U8, name="k_scales", align_bytes=64)
@@ -213,10 +213,10 @@ def tile_attend_x_alibi_gate_srt_kernel(tc, qT, kT, vT, vs, pos, slope, og, offs
         total = keep.tile([P, 1], F32, name="total")
         nc.scalar.activation(total[:], sums[:, 0:1], ACT.Identity, bias=sums[:, 1:2])
         w_first = keep.tile([P, P, 4], BF16, name="w_first", align_bytes=64)
-        w_grp = [w_first, buffer(4, "w_second", (P, P, 4), BF16, at=2048)]
-        w_codes = [buffer(4, f"w_codes{g}", (P, P), U32, at=512 * g) for g in range(2)]
+        w_grp = [w_first, buffer(7, "w_second", (P, P, 4), BF16, at=2048)]
+        w_codes = [buffer(7, f"w_codes{g}", (P, P), U32, at=512 * g) for g in range(2)]
         w_scales = [keep.tile([P, P], U8, name=f"w_scales{g}", align_bytes=64) for g in range(2)]
-        v_codes = [buffer(4, "v_codes0", (P, 2, P), U32, at=1024), buffer(4, "v_codes1", (P, 2, P), U32, at=4096)]
+        v_codes = [buffer(7, "v_codes0", (P, 2, P), U32, at=1024), buffer(7, "v_codes1", (P, 2, P), U32, at=4096)]
         v_scales = [keep.tile([P, 2, P], U8, name=f"v_scales{e}", align_bytes=64) for e in range(2)]
         turned_p = {}
         for g in (1, 0):
@@ -243,7 +243,7 @@ def tile_attend_x_alibi_gate_srt_kernel(tc, qT, kT, vT, vs, pos, slope, og, offs
             v_codes[0][:].rearrange("p g e -> p (g e)"), v_scales[0][:].rearrange("p g e -> p (g e)"), v_both[0][:]
         )
         quantise(w_codes[1][:], w_scales[1][:], w_grp[1][:].rearrange("p q t -> p (q t)"))
-        inv = buffer(4, "inv", (P, 1), at=6144)
+        inv = buffer(7, "inv", (P, 1), at=6144)
         nc.vector.reciprocal(inv[:], total[:])
         quantise(v_codes[1][:, 0], v_scales[1][:, 0], v_grp[1][0])
         quantise(v_codes[1][:, 1], v_scales[1][:, 1], v_grp[1][1])

@@ -89,24 +89,24 @@ def tile_attend_x_alibi_gate_srt_kernel(tc, qT, kT, vT, vs, pos, slope, og, offs
                 nc.sync.dma_start(tile[:], src)
 
         kp.append(buffer(6, "k_plane1"))
-        load(kp[1], k_planes[:, 2, :], False)
+        load(kp[1], k_planes[:, 1, :], False)
+        slope_sb = buffer(6, "slope_sb", (P, 1), at=4 * T + 64)
+        nc.sync.dma_start(slope_sb[:], slope[0])
         k_grp = [keep.tile([P, HALF, 4], BF16, name=f"k_grp{h}", align_bytes=64) for h in range(2)]
         listed = [offsets[:, h * 32 : (h + 1) * 32] for h in range(2)]
         k_cast = buffer(6, "k_cast", (P, T), BF16, at=-2 * T)
         for c in K_CHUNKS:
             nc.scalar.activation(k_cast[:, c], kp[0][:, c], ACT.Copy)
-        for h in range(2):
-            nc.scalar.activation(k_grp[h][:, :, 0], k_cast[:].indirect(listed[h]), ACT.Copy)
+        k_pair = keep.tile([P, 2 * N], BF16, name="k_pair")
+        nc.scalar.activation(k_pair[:, :N], k_cast[:].indirect(offsets[:]), ACT.Copy)
         kp.append(buffer(7, "k_plane2"))
-        load(kp[2], k_planes[:, 3, :], True)
-        slope_sb = buffer(6, "slope_sb", (P, 1), at=4 * T + 64)
-        nc.sync.dma_start(slope_sb[:], slope[0])
+        load(kp[2], k_planes[:, 2, :], True)
 
         pos_g = keep.tile([P, N], F32, name="pos_g")
         nc.vector.tensor_copy(pos_g[:], pos_row[:].indirect(offsets[:]))
         kp.append(buffer(5, "k_plane3"))
         for c in LAST_LOADS:
-            nc.sync.dma_start(kp[3][:, c], k_planes[:, 1, c])
+            nc.sync.dma_start(kp[3][:, c], k_planes[:, 3, c])
         vs_g = buffer(0, "vs_g", (P, N))
         nc.vector.tensor_copy(vs_g[:], vs_row[:].indirect(offsets[:]))
         pos_col = keep.tile([P, 2, 4], F32, name="pos_col")
@@ -123,8 +123,10 @@ def tile_attend_x_alibi_gate_srt_kernel(tc, qT, kT, vT, vs, pos, slope, og, offs
                 nc.tensor.transpose(spread[:, j, :], pos_col[:, g, j : j + 1].to_broadcast([P, P]), ident[:])
             dealt = spread[:].rearrange("q j n -> q (j n)").rearrange("q (p t) -> q t p", t=4)
             nc.scalar.activation(bias[:, g], dealt, ACT.Copy, scale=slope_sb[:])
+        nc.vector.tensor_copy(k_pair[:, N:], kp[1][:].indirect(offsets[:]))
         for h in range(2):
-            nc.vector.tensor_copy(k_grp[h][:, :, 2], kp[1][:].indirect(listed[h]))
+            c = slice(h * HALF, (h + 1) * HALF)
+            nc.scalar.copy(k_grp[h][:, :, 0:2], k_pair[:].rearrange("p (t n) -> p n t", t=2)[:, c, :])
         cols = buffer(6, "cols", (P, 32), at=-64)
         vs_col = cols[:, 16:24].rearrange("p (g o t) -> p g o t", g=2, o=1)
         for g in range(2):
@@ -137,15 +139,15 @@ def tile_attend_x_alibi_gate_srt_kernel(tc, qT, kT, vT, vs, pos, slope, og, offs
         load(vp[0], vT[0:P, :], False)
 
         for h in range(2):
-            nc.vector.tensor_copy(k_grp[h][:, :, 3], kp[2][:, : (FIRST, T)[h]].indirect(listed[h]))
+            nc.vector.tensor_copy(k_grp[h][:, :, 2], kp[2][:, : (FIRST, T)[h]].indirect(listed[h]))
         vp.append(buffer(7, "v_plane1"))
         load(vp[1], vT[P : 2 * P, :], True)
         last_cast = keep.tile([P, FIRST], BF16, name="last_cast")
         for c in LAST_CASTS[:-1]:
             nc.scalar.activation(last_cast[:, c], kp[3][:, c], ACT.Copy)
         nc.vector.tensor_copy(last_cast[:, LAST_CASTS[-1]], kp[3][:, LAST_CASTS[-1]])
-        nc.scalar.activation(k_grp[0][:, :, 1], last_cast[:].indirect(listed[0]), ACT.Copy)
-        nc.vector.tensor_copy(k_grp[1][:, :, 1], kp[3][:].indirect(listed[1]))
+        nc.scalar.activation(k_grp[0][:, :, 3], last_cast[:].indirect(listed[0]), ACT.Copy)
+        nc.vector.tensor_copy(k_grp[1][:, :, 3], kp[3][:].indirect(listed[1]))
         k_codes = buffer(5, "k_codes", (P, N), U32)
         k_scales = keep.tile([P, N], U8, name="k_scales", align_bytes=64)
         score = {}

@@ -40,7 +40,8 @@ def tile_attend_x_alibi_gate_srt_kernel(tc, qT, kT, vT, vs, pos, slope, og, offs
         planes = ctx.enter_context(tc.tile_pool(name="planes", bufs=1))
 
         def buffer(b, name, shape=(P, T), dtype=F32, at=0):
-            return planes.tile(list(shape), dtype, name=name, align_bytes=64, offset=(4 * T + SPARE) * b + at)
+            align = 256 if shape == (P, T) else 64
+            return planes.tile(list(shape), dtype, name=name, align_bytes=align, offset=(4 * T + SPARE) * b + at)
 
         pos_row = buffer(0, "pos_row")
         vs_row = buffer(1, "vs_row")
@@ -127,15 +128,14 @@ def tile_attend_x_alibi_gate_srt_kernel(tc, qT, kT, vT, vs, pos, slope, og, offs
         for h in range(2):
             c = slice(h * HALF, (h + 1) * HALF)
             nc.scalar.copy(k_grp[h][:, :, 0:2], k_pair[:].rearrange("p (t n) -> p n t", t=2)[:, c, :])
-        cols = buffer(6, "cols", (P, 32), at=-64)
-        vs_col = cols[:, 16:24].rearrange("p (g o t) -> p g o t", g=2, o=1)
+        vs_col = buffer(6, "vs_col", (P, 2, 1, 4), at=4 * T - 64)
         for g in range(2):
             turned = banks.tile([P, 4, P], F32, name="turned", tag="turn", bufs=4)
             for t in range(4):
                 nc.tensor.transpose(turned[:, t, :], vs_g[:, g * HALF + t : (g + 1) * HALF : 4], ident[:])
             nc.vector.tensor_reduce(vs_col[:, g, 0, :], turned[:, :, 4:P:64], AX.X, ALU.add)
 
-        vp = [buffer(6, "v_plane0", at=64)]
+        vp = [buffer(6, "v_plane0", at=-256)]
         load(vp[0], vT[0:P, :], False)
 
         for h in range(2):

@@ -117,23 +117,35 @@ def tile_attend_x_alibi_gate_srt_kernel(tc, qT, kT, vT, vs, pos, slope, og, offs
                 at = g * HALF + j * P
                 nc.tensor.transpose(turned[:, j, :], pos_g[:, at : at + P], ident[:])
             nc.vector.tensor_reduce(pos_col[:, g, :], turned[:, :, 0:P:64], AX.X, ALU.add)
-        bias = keep.tile([P, 2, 4, P], F32, name="bias")
+        def dealt(bank):
+            return bank[:].rearrange("q j n -> q (j n)").rearrange("q (b u j) -> q u b j", u=2, j=16)
+
+        def runs(row):
+            return row.rearrange("q (u b j) -> q u b j", u=2, j=16)
+
+        bias = keep.tile([P, 2, HALF], F32, name="bias")
         for g in (1, 0):
             spread = banks.tile([P, 4, P], F32, name="spread", tag="head", bufs=2)
             for j in range(4):
                 nc.tensor.transpose(spread[:, j, :], pos_col[:, g, j : j + 1].to_broadcast([P, P]), ident[:])
-            dealt = spread[:].rearrange("q j n -> q (j n)").rearrange("q (p t) -> q t p", t=4)
-            nc.scalar.activation(bias[:, g], dealt, ACT.Copy, scale=slope_sb[:])
+            nc.scalar.activation(runs(bias[:, g]), dealt(spread), ACT.Copy, scale=slope_sb[:])
         nc.vector.tensor_copy(k_pair[:, N:], kp[1][:].indirect(offsets[:]))
         for h in range(2):
             c = slice(h * HALF, (h + 1) * HALF)
             nc.scalar.copy(k_grp[h][:, :, 0:2], k_pair[:].rearrange("p (t n) -> p n t", t=2)[:, c, :])
-        vs_col = buffer(6, "vs_col", (P, 2, 1, 4), at=4 * T - 64)
+        vs_col = buffer(6, "vs_col", (P, 2, 4), at=4 * T - 64)
         for g in range(2):
             turned = banks.tile([P, 4, P], F32, name="turned", tag="turn", bufs=4)
-            for t in range(4):
-                nc.tensor.transpose(turned[:, t, :], vs_g[:, g * HALF + t : (g + 1) * HALF : 4], ident[:])
-            nc.vector.tensor_reduce(vs_col[:, g, 0, :], turned[:, :, 4:P:64], AX.X, ALU.add)
+            for j in range(4):
+                at = g * HALF + j * P
+                nc.tensor.transpose(turned[:, j, :], vs_g[:, at : at + P], ident[:])
+            nc.vector.tensor_reduce(vs_col[:, g, :], turned[:, :, 4:P:64], AX.X, ALU.add)
+        vs_all = keep.tile([P, 2, HALF], F32, name="vs_all")
+        for g in (1, 0):
+            spread = banks.tile([P, 4, P], F32, name="spread", tag="head", bufs=2)
+            for j in range(4):
+                nc.tensor.transpose(spread[:, j, :], vs_col[:, g, j : j + 1].to_broadcast([P, P]), ident[:])
+            nc.vector.tensor_copy(runs(vs_all[:, g]), dealt(spread))
 
         vp = [buffer(6, "v_plane0", at=-256)]
         load(vp[0], vT[0:P, :], False)
@@ -173,37 +185,42 @@ def tile_attend_x_alibi_gate_srt_kernel(tc, qT, kT, vT, vs, pos, slope, og, offs
         v_g = [[None, None], [None, None]]
 
         def gather_values(e, g, tag):
-            v_g[e][g] = keep.tile([P, 2, P, 2], BF16, name=f"v_g{e}{g}", tag=tag)
-            dealt = v_g[e][g][:].rearrange("p u m i -> p m u i")
-            nc.vector.tensor_copy(dealt, vp[e][:, : (FIRST, T)[g]].indirect(listed[g]))
+            v_g[e][g] = keep.tile([P, HALF], BF16, name=f"v_g{e}{g}", tag=tag)
+            places = v_g[e][g][:].rearrange("p (u b j) -> p b u j", u=2, j=16)
+            nc.vector.tensor_copy(places, vp[e][:, : (FIRST, T)[g]].indirect(listed[g]))
 
         v_both = [buffer(1, f"v_both{e}", (P, 2 * P * 4), BF16, at=2048 * e) for e in range(2)]
         v_grp = [[v_both[e][:, g * 4 * P : (g + 1) * 4 * P] for g in range(2)] for e in range(2)]
+
+        def turn(bank, rows, grouped):
+            words = rows.bitcast(F32)
+            for u in range(2):
+                nc.tensor.transpose(bank[:, u, :], words[:, u * P : (u + 1) * P], ident[:])
+            nc.scalar.copy(grouped.bitcast(F32).rearrange("p (e u) -> p e u", u=2), bank[:].rearrange("p u e -> p e u"))
 
         def turn_values(e, g):
             if e == 0:
                 v_ps = banks.tile([P, 2, P], F32, name="v_ps", tag="turn", bufs=4)
             else:
                 v_ps = banks.tile([P, 2, P], F32, name="v_ps", tag=f"s_ps{g}")
-            for u in range(2):
-                words = v_g[e][g][:, u].rearrange("p m i -> p (m i)").bitcast(F32)
-                nc.tensor.transpose(v_ps[:, u, :], words, ident[:])
-            grouped = v_grp[e][g].bitcast(F32)
-            nc.scalar.copy(grouped.rearrange("p (e u) -> p e u", u=2), v_ps[:].rearrange("p u e -> p e u"))
+            turn(v_ps, v_g[e][g][:], v_grp[e][g])
 
         def quantise(codes, scales, grouped):
             nc.vector.quantize_mx(out=codes.bitcast(FP8X4), scales=scales, in_=grouped)
 
-        s_sb = keep.tile([P, 2, 4, P], F32, name="s_sb", tag="scores")
+        s_sb = keep.tile([P, 2, HALF], F32, name="s_sb", tag="scores")
         for h in (1, 0):
             nc.vector.tensor_tensor(
-                s_sb[:, h], score[h][:].rearrange("q (p t) -> q t p", t=4), bias[:, h], ALU.add
+                runs(s_sb[:, h]),
+                score[h][:].rearrange("q (b u j) -> q u b j", u=2, j=16),
+                runs(bias[:, h]),
+                ALU.add,
             )
         neg_max = keep.tile([P, 1], F32, name="neg_max")
         nc.vector.tensor_reduce(
-            neg_max[:], s_sb[:].rearrange("q h t p -> q (h t p)"), AX.X, ALU.max, negate=True
+            neg_max[:], s_sb[:].rearrange("q h n -> q (h n)"), AX.X, ALU.max, negate=True
         )
-        prob = keep.tile([P, 2, 4, P], F32, name="prob")
+        prob = keep.tile([P, 2, HALF], F32, name="prob")
         sums = keep.tile([P, 2], F32, name="sums", tag="sums")
         for h in (1, 0):
             nc.scalar.activation(
@@ -214,37 +231,28 @@ def tile_attend_x_alibi_gate_srt_kernel(tc, qT, kT, vT, vs, pos, slope, og, offs
 
         total = keep.tile([P, 1], F32, name="total")
         nc.scalar.activation(total[:], sums[:, 0:1], ACT.Identity, bias=sums[:, 1:2])
-        w_first = keep.tile([P, P, 4], BF16, name="w_first", align_bytes=64)
-        w_grp = [w_first, buffer(7, "w_second", (P, P, 4), BF16, at=2048)]
+        w_row = [keep.tile([P, HALF], BF16, name=f"w_row{g}") for g in range(2)]
+        w_grp = [keep.tile([P, 4 * P], BF16, name=f"w_grp{g}", align_bytes=64) for g in range(2)]
         w_codes = [buffer(7, f"w_codes{g}", (P, P), U32, at=512 * g) for g in range(2)]
         w_scales = [keep.tile([P, P], U8, name=f"w_scales{g}", align_bytes=64) for g in range(2)]
         v_codes = [buffer(7, "v_codes0", (P, 2, P), U32, at=1024), buffer(7, "v_codes1", (P, 2, P), U32, at=4096)]
         v_scales = [keep.tile([P, 2, P], U8, name=f"v_scales{e}", align_bytes=64) for e in range(2)]
-        turned_p = {}
         for g in (1, 0):
-            p_ps = banks.tile([P, 4, P], F32, name="p_ps", tag="turn", bufs=4)
-            for t in range(4):
-                nc.tensor.transpose(p_ps[:, t, :], prob[:, g, t, :], ident[:])
-            turned_p[g] = p_ps
+            nc.gpsimd.tensor_tensor(w_row[g][:], prob[:, g], vs_all[:, g], ALU.mult)
         turn_values(0, 0)
-        for t in range(4):
-            nc.scalar.activation(w_grp[0][:, :, t], turned_p[0][:, t, :], ACT.Copy, scale=vs_col[:, 0, 0, t : t + 1])
         turn_values(0, 1)
+        for g in (1, 0):
+            w_ps = banks.tile([P, 2, P], F32, name="w_ps", tag="turn", bufs=4)
+            turn(w_ps, w_row[g][:], w_grp[g][:])
         gather_values(1, 0, "v_g10")
         gather_values(1, 1, "v_g11")
         turn_values(1, 0)
         turn_values(1, 1)
-        nc.vector.tensor_tensor(
-            w_grp[1][:],
-            turned_p[1][:].rearrange("p t q -> p q t"),
-            vs_col[:, 1].to_broadcast([P, P, 4]),
-            ALU.mult,
-        )
-        quantise(w_codes[0][:], w_scales[0][:], w_grp[0][:].rearrange("p q t -> p (q t)"))
+        quantise(w_codes[0][:], w_scales[0][:], w_grp[0][:])
         quantise(
             v_codes[0][:].rearrange("p g e -> p (g e)"), v_scales[0][:].rearrange("p g e -> p (g e)"), v_both[0][:]
         )
-        quantise(w_codes[1][:], w_scales[1][:], w_grp[1][:].rearrange("p q t -> p (q t)"))
+        quantise(w_codes[1][:], w_scales[1][:], w_grp[1][:])
         inv = buffer(7, "inv", (P, 1), at=6144)
         nc.vector.reciprocal(inv[:], total[:])
         quantise(v_codes[1][:, 0], v_scales[1][:, 0], v_grp[1][0])

@@ -22,8 +22,10 @@ HALF = 512
 FIRST = T - HALF
 LAST_CASTS = [slice(0, 1280), slice(1280, 2560), slice(2560, FIRST)]
 LAST_LOADS = LAST_CASTS + [slice(FIRST, T)]
+V_CASTS = [slice(0, 1536), slice(1536, 3072), slice(3072, FIRST)]
 K_CHUNKS = [slice(0, T // 2), slice(T // 2, T)]
 SPARE = 768
+SHIFT = 4 * HALF
 FLOPS = 2 * N * D * P + 2 * N * P * DV
 BYTES = 4 * (D * P + D * T + DV * T + 2 * T + P + 2 * P * DV) + 2 * P * (N // 16)
 
@@ -41,7 +43,7 @@ def tile_attend_x_alibi_gate_srt_kernel(tc, qT, kT, vT, vs, pos, slope, og, offs
 
         def buffer(b, name, shape=(P, T), dtype=F32, at=0):
             align = 256 if shape == (P, T) else 64
-            return planes.tile(list(shape), dtype, name=name, align_bytes=align, offset=(4 * T + SPARE) * b + at)
+            return planes.tile(list(shape), dtype, name=name, align_bytes=align, offset=(4 * T + SPARE) * b + at + SHIFT * (b > 6))
 
         pos_row = buffer(0, "pos_row")
         vs_row = buffer(1, "vs_row")
@@ -79,7 +81,7 @@ def tile_attend_x_alibi_gate_srt_kernel(tc, qT, kT, vT, vs, pos, slope, og, offs
             in_=q_grp[:].rearrange("p q t -> p (q t)"),
         )
 
-        ident = buffer(6, "ident", (P, P), at=4 * T + 128)
+        ident = buffer(6, "ident", (P, P), at=SHIFT + 4 * T + 128)
         make_identity(nc, ident[:])
 
         def load(tile, src, cut):
@@ -89,9 +91,9 @@ def tile_attend_x_alibi_gate_srt_kernel(tc, qT, kT, vT, vs, pos, slope, og, offs
             else:
                 nc.sync.dma_start(tile[:], src)
 
-        kp.append(buffer(6, "k_plane1"))
+        kp.append(buffer(6, "k_plane1", at=SHIFT))
         load(kp[1], k_planes[:, 1, :], False)
-        slope_sb = buffer(6, "slope_sb", (P, 1), at=4 * T + 64)
+        slope_sb = buffer(6, "slope_sb", (P, 1), at=SHIFT + 4 * T + 64)
         nc.sync.dma_start(slope_sb[:], slope[0])
         k_grp = [keep.tile([P, HALF, 4], BF16, name=f"k_grp{h}", align_bytes=64) for h in range(2)]
         listed = [offsets[:, h * 32 : (h + 1) * 32] for h in range(2)]
@@ -133,22 +135,23 @@ def tile_attend_x_alibi_gate_srt_kernel(tc, qT, kT, vT, vs, pos, slope, og, offs
         for h in range(2):
             c = slice(h * HALF, (h + 1) * HALF)
             nc.scalar.copy(k_grp[h][:, :, 0:2], k_pair[:].rearrange("p (t n) -> p n t", t=2)[:, c, :])
-        vs_col = buffer(6, "vs_col", (P, 2, 4), at=4 * T - 64)
+        vs_col = buffer(6, "vs_col", (P, 2, 4), at=SHIFT + 4 * T - 64)
         for g in range(2):
             turned = banks.tile([P, 4, P], F32, name="turned", tag="turn", bufs=4)
             for j in range(4):
                 at = g * HALF + j * P
                 nc.tensor.transpose(turned[:, j, :], vs_g[:, at : at + P], ident[:])
             nc.vector.tensor_reduce(vs_col[:, g, :], turned[:, :, 4:P:64], AX.X, ALU.add)
-        vs_all = keep.tile([P, 2, HALF], F32, name="vs_all")
+        vs_all = {}
         for g in (1, 0):
             spread = banks.tile([P, 4, P], F32, name="spread", tag="head", bufs=2)
             for j in range(4):
                 nc.tensor.transpose(spread[:, j, :], vs_col[:, g, j : j + 1].to_broadcast([P, P]), ident[:])
-            nc.vector.tensor_copy(runs(vs_all[:, g]), dealt(spread))
+            vs_all[g] = spread
 
         vp = [buffer(6, "v_plane0", at=-256)]
-        load(vp[0], vT[0:P, :], False)
+        for c in V_CASTS[:-1] + [slice(V_CASTS[-1].start, T)]:
+            nc.sync.dma_start(vp[0][:, c], vT[0:P, c])
 
         for h in range(2):
             nc.vector.tensor_copy(k_grp[h][:, :, 2], kp[2][:, : (FIRST, T)[h]].indirect(listed[h]))
@@ -182,14 +185,23 @@ def tile_attend_x_alibi_gate_srt_kernel(tc, qT, kT, vT, vs, pos, slope, og, offs
             )
             score[h] = s_ps
 
+        v_cast = buffer(0, "v_cast", (P, FIRST), BF16, at=4 * N)
+        for c in V_CASTS:
+            nc.scalar.activation(v_cast[:, c], vp[0][:, c], ACT.Copy)
         v_g = [[None, None], [None, None]]
 
         def gather_values(e, g, tag):
-            v_g[e][g] = keep.tile([P, HALF], BF16, name=f"v_g{e}{g}", tag=tag)
+            if (e, g) == (0, 0):
+                v_g[e][g] = buffer(3, "v_g00", (P, HALF), BF16)
+            else:
+                v_g[e][g] = keep.tile([P, HALF], BF16, name=f"v_g{e}{g}", tag=tag)
             places = v_g[e][g][:].rearrange("p (u b j) -> p b u j", u=2, j=16)
-            nc.vector.tensor_copy(places, vp[e][:, : (FIRST, T)[g]].indirect(listed[g]))
+            if (e, g) == (0, 0):
+                nc.scalar.activation(places, v_cast[:].indirect(listed[g]), ACT.Copy)
+            else:
+                nc.vector.tensor_copy(places, vp[e][:, : (FIRST, T)[g]].indirect(listed[g]))
 
-        v_both = [buffer(1, f"v_both{e}", (P, 2 * P * 4), BF16, at=2048 * e) for e in range(2)]
+        v_both = [buffer((3, 1)[e], f"v_both{e}", (P, 2 * P * 4), BF16, at=2048) for e in range(2)]
         v_grp = [[v_both[e][:, g * 4 * P : (g + 1) * 4 * P] for g in range(2)] for e in range(2)]
 
         def turn(bank, rows, grouped):
@@ -208,7 +220,7 @@ def tile_attend_x_alibi_gate_srt_kernel(tc, qT, kT, vT, vs, pos, slope, og, offs
         def quantise(codes, scales, grouped):
             nc.vector.quantize_mx(out=codes.bitcast(FP8X4), scales=scales, in_=grouped)
 
-        s_sb = keep.tile([P, 2, HALF], F32, name="s_sb", tag="scores")
+        s_sb = buffer(3, "s_sb", (P, 2, HALF))
         for h in (1, 0):
             nc.vector.tensor_tensor(
                 runs(s_sb[:, h]),
@@ -220,14 +232,14 @@ def tile_attend_x_alibi_gate_srt_kernel(tc, qT, kT, vT, vs, pos, slope, og, offs
         nc.vector.tensor_reduce(
             neg_max[:], s_sb[:].rearrange("q h n -> q (h n)"), AX.X, ALU.max, negate=True
         )
-        prob = keep.tile([P, 2, HALF], F32, name="prob")
-        sums = keep.tile([P, 2], F32, name="sums", tag="sums")
+        prob = [keep.tile([P, HALF], F32, name=f"prob{h}") for h in range(2)]
+        sums = keep.tile([P, 2], F32, name="sums")
         for h in (1, 0):
             nc.scalar.activation(
-                prob[:, h], s_sb[:, h], ACT.Exp, bias=neg_max[:], accum_out=sums[:, h : h + 1]
+                prob[h][:], s_sb[:, h], ACT.Exp, bias=neg_max[:], accum_out=sums[:, h : h + 1]
             )
-        gather_values(0, 0, "bias")
-        gather_values(0, 1, "v_g01")
+        gather_values(0, 0, "scores")
+        gather_values(0, 1, "bias")
 
         total = keep.tile([P, 1], F32, name="total")
         nc.scalar.activation(total[:], sums[:, 0:1], ACT.Identity, bias=sums[:, 1:2])
@@ -238,12 +250,12 @@ def tile_attend_x_alibi_gate_srt_kernel(tc, qT, kT, vT, vs, pos, slope, og, offs
         v_codes = [buffer(7, "v_codes0", (P, 2, P), U32, at=1024), buffer(7, "v_codes1", (P, 2, P), U32, at=4096)]
         v_scales = [keep.tile([P, 2, P], U8, name=f"v_scales{e}", align_bytes=64) for e in range(2)]
         for g in (1, 0):
-            nc.gpsimd.tensor_tensor(w_row[g][:], prob[:, g], vs_all[:, g], ALU.mult)
-        turn_values(0, 0)
+            nc.vector.tensor_tensor(runs(w_row[g][:]), runs(prob[g][:]), dealt(vs_all[g]), ALU.mult)
         turn_values(0, 1)
         for g in (1, 0):
             w_ps = banks.tile([P, 2, P], F32, name="w_ps", tag="turn", bufs=4)
             turn(w_ps, w_row[g][:], w_grp[g][:])
+        turn_values(0, 0)
         gather_values(1, 0, "v_g10")
         gather_values(1, 1, "v_g11")
         turn_values(1, 0)

@@ -24,8 +24,18 @@ LAST_CASTS = [slice(0, 1280), slice(1280, 2560), slice(2560, FIRST)]
 LAST_LOADS = LAST_CASTS + [slice(FIRST, T)]
 V_CASTS = [slice(0, 1536), slice(1536, 3072), slice(3072, FIRST)]
 K_CHUNKS = [slice(0, T // 2), slice(T // 2, T)]
-SPARE = 768
-SHIFT = 4 * HALF
+WHOLE = [slice(0, T)]
+HALVES = [slice(0, FIRST), slice(FIRST, T)]
+PLANE = 4 * T
+AT_POS = 0
+AT_VS = PLANE + 256
+AT_K1 = AT_VS + PLANE
+AT_K0 = AT_K1 + PLANE
+AT_K2 = AT_K0 + PLANE
+AT_V1 = AT_K2 + 256
+AT_S = AT_V1 + PLANE
+AT_PAIR = AT_S + 8192
+AT_GRP = AT_PAIR + 4096
 FLOPS = 2 * N * D * P + 2 * N * P * DV
 BYTES = 4 * (D * P + D * T + DV * T + 2 * T + P + 2 * P * DV) + 2 * P * (N // 16)
 
@@ -36,134 +46,125 @@ def tile_attend_x_alibi_gate_srt_kernel(tc, qT, kT, vT, vs, pos, slope, og, offs
         keep = ctx.enter_context(tc.tile_pool(name="keep", bufs=1))
         banks = ctx.enter_context(tc.psum_pool(name="banks", bufs=1))
 
-        offsets = keep.tile([P, N // 16], U16, name="offsets")
+        offsets = keep.tile([P, N // 16], U16, name="offsets", align_bytes=256)
         nc.sync.dma_start(offsets[:], offs)
 
         planes = ctx.enter_context(tc.tile_pool(name="planes", bufs=1))
 
-        def buffer(b, name, shape=(P, T), dtype=F32, at=0):
-            align = 256 if shape == (P, T) else 64
-            return planes.tile(list(shape), dtype, name=name, align_bytes=align, offset=(4 * T + SPARE) * b + at + SHIFT * (b > 6))
+        def placed(name, at, shape=(P, T), dtype=F32, align=256):
+            return planes.tile(list(shape), dtype, name=name, align_bytes=align, offset=at)
 
-        pos_row = buffer(0, "pos_row")
-        vs_row = buffer(1, "vs_row")
+        pos_row = placed("pos_row", AT_POS)
+        vs_row = placed("vs_row", AT_VS - 128, align=64)
+        ident_made = placed("ident_made", AT_K1 - 192, (P, P), BF16, 64)
+        make_identity(nc, ident_made[:])
         k_planes = kT.rearrange("(p t) n -> p t n", t=4)
-        kp = [buffer(2, "k_plane0")]
-        q_grp = buffer(7, "q_grp", (P, P, 4), BF16, at=-SPARE - 128)
+        slope_row = keep.tile([P, P], F32, name="slope_row", align_bytes=256)
+        nc.vector.memset(slope_row[:], 0.0)
+        nc.vector.memset(pos_row[:], 0.0)
+        ident = keep.tile([P, P], F32, name="ident", align_bytes=64)
+        nc.vector.tensor_copy(ident[:], ident_made[:])
+        nc.vector.memset(vs_row[:], 0.0)
 
-        nc.gpsimd.memset(vs_row[:], 0.0)
-        nc.vector.memset(pos_row[:, : T - 1], 0.0)
-        nc.vector.memset(pos_row[:, T - 1 :], 0.0)
+        def load(tile, src, cuts):
+            for c in cuts:
+                nc.sync.dma_start(tile[:, c], src[:, c])
 
-        q_raw = keep.tile([P, 4, P], F32, name="q_raw")
-        nc.scalar.dma_start(q_raw[:], qT[0].rearrange("(p t) q -> p t q", t=4))
-        og_sb = keep.tile([P, DV], F32, name="og_sb")
-        nc.scalar.dma_start(og_sb[:], og[0])
-        for c in K_CHUNKS:
-            nc.sync.dma_start(kp[0][:, c], k_planes[:, 0, c])
-        for row, src, first, queue in ((pos_row, pos, 0, nc.sync), (vs_row, vs, 4, nc.scalar)):
+        def load_row(row, src, first):
             for u in range(2):
                 c = slice(u * T // 2, (u + 1) * T // 2)
                 at = first + 64 * u
-                queue.dma_start(row[at : at + 1, c], src[0:1, c])
+                nc.sync.dma_start(row[at : at + 1, c], src[0:1, c])
 
-        gate = keep.tile([P, DV], F32, name="gate")
-        half_tanh = keep.tile([P, DV], F32, name="half_tanh")
-        nc.scalar.activation(half_tanh[:], og_sb[:], ACT.Tanh, scale=0.5)
-        nc.scalar.activation(gate[:], half_tanh[:], ACT.Identity, scale=0.5, bias=0.5)
+        q_raw = keep.tile([P, 4, P], F32, name="q_raw", align_bytes=256)
+        nc.scalar.dma_start(q_raw[:], qT[0].rearrange("(p t) q -> p t q", t=4))
+        nc.scalar.dma_start(slope_row[0:1, :], slope[0].rearrange("q o -> o q"))
+        kp = [placed("k_plane0", AT_K0)]
+        load(kp[0], k_planes[:, 0, :], K_CHUNKS)
+        load_row(pos_row, pos, 0)
+        kp.append(placed("k_plane1", AT_K1))
+        load(kp[1], k_planes[:, 1, :], WHOLE)
+        load_row(vs_row, vs, 4)
 
+        q_grp = placed("q_grp", AT_K2, (P, P, 4), BF16)
         nc.scalar.copy(q_grp[:], q_raw[:].rearrange("p t q -> p q t"))
         q_codes = keep.tile([P, P], U32, name="q_codes", align_bytes=64)
-        q_scales = keep.tile([P, P], U8, name="q_scales", align_bytes=64)
+        q_scales = placed("q_scales", AT_K1 - 128, (P, P), U8, 64)
         nc.vector.quantize_mx(
             out=q_codes[:].bitcast(FP8X4),
             scales=q_scales[:],
             in_=q_grp[:].rearrange("p q t -> p (q t)"),
         )
+        kp.append(placed("k_plane2", AT_K2))
+        load(kp[2], k_planes[:, 2, :], HALVES)
 
-        ident = buffer(6, "ident", (P, P), at=SHIFT + 4 * T + 128)
-        make_identity(nc, ident[:])
+        slope_col = banks.tile([P, P], F32, name="slope_col", tag="turn", bufs=4)
+        nc.tensor.transpose(slope_col[:], slope_row[:], ident[:])
+        slope_sb = keep.tile([P, 1], F32, name="slope_sb")
+        nc.scalar.copy(slope_sb[:], slope_col[:, 0:1])
 
-        def load(tile, src, cut):
-            if cut:
-                nc.sync.dma_start(tile[:, :FIRST], src[:, :FIRST])
-                nc.sync.dma_start(tile[:, FIRST:], src[:, FIRST:])
-            else:
-                nc.sync.dma_start(tile[:], src)
-
-        kp.append(buffer(6, "k_plane1", at=SHIFT))
-        load(kp[1], k_planes[:, 1, :], False)
-        slope_sb = buffer(6, "slope_sb", (P, 1), at=SHIFT + 4 * T + 64)
-        nc.sync.dma_start(slope_sb[:], slope[0])
-        k_grp = [keep.tile([P, HALF, 4], BF16, name=f"k_grp{h}", align_bytes=64) for h in range(2)]
+        k_grp = [placed(f"k_grp{h}", AT_GRP + 4096 * h, (P, HALF, 4), BF16) for h in range(2)]
         listed = [offsets[:, h * 32 : (h + 1) * 32] for h in range(2)]
-        k_cast = buffer(6, "k_cast", (P, T), BF16, at=-2 * T)
+        k_cast = keep.tile([P, T], BF16, name="k_cast", align_bytes=64)
         for c in K_CHUNKS:
             nc.scalar.activation(k_cast[:, c], kp[0][:, c], ACT.Copy)
-        k_pair = keep.tile([P, 2 * N], BF16, name="k_pair")
-        nc.scalar.activation(k_pair[:, :N], k_cast[:].indirect(offsets[:]), ACT.Copy)
-        kp.append(buffer(7, "k_plane2"))
-        load(kp[2], k_planes[:, 2, :], True)
 
-        pos_g = keep.tile([P, N], F32, name="pos_g")
-        nc.vector.tensor_copy(pos_g[:], pos_row[:].indirect(offsets[:]))
-        kp.append(buffer(5, "k_plane3"))
-        for c in LAST_LOADS:
-            nc.sync.dma_start(kp[3][:, c], k_planes[:, 3, c])
-        vs_g = buffer(0, "vs_g", (P, N))
-        nc.vector.tensor_copy(vs_g[:], vs_row[:].indirect(offsets[:]))
-        pos_col = keep.tile([P, 2, 4], F32, name="pos_col")
-        for g in range(2):
-            turned = banks.tile([P, 4, P], F32, name="turned", tag="turn", bufs=4)
-            for j in range(4):
-                at = g * HALF + j * P
-                nc.tensor.transpose(turned[:, j, :], pos_g[:, at : at + P], ident[:])
-            nc.vector.tensor_reduce(pos_col[:, g, :], turned[:, :, 0:P:64], AX.X, ALU.add)
         def dealt(bank):
             return bank[:].rearrange("q j n -> q (j n)").rearrange("q (b u j) -> q u b j", u=2, j=16)
 
         def runs(row):
             return row.rearrange("q (u b j) -> q u b j", u=2, j=16)
 
+        def spread_out(gathered, first, col):
+            for g in range(2):
+                turned = banks.tile([P, 4, P], F32, name="turned", tag="turn", bufs=4)
+                for j in range(4):
+                    at = g * HALF + j * P
+                    nc.tensor.transpose(turned[:, j, :], gathered[:, at : at + P], ident[:])
+                nc.vector.tensor_reduce(col[:, g, :4], turned[:, :, first:P:64], AX.X, ALU.add)
+            spreads = {}
+            for g in (1, 0):
+                spread = banks.tile([P, 4, P], F32, name="spread", tag="head", bufs=2)
+                for j in range(4):
+                    nc.tensor.transpose(spread[:, j, :], col[:, g, j : j + 1].to_broadcast([P, P]), ident[:])
+                spreads[g] = spread
+            return spreads
+
+        pos_g = placed("pos_g", AT_PAIR, (P, N))
+        for h in range(2):
+            nc.vector.tensor_copy(pos_g[:, h * HALF : (h + 1) * HALF], pos_row[:].indirect(listed[h]))
+        kp.append(placed("k_plane3", AT_POS))
+        load(kp[3], k_planes[:, 3, :], LAST_LOADS)
+        pos_col = placed("pos_col", AT_GRP + 4096 - 32, (P, 2, 8), F32, 32)
+        pos_all = spread_out(pos_g, 0, pos_col)
+        k_pair = placed("k_pair", AT_PAIR, (P, 2 * N), BF16)
+        nc.scalar.activation(k_pair[:, :N], k_cast[:].indirect(offsets[:]), ACT.Copy)
         bias = keep.tile([P, 2, HALF], F32, name="bias")
         for g in (1, 0):
-            spread = banks.tile([P, 4, P], F32, name="spread", tag="head", bufs=2)
-            for j in range(4):
-                nc.tensor.transpose(spread[:, j, :], pos_col[:, g, j : j + 1].to_broadcast([P, P]), ident[:])
-            nc.scalar.activation(runs(bias[:, g]), dealt(spread), ACT.Copy, scale=slope_sb[:])
+            nc.scalar.activation(runs(bias[:, g]), dealt(pos_all[g]), ACT.Copy, scale=slope_sb[:])
+
         nc.vector.tensor_copy(k_pair[:, N:], kp[1][:].indirect(offsets[:]))
         for h in range(2):
             c = slice(h * HALF, (h + 1) * HALF)
             nc.scalar.copy(k_grp[h][:, :, 0:2], k_pair[:].rearrange("p (t n) -> p n t", t=2)[:, c, :])
-        vs_col = buffer(6, "vs_col", (P, 2, 4), at=SHIFT + 4 * T - 64)
-        for g in range(2):
-            turned = banks.tile([P, 4, P], F32, name="turned", tag="turn", bufs=4)
-            for j in range(4):
-                at = g * HALF + j * P
-                nc.tensor.transpose(turned[:, j, :], vs_g[:, at : at + P], ident[:])
-            nc.vector.tensor_reduce(vs_col[:, g, :], turned[:, :, 4:P:64], AX.X, ALU.add)
-        vs_all = {}
-        for g in (1, 0):
-            spread = banks.tile([P, 4, P], F32, name="spread", tag="head", bufs=2)
-            for j in range(4):
-                nc.tensor.transpose(spread[:, j, :], vs_col[:, g, j : j + 1].to_broadcast([P, P]), ident[:])
-            vs_all[g] = spread
-
-        vp = [buffer(6, "v_plane0", at=-256)]
-        for c in V_CASTS[:-1] + [slice(V_CASTS[-1].start, T)]:
-            nc.sync.dma_start(vp[0][:, c], vT[0:P, c])
+        vs_g = placed("vs_g", AT_K1 + 256, (P, N))
+        nc.vector.tensor_copy(vs_g[:], vs_row[:].indirect(offsets[:]))
+        vp = [placed("v_plane0", AT_VS - 256)]
+        load(vp[0], vT[0:P, :], V_CASTS[:-1] + [slice(V_CASTS[-1].start, T)])
 
         for h in range(2):
             nc.vector.tensor_copy(k_grp[h][:, :, 2], kp[2][:, : (FIRST, T)[h]].indirect(listed[h]))
-        vp.append(buffer(7, "v_plane1"))
-        load(vp[1], vT[P : 2 * P, :], True)
-        last_cast = keep.tile([P, FIRST], BF16, name="last_cast")
+        vs_col = placed("vs_col", AT_K2, (P, 2, 4))
+        vs_all = spread_out(vs_g, 4, vs_col)
+        vp.append(placed("v_plane1", AT_V1))
+        load(vp[1], vT[P : 2 * P, :], HALVES)
+        last_cast = keep.tile([P, FIRST], BF16, name="last_cast", align_bytes=64)
         for c in LAST_CASTS[:-1]:
             nc.scalar.activation(last_cast[:, c], kp[3][:, c], ACT.Copy)
         nc.vector.tensor_copy(last_cast[:, LAST_CASTS[-1]], kp[3][:, LAST_CASTS[-1]])
         nc.scalar.activation(k_grp[0][:, :, 3], last_cast[:].indirect(listed[0]), ACT.Copy)
         nc.vector.tensor_copy(k_grp[1][:, :, 3], kp[3][:].indirect(listed[1]))
-        k_codes = buffer(5, "k_codes", (P, N), U32)
+        k_codes = placed("k_codes", AT_POS, (P, N), U32)
         k_scales = keep.tile([P, N], U8, name="k_scales", align_bytes=64)
         score = {}
         for h in (1, 0):
@@ -185,14 +186,14 @@ def tile_attend_x_alibi_gate_srt_kernel(tc, qT, kT, vT, vs, pos, slope, og, offs
             )
             score[h] = s_ps
 
-        v_cast = buffer(0, "v_cast", (P, FIRST), BF16, at=4 * N)
+        v_cast = keep.tile([P, FIRST], BF16, name="v_cast", align_bytes=64)
         for c in V_CASTS:
             nc.scalar.activation(v_cast[:, c], vp[0][:, c], ACT.Copy)
         v_g = [[None, None], [None, None]]
 
         def gather_values(e, g, tag):
             if (e, g) == (0, 0):
-                v_g[e][g] = buffer(3, "v_g00", (P, HALF), BF16)
+                v_g[e][g] = placed("v_g00", AT_S, (P, HALF), BF16)
             else:
                 v_g[e][g] = keep.tile([P, HALF], BF16, name=f"v_g{e}{g}", tag=tag)
             places = v_g[e][g][:].rearrange("p (u b j) -> p b u j", u=2, j=16)
@@ -201,8 +202,10 @@ def tile_attend_x_alibi_gate_srt_kernel(tc, qT, kT, vT, vs, pos, slope, og, offs
             else:
                 nc.vector.tensor_copy(places, vp[e][:, : (FIRST, T)[g]].indirect(listed[g]))
 
-        v_both = [buffer((3, 1)[e], f"v_both{e}", (P, 2 * P * 4), BF16, at=2048) for e in range(2)]
-        v_grp = [[v_both[e][:, g * 4 * P : (g + 1) * 4 * P] for g in range(2)] for e in range(2)]
+        early = placed("early", AT_S + 2048, (P, 4 * HALF), BF16)
+        late = [placed(f"late{g}", AT_S + 6144 + 1024 * g, (P, HALF), BF16) for g in range(2)]
+        v_grp = [[early[:, g * HALF : (g + 1) * HALF] for g in range(2)], [late[g][:] for g in range(2)]]
+        w_grp = [early[:, (2 + g) * HALF : (3 + g) * HALF] for g in range(2)]
 
         def turn(bank, rows, grouped):
             words = rows.bitcast(F32)
@@ -220,7 +223,7 @@ def tile_attend_x_alibi_gate_srt_kernel(tc, qT, kT, vT, vs, pos, slope, og, offs
         def quantise(codes, scales, grouped):
             nc.vector.quantize_mx(out=codes.bitcast(FP8X4), scales=scales, in_=grouped)
 
-        s_sb = buffer(3, "s_sb", (P, 2, HALF))
+        s_sb = placed("s_sb", AT_S, (P, 2, HALF))
         for h in (1, 0):
             nc.vector.tensor_tensor(
                 runs(s_sb[:, h]),
@@ -244,45 +247,51 @@ def tile_attend_x_alibi_gate_srt_kernel(tc, qT, kT, vT, vs, pos, slope, og, offs
         total = keep.tile([P, 1], F32, name="total")
         nc.scalar.activation(total[:], sums[:, 0:1], ACT.Identity, bias=sums[:, 1:2])
         w_row = [keep.tile([P, HALF], BF16, name=f"w_row{g}") for g in range(2)]
-        w_grp = [keep.tile([P, 4 * P], BF16, name=f"w_grp{g}", align_bytes=64) for g in range(2)]
-        w_codes = [buffer(7, f"w_codes{g}", (P, P), U32, at=512 * g) for g in range(2)]
-        w_scales = [keep.tile([P, P], U8, name=f"w_scales{g}", align_bytes=64) for g in range(2)]
-        v_codes = [buffer(7, "v_codes0", (P, 2, P), U32, at=1024), buffer(7, "v_codes1", (P, 2, P), U32, at=4096)]
-        v_scales = [keep.tile([P, 2, P], U8, name=f"v_scales{e}", align_bytes=64) for e in range(2)]
+        early_codes = placed("early_codes", AT_V1, (P, 4 * P), U32)
+        early_scales = keep.tile([P, 4 * P], U8, name="early_scales", align_bytes=64)
+        late_codes = placed("late_codes", AT_V1 + 2048, (P, 2 * P), U32)
+        late_scales = keep.tile([P, 2 * P], U8, name="late_scales", align_bytes=64)
+        blocks = [slice(j * P, (j + 1) * P) for j in range(4)]
+        w_codes = [early_codes[:, blocks[2 + g]] for g in range(2)]
+        w_scales = [early_scales[:, blocks[2 + g]] for g in range(2)]
+        v_codes = [[codes[:, blocks[g]] for g in range(2)] for codes in (early_codes, late_codes)]
+        v_scales = [[scales[:, blocks[g]] for g in range(2)] for scales in (early_scales, late_scales)]
         for g in (1, 0):
             nc.vector.tensor_tensor(runs(w_row[g][:]), runs(prob[g][:]), dealt(vs_all[g]), ALU.mult)
         turn_values(0, 1)
         for g in (1, 0):
             w_ps = banks.tile([P, 2, P], F32, name="w_ps", tag="turn", bufs=4)
-            turn(w_ps, w_row[g][:], w_grp[g][:])
+            turn(w_ps, w_row[g][:], w_grp[g])
         turn_values(0, 0)
+        og_sb = placed("og_sb", AT_POS + 8192, (P, DV))
+        nc.sync.dma_start(og_sb[:], og[0])
+        half_tanh = keep.tile([P, DV], F32, name="half_tanh")
+        nc.scalar.activation(half_tanh[:], og_sb[:], ACT.Tanh, scale=0.5)
         gather_values(1, 0, "v_g10")
         gather_values(1, 1, "v_g11")
         turn_values(1, 0)
         turn_values(1, 1)
-        quantise(w_codes[0][:], w_scales[0][:], w_grp[0][:])
-        quantise(
-            v_codes[0][:].rearrange("p g e -> p (g e)"), v_scales[0][:].rearrange("p g e -> p (g e)"), v_both[0][:]
-        )
-        quantise(w_codes[1][:], w_scales[1][:], w_grp[1][:])
-        inv = buffer(7, "inv", (P, 1), at=6144)
+        gate = keep.tile([P, DV], F32, name="gate", tag="v_g11")
+        nc.scalar.activation(gate[:], half_tanh[:], ACT.Identity, scale=0.5, bias=0.5)
+        quantise(early_codes[:], early_scales[:], early[:])
+        quantise(v_codes[1][0], v_scales[1][0], v_grp[1][0])
+        inv = placed("inv", AT_V1 + 4096, (P, 1))
         nc.vector.reciprocal(inv[:], total[:])
-        quantise(v_codes[1][:, 0], v_scales[1][:, 0], v_grp[1][0])
-        quantise(v_codes[1][:, 1], v_scales[1][:, 1], v_grp[1][1])
+        quantise(v_codes[1][1], v_scales[1][1], v_grp[1][1])
 
         for e in range(2):
             y_ps = banks.tile([P, P], F32, name="y_ps", tag="head", bufs=2)
             for g in range(2):
                 nc.tensor.matmul_mx(
                     out=y_ps[:],
-                    lhsT=w_codes[g][:].bitcast(FP8X4),
-                    lhsT_scale=w_scales[g][:],
-                    rhs=v_codes[e][:, g].bitcast(FP8X4),
-                    rhs_scale=v_scales[e][:, g],
+                    lhsT=w_codes[g].bitcast(FP8X4),
+                    lhsT_scale=w_scales[g],
+                    rhs=v_codes[e][g].bitcast(FP8X4),
+                    rhs_scale=v_scales[e][g],
                     start=(g == 0),
                     stop=(g == 1),
                 )
             c = slice(e * P, (e + 1) * P)
-            y_sb = keep.tile([P, P], F32, name=f"y_sb{e}")
+            y_sb = keep.tile([P, P], F32, name=f"y_sb{e}", align_bytes=256)
             nc.vector.scalar_tensor_tensor(y_sb[:], y_ps[:], inv[:], gate[:, c], ALU.mult, ALU.mult)
             nc.sync.dma_start(out[0][:, c], y_sb[:])

@@ -22,8 +22,6 @@ HALF = 512
 FIRST = T - HALF
 LAST_CASTS = [slice(0, 1280), slice(1280, 2560), slice(2560, FIRST)]
 LAST_LOADS = LAST_CASTS + [slice(FIRST, T)]
-V_CASTS = [slice(0, 1536), slice(1536, 3072), slice(3072, FIRST)]
-K_CHUNKS = [slice(0, T // 2), slice(T // 2, T)]
 WHOLE = [slice(0, T)]
 HALVES = [slice(0, FIRST), slice(FIRST, T)]
 PLANE = 4 * T
@@ -80,7 +78,7 @@ def tile_attend_x_alibi_gate_srt_kernel(tc, qT, kT, vT, vs, pos, slope, og, offs
         nc.scalar.dma_start(q_raw[:], qT[0].rearrange("(p t) q -> p t q", t=4))
         nc.scalar.dma_start(slope_row[0:1, :], slope[0].rearrange("q o -> o q"))
         kp = [placed("k_plane0", AT_K0)]
-        load(kp[0], k_planes[:, 0, :], K_CHUNKS)
+        load(kp[0], k_planes[:, 0, :], WHOLE)
         load_row(pos_row, pos, 0)
         kp.append(placed("k_plane1", AT_K1))
         load(kp[1], k_planes[:, 1, :], WHOLE)
@@ -105,9 +103,6 @@ def tile_attend_x_alibi_gate_srt_kernel(tc, qT, kT, vT, vs, pos, slope, og, offs
 
         k_grp = [placed(f"k_grp{h}", AT_GRP + 4096 * h, (P, HALF, 4), BF16) for h in range(2)]
         listed = [offsets[:, h * 32 : (h + 1) * 32] for h in range(2)]
-        k_cast = keep.tile([P, T], BF16, name="k_cast", align_bytes=64)
-        for c in K_CHUNKS:
-            nc.scalar.activation(k_cast[:, c], kp[0][:, c], ACT.Copy)
 
         def dealt(bank):
             return bank[:].rearrange("q j n -> q (j n)").rearrange("q (b u j) -> q u b j", u=2, j=16)
@@ -138,7 +133,7 @@ def tile_attend_x_alibi_gate_srt_kernel(tc, qT, kT, vT, vs, pos, slope, og, offs
         pos_col = placed("pos_col", AT_GRP + 4096 - 32, (P, 2, 8), F32, 32)
         pos_all = spread_out(pos_g, 0, pos_col)
         k_pair = placed("k_pair", AT_PAIR, (P, 2 * N), BF16)
-        nc.scalar.activation(k_pair[:, :N], k_cast[:].indirect(offsets[:]), ACT.Copy)
+        nc.scalar.activation(k_pair[:, :N], kp[0][:].indirect(offsets[:]), ACT.Copy)
         bias = keep.tile([P, 2, HALF], F32, name="bias")
         for g in (1, 0):
             nc.scalar.activation(runs(bias[:, g]), dealt(pos_all[g]), ACT.Copy, scale=slope_sb[:])
@@ -150,7 +145,7 @@ def tile_attend_x_alibi_gate_srt_kernel(tc, qT, kT, vT, vs, pos, slope, og, offs
         vs_g = placed("vs_g", AT_K1 + 256, (P, N))
         nc.vector.tensor_copy(vs_g[:], vs_row[:].indirect(offsets[:]))
         vp = [placed("v_plane0", AT_VS - 256)]
-        load(vp[0], vT[0:P, :], V_CASTS[:-1] + [slice(V_CASTS[-1].start, T)])
+        load(vp[0], vT[0:P, :], WHOLE)
 
         for h in range(2):
             nc.vector.tensor_copy(k_grp[h][:, :, 2], kp[2][:, : (FIRST, T)[h]].indirect(listed[h]))
@@ -186,21 +181,19 @@ def tile_attend_x_alibi_gate_srt_kernel(tc, qT, kT, vT, vs, pos, slope, og, offs
             )
             score[h] = s_ps
 
-        v_cast = keep.tile([P, FIRST], BF16, name="v_cast", align_bytes=64)
-        for c in V_CASTS:
-            nc.scalar.activation(v_cast[:, c], vp[0][:, c], ACT.Copy)
+        v_listed = keep.tile([P, HALF], BF16, name="v_listed", align_bytes=64)
+        nc.scalar.activation(v_listed[:], vp[0][:].indirect(listed[0]), ACT.Copy)
         v_g = [[None, None], [None, None]]
+        v_g[0][0] = keep.tile([P, HALF], BF16, name="v_g00", align_bytes=64)
+        nc.scalar.copy(
+            v_g[0][0][:].bitcast(F32).rearrange("e (u b r) -> e u b r", u=2, r=8),
+            v_listed[:].bitcast(F32).rearrange("e (b u r) -> e u b r", u=2, r=8),
+        )
 
         def gather_values(e, g, tag):
-            if (e, g) == (0, 0):
-                v_g[e][g] = placed("v_g00", AT_S, (P, HALF), BF16)
-            else:
-                v_g[e][g] = keep.tile([P, HALF], BF16, name=f"v_g{e}{g}", tag=tag)
+            v_g[e][g] = keep.tile([P, HALF], BF16, name=f"v_g{e}{g}", tag=tag)
             places = v_g[e][g][:].rearrange("p (u b j) -> p b u j", u=2, j=16)
-            if (e, g) == (0, 0):
-                nc.scalar.activation(places, v_cast[:].indirect(listed[g]), ACT.Copy)
-            else:
-                nc.vector.tensor_copy(places, vp[e][:, : (FIRST, T)[g]].indirect(listed[g]))
+            nc.vector.tensor_copy(places, vp[e][:, : (FIRST, T)[g]].indirect(listed[g]))
 
         early = placed("early", AT_S + 2048, (P, 4 * HALF), BF16)
         late = [placed(f"late{g}", AT_S + 6144 + 1024 * g, (P, HALF), BF16) for g in range(2)]
@@ -235,13 +228,13 @@ def tile_attend_x_alibi_gate_srt_kernel(tc, qT, kT, vT, vs, pos, slope, og, offs
         nc.vector.tensor_reduce(
             neg_max[:], s_sb[:].rearrange("q h n -> q (h n)"), AX.X, ALU.max, negate=True
         )
-        prob = [keep.tile([P, HALF], F32, name=f"prob{h}") for h in range(2)]
+        prob_all = keep.tile([P, N], F32, name="prob", tag="v_listed", align_bytes=64)
+        prob = [prob_all[:, h * HALF : (h + 1) * HALF] for h in range(2)]
         sums = keep.tile([P, 2], F32, name="sums")
         for h in (1, 0):
             nc.scalar.activation(
-                prob[h][:], s_sb[:, h], ACT.Exp, bias=neg_max[:], accum_out=sums[:, h : h + 1]
+                prob[h], s_sb[:, h], ACT.Exp, bias=neg_max[:], accum_out=sums[:, h : h + 1]
             )
-        gather_values(0, 0, "scores")
         gather_values(0, 1, "bias")
 
         total = keep.tile([P, 1], F32, name="total")
@@ -257,12 +250,12 @@ def tile_attend_x_alibi_gate_srt_kernel(tc, qT, kT, vT, vs, pos, slope, og, offs
         v_codes = [[codes[:, blocks[g]] for g in range(2)] for codes in (early_codes, late_codes)]
         v_scales = [[scales[:, blocks[g]] for g in range(2)] for scales in (early_scales, late_scales)]
         for g in (1, 0):
-            nc.vector.tensor_tensor(runs(w_row[g][:]), runs(prob[g][:]), dealt(vs_all[g]), ALU.mult)
+            nc.vector.tensor_tensor(runs(w_row[g][:]), runs(prob[g]), dealt(vs_all[g]), ALU.mult)
+        turn_values(0, 0)
         turn_values(0, 1)
         for g in (1, 0):
             w_ps = banks.tile([P, 2, P], F32, name="w_ps", tag="turn", bufs=4)
             turn(w_ps, w_row[g][:], w_grp[g])
-        turn_values(0, 0)
         og_sb = placed("og_sb", AT_POS + 8192, (P, DV))
         nc.sync.dma_start(og_sb[:], og[0])
         half_tanh = keep.tile([P, DV], F32, name="half_tanh")

@@ -22,6 +22,8 @@ HALF = 512
 FIRST = T - HALF
 LAST_CASTS = [slice(0, 1280), slice(1280, 2560), slice(2560, FIRST)]
 LAST_LOADS = LAST_CASTS + [slice(FIRST, T)]
+RUNS = (16, 2)
+V_SHARE = 224
 WHOLE = [slice(0, T)]
 HALVES = [slice(0, FIRST), slice(FIRST, T)]
 PLANE = 4 * T
@@ -104,11 +106,11 @@ def tile_attend_x_alibi_gate_srt_kernel(tc, qT, kT, vT, vs, pos, slope, og, offs
         k_grp = [placed(f"k_grp{h}", AT_GRP + 4096 * h, (P, HALF, 4), BF16) for h in range(2)]
         listed = [offsets[:, h * 32 : (h + 1) * 32] for h in range(2)]
 
-        def dealt(bank):
-            return bank[:].rearrange("q j n -> q (j n)").rearrange("q (b u j) -> q u b j", u=2, j=16)
+        def dealt(bank, g):
+            return bank[:].rearrange("q j n -> q (j n)").rearrange("q (b u j) -> q u b j", u=2, j=RUNS[g])
 
-        def runs(row):
-            return row.rearrange("q (u b j) -> q u b j", u=2, j=16)
+        def runs(row, g):
+            return row.rearrange("q (u b j) -> q u b j", u=2, j=RUNS[g])
 
         def spread_out(gathered, first, col):
             for g in range(2):
@@ -136,7 +138,7 @@ def tile_attend_x_alibi_gate_srt_kernel(tc, qT, kT, vT, vs, pos, slope, og, offs
         nc.scalar.activation(k_pair[:, :N], kp[0][:].indirect(offsets[:]), ACT.Copy)
         bias = keep.tile([P, 2, HALF], F32, name="bias")
         for g in (1, 0):
-            nc.scalar.activation(runs(bias[:, g]), dealt(pos_all[g]), ACT.Copy, scale=slope_sb[:])
+            nc.scalar.activation(runs(bias[:, g], g), dealt(pos_all[g], g), ACT.Copy, scale=slope_sb[:])
 
         nc.vector.tensor_copy(k_pair[:, N:], kp[1][:].indirect(offsets[:]))
         for h in range(2):
@@ -192,18 +194,26 @@ def tile_attend_x_alibi_gate_srt_kernel(tc, qT, kT, vT, vs, pos, slope, og, offs
 
         def gather_values(e, g, tag):
             v_g[e][g] = keep.tile([P, HALF], BF16, name=f"v_g{e}{g}", tag=tag)
-            places = v_g[e][g][:].rearrange("p (u b j) -> p b u j", u=2, j=16)
-            nc.vector.tensor_copy(places, vp[e][:, : (FIRST, T)[g]].indirect(listed[g]))
+            if g == 0:
+                places = v_g[e][g][:].rearrange("p (u b j) -> p b u j", u=2, j=16)
+                nc.vector.tensor_copy(places, vp[e][:, :FIRST].indirect(listed[g]))
+            elif e == 0:
+                nc.vector.tensor_copy(v_g[e][g][:], vp[e][:].indirect(listed[g]))
+            else:
+                cut = (HALF + V_SHARE) // 16
+                nc.scalar.activation(v_g[e][g][:, :V_SHARE], vp[e][:].indirect(offsets[:, HALF // 16 : cut]), ACT.Copy)
+                nc.vector.tensor_copy(v_g[e][g][:, V_SHARE:], vp[e][:].indirect(offsets[:, cut:]))
 
         early = placed("early", AT_S + 2048, (P, 4 * HALF), BF16)
         late = [placed(f"late{g}", AT_S + 6144 + 1024 * g, (P, HALF), BF16) for g in range(2)]
         v_grp = [[early[:, g * HALF : (g + 1) * HALF] for g in range(2)], [late[g][:] for g in range(2)]]
         w_grp = [early[:, (2 + g) * HALF : (3 + g) * HALF] for g in range(2)]
 
-        def turn(bank, rows, grouped):
+        def turn(bank, rows, grouped, in_list_order=False):
             words = rows.bitcast(F32)
             for u in range(2):
-                nc.tensor.transpose(bank[:, u, :], words[:, u * P : (u + 1) * P], ident[:])
+                pairs = words[:, u : 2 * P : 2] if in_list_order else words[:, u * P : (u + 1) * P]
+                nc.tensor.transpose(bank[:, u, :], pairs, ident[:])
             nc.scalar.copy(grouped.bitcast(F32).rearrange("p (e u) -> p e u", u=2), bank[:].rearrange("p u e -> p e u"))
 
         def turn_values(e, g):
@@ -211,7 +221,7 @@ def tile_attend_x_alibi_gate_srt_kernel(tc, qT, kT, vT, vs, pos, slope, og, offs
                 v_ps = banks.tile([P, 2, P], F32, name="v_ps", tag="turn", bufs=4)
             else:
                 v_ps = banks.tile([P, 2, P], F32, name="v_ps", tag=f"s_ps{g}")
-            turn(v_ps, v_g[e][g][:], v_grp[e][g])
+            turn(v_ps, v_g[e][g][:], v_grp[e][g], g == 1)
 
         def quantise(codes, scales, grouped):
             nc.vector.quantize_mx(out=codes.bitcast(FP8X4), scales=scales, in_=grouped)
@@ -219,9 +229,9 @@ def tile_attend_x_alibi_gate_srt_kernel(tc, qT, kT, vT, vs, pos, slope, og, offs
         s_sb = placed("s_sb", AT_S, (P, 2, HALF))
         for h in (1, 0):
             nc.vector.tensor_tensor(
-                runs(s_sb[:, h]),
-                score[h][:].rearrange("q (b u j) -> q u b j", u=2, j=16),
-                runs(bias[:, h]),
+                runs(s_sb[:, h], h),
+                score[h][:].rearrange("q (b u j) -> q u b j", u=2, j=RUNS[h]),
+                runs(bias[:, h], h),
                 ALU.add,
             )
         neg_max = keep.tile([P, 1], F32, name="neg_max")
@@ -250,7 +260,7 @@ def tile_attend_x_alibi_gate_srt_kernel(tc, qT, kT, vT, vs, pos, slope, og, offs
         v_codes = [[codes[:, blocks[g]] for g in range(2)] for codes in (early_codes, late_codes)]
         v_scales = [[scales[:, blocks[g]] for g in range(2)] for scales in (early_scales, late_scales)]
         for g in (1, 0):
-            nc.vector.tensor_tensor(runs(w_row[g][:]), runs(prob[g]), dealt(vs_all[g]), ALU.mult)
+            nc.vector.tensor_tensor(runs(w_row[g][:], g), runs(prob[g], g), dealt(vs_all[g], g), ALU.mult)
         turn_values(0, 0)
         turn_values(0, 1)
         for g in (1, 0):

@@ -20,22 +20,15 @@ T = 4096
 N = 1024
 HALF = 512
 FIRST = T - HALF
-LAST_CASTS = [slice(0, 1280), slice(1280, 2560), slice(2560, FIRST)]
-LAST_LOADS = LAST_CASTS + [slice(FIRST, T)]
-RUNS = (16, 2)
-V_SHARE = 224
+V0_SCALAR = 256
+V1_SCALAR = 288
 WHOLE = [slice(0, T)]
 HALVES = [slice(0, FIRST), slice(FIRST, T)]
 PLANE = 4 * T
 AT_POS = 0
-AT_VS = PLANE + 256
-AT_K1 = AT_VS + PLANE
-AT_K0 = AT_K1 + PLANE
-AT_K2 = AT_K0 + PLANE
-AT_V1 = AT_K2 + 256
-AT_S = AT_V1 + PLANE
-AT_PAIR = AT_S + 8192
-AT_GRP = AT_PAIR + 4096
+AT_VS = PLANE
+AT_K = [(2 + t) * PLANE for t in range(4)]
+AT_V = AT_K[:2]
 FLOPS = 2 * N * D * P + 2 * N * P * DV
 BYTES = 4 * (D * P + D * T + DV * T + 2 * T + P + 2 * P * DV) + 2 * P * (N // 16)
 
@@ -54,17 +47,8 @@ def tile_attend_x_alibi_gate_srt_kernel(tc, qT, kT, vT, vs, pos, slope, og, offs
         def placed(name, at, shape=(P, T), dtype=F32, align=256):
             return planes.tile(list(shape), dtype, name=name, align_bytes=align, offset=at)
 
-        pos_row = placed("pos_row", AT_POS)
-        vs_row = placed("vs_row", AT_VS - 128, align=64)
-        ident_made = placed("ident_made", AT_K1 - 192, (P, P), BF16, 64)
-        make_identity(nc, ident_made[:])
-        k_planes = kT.rearrange("(p t) n -> p t n", t=4)
-        slope_row = keep.tile([P, P], F32, name="slope_row", align_bytes=256)
-        nc.vector.memset(slope_row[:], 0.0)
-        nc.vector.memset(pos_row[:], 0.0)
-        ident = keep.tile([P, P], F32, name="ident", align_bytes=64)
-        nc.vector.tensor_copy(ident[:], ident_made[:])
-        nc.vector.memset(vs_row[:], 0.0)
+        def listed(lo, hi):
+            return offsets[:, lo // 16 : hi // 16]
 
         def load(tile, src, cuts):
             for c in cuts:
@@ -76,101 +60,97 @@ def tile_attend_x_alibi_gate_srt_kernel(tc, qT, kT, vT, vs, pos, slope, og, offs
                 at = first + 64 * u
                 nc.sync.dma_start(row[at : at + 1, c], src[0:1, c])
 
+        def quantise(codes, scales, grouped):
+            nc.vector.quantize_mx(out=codes.bitcast(FP8X4), scales=scales, in_=grouped)
+
+        pos_row = placed("pos_row", AT_POS)
+        vs_row = placed("vs_row", AT_VS)
+        ident_made = placed("ident_made", AT_K[2], (P, P), BF16)
+        make_identity(nc, ident_made[:])
+        slope_row = keep.tile([P, P], F32, name="slope_row", align_bytes=256)
+        nc.vector.memset(slope_row[:], 0.0)
+        nc.vector.memset(pos_row[:], 0.0)
+        nc.vector.memset(vs_row[:], 0.0)
+        ident = keep.tile([P, P], F32, name="ident", align_bytes=64)
+        nc.vector.tensor_copy(ident[:], ident_made[:])
+
+        k_planes = kT.rearrange("(p t) n -> p t n", t=4)
         q_raw = keep.tile([P, 4, P], F32, name="q_raw", align_bytes=256)
-        nc.scalar.dma_start(q_raw[:], qT[0].rearrange("(p t) q -> p t q", t=4))
-        nc.scalar.dma_start(slope_row[0:1, :], slope[0].rearrange("q o -> o q"))
-        kp = [placed("k_plane0", AT_K0)]
-        load(kp[0], k_planes[:, 0, :], WHOLE)
+        nc.sync.dma_start(q_raw[:], qT[0].rearrange("(p t) q -> p t q", t=4))
+        kp = [placed(f"k_plane{t}", AT_K[t]) for t in range(2)]
+        for t in range(2):
+            load(kp[t], k_planes[:, t, :], WHOLE)
+        nc.sync.dma_start(slope_row[0:1, :], slope[0].rearrange("q o -> o q"))
         load_row(pos_row, pos, 0)
-        kp.append(placed("k_plane1", AT_K1))
-        load(kp[1], k_planes[:, 1, :], WHOLE)
         load_row(vs_row, vs, 4)
 
-        q_grp = placed("q_grp", AT_K2, (P, P, 4), BF16)
+        q_grp = placed("q_grp", AT_K[3], (P, P, 4), BF16)
         nc.scalar.copy(q_grp[:], q_raw[:].rearrange("p t q -> p q t"))
         q_codes = keep.tile([P, P], U32, name="q_codes", align_bytes=64)
-        q_scales = placed("q_scales", AT_K1 - 128, (P, P), U8, 64)
-        nc.vector.quantize_mx(
-            out=q_codes[:].bitcast(FP8X4),
-            scales=q_scales[:],
-            in_=q_grp[:].rearrange("p q t -> p (q t)"),
-        )
-        kp.append(placed("k_plane2", AT_K2))
-        load(kp[2], k_planes[:, 2, :], HALVES)
+        q_scales = keep.tile([P, P], U8, name="q_scales", align_bytes=64)
+        quantise(q_codes[:], q_scales[:], q_grp[:].rearrange("p q t -> p (q t)"))
+
+        kp.extend(placed(f"k_plane{t}", AT_K[t]) for t in range(2, 4))
+        load(kp[2], k_planes[:, 2, :], WHOLE)
+        load(kp[3], k_planes[:, 3, :], HALVES)
 
         slope_col = banks.tile([P, P], F32, name="slope_col", tag="turn", bufs=4)
         nc.tensor.transpose(slope_col[:], slope_row[:], ident[:])
         slope_sb = keep.tile([P, 1], F32, name="slope_sb")
         nc.scalar.copy(slope_sb[:], slope_col[:, 0:1])
 
-        k_grp = [placed(f"k_grp{h}", AT_GRP + 4096 * h, (P, HALF, 4), BF16) for h in range(2)]
-        listed = [offsets[:, h * 32 : (h + 1) * 32] for h in range(2)]
+        k_grp = [keep.tile([P, HALF, 4], BF16, name=f"k_grp{h}", align_bytes=64) for h in range(2)]
 
-        def dealt(bank, g):
-            return bank[:].rearrange("q j n -> q (j n)").rearrange("q (b u j) -> q u b j", u=2, j=RUNS[g])
+        def gather_keys(t):
+            nc.vector.tensor_copy(k_grp[0][:, :, t], kp[t][:, : FIRST if t == 3 else T].indirect(listed(0, HALF)))
+            nc.scalar.activation(k_grp[1][:, :, t], kp[t][:].indirect(listed(HALF, N)), ACT.Copy)
 
-        def runs(row, g):
-            return row.rearrange("q (u b j) -> q u b j", u=2, j=RUNS[g])
-
-        def spread_out(gathered, first, col):
-            for g in range(2):
-                turned = banks.tile([P, 4, P], F32, name="turned", tag="turn", bufs=4)
-                for j in range(4):
-                    at = g * HALF + j * P
-                    nc.tensor.transpose(turned[:, j, :], gathered[:, at : at + P], ident[:])
-                nc.vector.tensor_reduce(col[:, g, :4], turned[:, :, first:P:64], AX.X, ALU.add)
-            spreads = {}
-            for g in (1, 0):
-                spread = banks.tile([P, 4, P], F32, name="spread", tag="head", bufs=2)
-                for j in range(4):
-                    nc.tensor.transpose(spread[:, j, :], col[:, g, j : j + 1].to_broadcast([P, P]), ident[:])
-                spreads[g] = spread
-            return spreads
-
-        pos_g = placed("pos_g", AT_PAIR, (P, N))
-        for h in range(2):
-            nc.vector.tensor_copy(pos_g[:, h * HALF : (h + 1) * HALF], pos_row[:].indirect(listed[h]))
-        kp.append(placed("k_plane3", AT_POS))
-        load(kp[3], k_planes[:, 3, :], LAST_LOADS)
-        pos_col = placed("pos_col", AT_GRP + 4096 - 32, (P, 2, 8), F32, 32)
-        pos_all = spread_out(pos_g, 0, pos_col)
-        k_pair = placed("k_pair", AT_PAIR, (P, 2 * N), BF16)
-        nc.scalar.activation(k_pair[:, :N], kp[0][:].indirect(offsets[:]), ACT.Copy)
-        bias = keep.tile([P, 2, HALF], F32, name="bias")
-        for g in (1, 0):
-            nc.scalar.activation(runs(bias[:, g], g), dealt(pos_all[g], g), ACT.Copy, scale=slope_sb[:])
-
-        nc.vector.tensor_copy(k_pair[:, N:], kp[1][:].indirect(offsets[:]))
-        for h in range(2):
-            c = slice(h * HALF, (h + 1) * HALF)
-            nc.scalar.copy(k_grp[h][:, :, 0:2], k_pair[:].rearrange("p (t n) -> p n t", t=2)[:, c, :])
-        vs_g = placed("vs_g", AT_K1 + 256, (P, N))
-        nc.vector.tensor_copy(vs_g[:], vs_row[:].indirect(offsets[:]))
-        vp = [placed("v_plane0", AT_VS - 256)]
+        gather_keys(0)
+        gather_keys(1)
+        vp = [placed(f"v_plane{e}", AT_V[e]) for e in range(2)]
         load(vp[0], vT[0:P, :], WHOLE)
-
-        for h in range(2):
-            nc.vector.tensor_copy(k_grp[h][:, :, 2], kp[2][:, : (FIRST, T)[h]].indirect(listed[h]))
-        vs_col = placed("vs_col", AT_K2, (P, 2, 4))
-        vs_all = spread_out(vs_g, 4, vs_col)
-        vp.append(placed("v_plane1", AT_V1))
         load(vp[1], vT[P : 2 * P, :], HALVES)
-        last_cast = keep.tile([P, FIRST], BF16, name="last_cast", align_bytes=64)
-        for c in LAST_CASTS[:-1]:
-            nc.scalar.activation(last_cast[:, c], kp[3][:, c], ACT.Copy)
-        nc.vector.tensor_copy(last_cast[:, LAST_CASTS[-1]], kp[3][:, LAST_CASTS[-1]])
-        nc.scalar.activation(k_grp[0][:, :, 3], last_cast[:].indirect(listed[0]), ACT.Copy)
-        nc.vector.tensor_copy(k_grp[1][:, :, 3], kp[3][:].indirect(listed[1]))
-        k_codes = placed("k_codes", AT_POS, (P, N), U32)
-        k_scales = keep.tile([P, N], U8, name="k_scales", align_bytes=64)
-        score = {}
-        for h in (1, 0):
+
+        pos_g = keep.tile([P, N], F32, name="pos_g")
+        vs_g = keep.tile([P, N], F32, name="vs_g")
+        for h in range(2):
             c = slice(h * HALF, (h + 1) * HALF)
-            nc.vector.quantize_mx(
-                out=k_codes[:, c].bitcast(FP8X4),
-                scales=k_scales[:, c],
-                in_=k_grp[h][:].rearrange("p n t -> p (n t)"),
-            )
+            nc.vector.tensor_copy(pos_g[:, c], pos_row[:].indirect(listed(c.start, c.stop)))
+            nc.scalar.activation(vs_g[:, c], vs_row[:].indirect(listed(c.start, c.stop)), ACT.Copy)
+        og_sb = placed("og_sb", AT_POS, (P, DV))
+        nc.sync.dma_start(og_sb[:], og[0])
+
+        def columns(gathered, first, col, step):
+            for h in range(2):
+                turned = banks.tile([P, 4, P], F32, name="turned", tag="turn", bufs=4)
+                half = gathered[:, h * HALF : (h + 1) * HALF]
+                for j in range(4):
+                    nc.tensor.transpose(turned[:, j, :], half[:, j::4] if step else half[:, j * P : (j + 1) * P], ident[:])
+                nc.vector.tensor_reduce(col[:, h, :4], turned[:, :, first:P:64], AX.X, ALU.add)
+
+        pos_col = keep.tile([P, 2, 8], F32, name="pos_col")
+        columns(pos_g, 0, pos_col, False)
+        spreads = []
+        for h in range(2):
+            spread = banks.tile([P, 4, P], F32, name="spread", tag="head", bufs=2)
+            for j in range(4):
+                nc.tensor.transpose(spread[:, j, :], pos_col[:, h, j : j + 1].to_broadcast([P, P]), ident[:])
+            spreads.append(spread)
+        gather_keys(2)
+        bias = placed("bias", AT_K[2], (P, 2, HALF))
+        for h in range(2):
+            nc.scalar.activation(bias[:, h], spreads[h][:].rearrange("q j n -> q (j n)"), ACT.Copy, scale=slope_sb[:])
+        vs_col = placed("vs_col", AT_K[2] + 4096, (P, 2, 8))
+        columns(vs_g, 4, vs_col, True)
+
+        gather_keys(3)
+        k_codes = keep.tile([P, N], U32, name="k_codes", align_bytes=64)
+        k_scales = keep.tile([P, N], U8, name="k_scales", align_bytes=64)
+        s_sb = keep.tile([P, 2, HALF], F32, name="s_sb")
+        score = []
+        for h in range(2):
+            c = slice(h * HALF, (h + 1) * HALF)
+            quantise(k_codes[:, c], k_scales[:, c], k_grp[h][:].rearrange("p n t -> p (n t)"))
             s_ps = banks.tile([P, HALF], F32, name=f"s_ps{h}")
             nc.tensor.matmul_mx(
                 out=s_ps[:],
@@ -181,118 +161,96 @@ def tile_attend_x_alibi_gate_srt_kernel(tc, qT, kT, vT, vs, pos, slope, og, offs
                 start=True,
                 stop=True,
             )
-            score[h] = s_ps
-
-        v_listed = keep.tile([P, HALF], BF16, name="v_listed", align_bytes=64)
-        nc.scalar.activation(v_listed[:], vp[0][:].indirect(listed[0]), ACT.Copy)
-        v_g = [[None, None], [None, None]]
-        v_g[0][0] = keep.tile([P, HALF], BF16, name="v_g00", align_bytes=64)
-        nc.scalar.copy(
-            v_g[0][0][:].bitcast(F32).rearrange("e (u b r) -> e u b r", u=2, r=8),
-            v_listed[:].bitcast(F32).rearrange("e (b u r) -> e u b r", u=2, r=8),
-        )
-
-        def gather_values(e, g, tag):
-            v_g[e][g] = keep.tile([P, HALF], BF16, name=f"v_g{e}{g}", tag=tag)
-            if g == 0:
-                places = v_g[e][g][:].rearrange("p (u b j) -> p b u j", u=2, j=16)
-                nc.vector.tensor_copy(places, vp[e][:, :FIRST].indirect(listed[g]))
-            elif e == 0:
-                nc.vector.tensor_copy(v_g[e][g][:], vp[e][:].indirect(listed[g]))
-            else:
-                cut = (HALF + V_SHARE) // 16
-                nc.scalar.activation(v_g[e][g][:, :V_SHARE], vp[e][:].indirect(offsets[:, HALF // 16 : cut]), ACT.Copy)
-                nc.vector.tensor_copy(v_g[e][g][:, V_SHARE:], vp[e][:].indirect(offsets[:, cut:]))
-
-        early = placed("early", AT_S + 2048, (P, 4 * HALF), BF16)
-        late = [placed(f"late{g}", AT_S + 6144 + 1024 * g, (P, HALF), BF16) for g in range(2)]
-        v_grp = [[early[:, g * HALF : (g + 1) * HALF] for g in range(2)], [late[g][:] for g in range(2)]]
-        w_grp = [early[:, (2 + g) * HALF : (3 + g) * HALF] for g in range(2)]
-
-        def turn(bank, rows, grouped, in_list_order=False):
-            words = rows.bitcast(F32)
-            for u in range(2):
-                pairs = words[:, u : 2 * P : 2] if in_list_order else words[:, u * P : (u + 1) * P]
-                nc.tensor.transpose(bank[:, u, :], pairs, ident[:])
-            nc.scalar.copy(grouped.bitcast(F32).rearrange("p (e u) -> p e u", u=2), bank[:].rearrange("p u e -> p e u"))
-
-        def turn_values(e, g):
-            if e == 0:
-                v_ps = banks.tile([P, 2, P], F32, name="v_ps", tag="turn", bufs=4)
-            else:
-                v_ps = banks.tile([P, 2, P], F32, name="v_ps", tag=f"s_ps{g}")
-            turn(v_ps, v_g[e][g][:], v_grp[e][g], g == 1)
-
-        def quantise(codes, scales, grouped):
-            nc.vector.quantize_mx(out=codes.bitcast(FP8X4), scales=scales, in_=grouped)
-
-        s_sb = placed("s_sb", AT_S, (P, 2, HALF))
-        for h in (1, 0):
-            nc.vector.tensor_tensor(
-                runs(s_sb[:, h], h),
-                score[h][:].rearrange("q (b u j) -> q u b j", u=2, j=RUNS[h]),
-                runs(bias[:, h], h),
-                ALU.add,
-            )
+            score.append(s_ps)
+        for h in range(2):
+            nc.vector.tensor_tensor(s_sb[:, h], score[h][:], bias[:, h], ALU.add)
         neg_max = keep.tile([P, 1], F32, name="neg_max")
-        nc.vector.tensor_reduce(
-            neg_max[:], s_sb[:].rearrange("q h n -> q (h n)"), AX.X, ALU.max, negate=True
-        )
-        prob_all = keep.tile([P, N], F32, name="prob", tag="v_listed", align_bytes=64)
-        prob = [prob_all[:, h * HALF : (h + 1) * HALF] for h in range(2)]
+        nc.vector.tensor_reduce(neg_max[:], s_sb[:].rearrange("q h n -> q (h n)"), AX.X, ALU.max, negate=True)
+        prob = [keep.tile([P, 4, P], F32, name=f"prob{h}") for h in range(2)]
         sums = keep.tile([P, 2], F32, name="sums")
-        for h in (1, 0):
+        for h in range(2):
             nc.scalar.activation(
-                prob[h], s_sb[:, h], ACT.Exp, bias=neg_max[:], accum_out=sums[:, h : h + 1]
+                prob[h][:].rearrange("q t p -> q p t"),
+                s_sb[:, h].rearrange("q (p t) -> q p t", t=4),
+                ACT.Exp,
+                bias=neg_max[:],
+                accum_out=sums[:, h : h + 1],
             )
-        gather_values(0, 1, "bias")
 
+        v_g = [[keep.tile([P, HALF], BF16, name=f"v_g{e}{h}", align_bytes=64) for h in range(2)] for e in range(2)]
+
+        def gather_values(e, scalar_share):
+            dealt = v_g[e][0][:].rearrange("f (u p j) -> f p u j", u=2, j=2)
+            nc.vector.tensor_copy(dealt, vp[e][:, : FIRST if e == 1 else T].indirect(listed(0, HALF)))
+            cut = N - scalar_share
+            nc.vector.tensor_copy(v_g[e][1][:, : cut - HALF], vp[e][:].indirect(listed(HALF, cut)))
+            nc.scalar.activation(v_g[e][1][:, cut - HALF :], vp[e][:].indirect(listed(cut, N)), ACT.Copy)
+
+        early = keep.tile([P, 4, HALF], BF16, name="early", align_bytes=64)
+        late = [keep.tile([P, HALF], BF16, name=f"late{h}", align_bytes=64) for h in range(2)]
+        v_grp = [[early[:, h] for h in range(2)], [late[h][:] for h in range(2)]]
+        w_grp = [early[:, 2 + h] for h in range(2)]
+
+        def turn_values(e, h):
+            if e == 0:
+                bank = banks.tile([P, 2, P], F32, name="v_ps", tag="turn", bufs=4)
+            else:
+                bank = banks.tile([P, 2, P], F32, name="v_ps", tag=f"s_ps{h}")
+            words = v_g[e][h][:].bitcast(F32)
+            for u in range(2):
+                pairs = words[:, u : 2 * P : 2] if h == 1 else words[:, u * P : (u + 1) * P]
+                nc.tensor.transpose(bank[:, u, :], pairs, ident[:])
+            nc.scalar.copy(v_grp[e][h].bitcast(F32).rearrange("p (f u) -> p f u", u=2), bank[:].rearrange("p u f -> p f u"))
+
+        gather_values(0, V0_SCALAR)
+        for h in range(2):
+            p_ps = banks.tile([P, 4, P], F32, name="p_ps", tag="turn", bufs=4)
+            for t in range(4):
+                nc.tensor.transpose(p_ps[:, t, :], prob[h][:, t, :], ident[:])
+            nc.vector.tensor_tensor(
+                w_grp[h].rearrange("p (q t) -> p q t", t=4),
+                p_ps[:].rearrange("p t q -> p q t"),
+                vs_col[:, h, :4].unsqueeze(1).to_broadcast([P, P, 4]),
+                ALU.mult,
+            )
         total = keep.tile([P, 1], F32, name="total")
         nc.scalar.activation(total[:], sums[:, 0:1], ACT.Identity, bias=sums[:, 1:2])
-        w_row = [keep.tile([P, HALF], BF16, name=f"w_row{g}") for g in range(2)]
-        early_codes = placed("early_codes", AT_V1, (P, 4 * P), U32)
-        early_scales = keep.tile([P, 4 * P], U8, name="early_scales", align_bytes=64)
-        late_codes = placed("late_codes", AT_V1 + 2048, (P, 2 * P), U32)
-        late_scales = keep.tile([P, 2 * P], U8, name="late_scales", align_bytes=64)
-        blocks = [slice(j * P, (j + 1) * P) for j in range(4)]
-        w_codes = [early_codes[:, blocks[2 + g]] for g in range(2)]
-        w_scales = [early_scales[:, blocks[2 + g]] for g in range(2)]
-        v_codes = [[codes[:, blocks[g]] for g in range(2)] for codes in (early_codes, late_codes)]
-        v_scales = [[scales[:, blocks[g]] for g in range(2)] for scales in (early_scales, late_scales)]
-        for g in (1, 0):
-            nc.vector.tensor_tensor(runs(w_row[g][:], g), runs(prob[g], g), dealt(vs_all[g], g), ALU.mult)
         turn_values(0, 0)
         turn_values(0, 1)
-        for g in (1, 0):
-            w_ps = banks.tile([P, 2, P], F32, name="w_ps", tag="turn", bufs=4)
-            turn(w_ps, w_row[g][:], w_grp[g])
-        og_sb = placed("og_sb", AT_POS + 8192, (P, DV))
-        nc.sync.dma_start(og_sb[:], og[0])
+        gather_values(1, V1_SCALAR)
+        turn_values(1, 0)
         half_tanh = keep.tile([P, DV], F32, name="half_tanh")
         nc.scalar.activation(half_tanh[:], og_sb[:], ACT.Tanh, scale=0.5)
-        gather_values(1, 0, "v_g10")
-        gather_values(1, 1, "v_g11")
-        turn_values(1, 0)
         turn_values(1, 1)
-        gate = keep.tile([P, DV], F32, name="gate", tag="v_g11")
+        gate = keep.tile([P, DV], F32, name="gate", tag="v_g11", align_bytes=64)
         nc.scalar.activation(gate[:], half_tanh[:], ACT.Identity, scale=0.5, bias=0.5)
-        quantise(early_codes[:], early_scales[:], early[:])
+
+        early_codes = placed("early_codes", AT_V[1], (P, 4 * P), U32)
+        early_scales = keep.tile([P, 4 * P], U8, name="early_scales", align_bytes=64)
+        late_codes = placed("late_codes", AT_V[1] + 2048, (P, 2 * P), U32)
+        late_scales = keep.tile([P, 2 * P], U8, name="late_scales", align_bytes=64)
+        blocks = [slice(j * P, (j + 1) * P) for j in range(4)]
+        w_codes = [early_codes[:, blocks[2 + h]] for h in range(2)]
+        w_scales = [early_scales[:, blocks[2 + h]] for h in range(2)]
+        v_codes = [[codes[:, blocks[h]] for h in range(2)] for codes in (early_codes, late_codes)]
+        v_scales = [[scales[:, blocks[h]] for h in range(2)] for scales in (early_scales, late_scales)]
+        quantise(early_codes[:], early_scales[:], early[:].rearrange("p b n -> p (b n)"))
         quantise(v_codes[1][0], v_scales[1][0], v_grp[1][0])
-        inv = placed("inv", AT_V1 + 4096, (P, 1))
+        inv = placed("inv", AT_V[1] + 4096, (P, 1))
         nc.vector.reciprocal(inv[:], total[:])
         quantise(v_codes[1][1], v_scales[1][1], v_grp[1][1])
 
         for e in range(2):
             y_ps = banks.tile([P, P], F32, name="y_ps", tag="head", bufs=2)
-            for g in range(2):
+            for h in range(2):
                 nc.tensor.matmul_mx(
                     out=y_ps[:],
-                    lhsT=w_codes[g].bitcast(FP8X4),
-                    lhsT_scale=w_scales[g],
-                    rhs=v_codes[e][g].bitcast(FP8X4),
-                    rhs_scale=v_scales[e][g],
-                    start=(g == 0),
-                    stop=(g == 1),
+                    lhsT=w_codes[h].bitcast(FP8X4),
+                    lhsT_scale=w_scales[h],
+                    rhs=v_codes[e][h].bitcast(FP8X4),
+                    rhs_scale=v_scales[e][h],
+                    start=(h == 0),
+                    stop=(h == 1),
                 )
             c = slice(e * P, (e + 1) * P)
             y_sb = keep.tile([P, P], F32, name=f"y_sb{e}", align_bytes=256)

@@ -19,6 +19,7 @@ DV = 256
 T = 4096
 N = 1024
 HALF = 512
+QUARTER = 256
 FIRST = T - HALF
 V0_SCALAR = 256
 V1_SCALAR = 288
@@ -149,33 +150,36 @@ def tile_attend_x_alibi_gate_srt_kernel(tc, qT, kT, vT, vs, pos, slope, og, offs
         s_sb = keep.tile([P, 2, HALF], F32, name="s_sb")
         score = []
         for h in range(2):
-            c = slice(h * HALF, (h + 1) * HALF)
-            quantise(k_codes[:, c], k_scales[:, c], k_grp[h][:].rearrange("p n t -> p (n t)"))
             s_ps = banks.tile([P, HALF], F32, name=f"s_ps{h}")
-            nc.tensor.matmul_mx(
-                out=s_ps[:],
-                lhsT=q_codes[:].bitcast(FP8X4),
-                lhsT_scale=q_scales[:],
-                rhs=k_codes[:, c].bitcast(FP8X4),
-                rhs_scale=k_scales[:, c],
-                start=True,
-                stop=True,
-            )
+            for part in range(2):
+                within = slice(part * QUARTER, (part + 1) * QUARTER)
+                c = slice(h * HALF + within.start, h * HALF + within.stop)
+                quantise(k_codes[:, c], k_scales[:, c], k_grp[h][:, within, :].rearrange("p n t -> p (n t)"))
+                nc.tensor.matmul_mx(
+                    out=s_ps[:, within],
+                    lhsT=q_codes[:].bitcast(FP8X4),
+                    lhsT_scale=q_scales[:],
+                    rhs=k_codes[:, c].bitcast(FP8X4),
+                    rhs_scale=k_scales[:, c],
+                    start=True,
+                    stop=True,
+                )
             score.append(s_ps)
         for h in range(2):
             nc.vector.tensor_tensor(s_sb[:, h], score[h][:], bias[:, h], ALU.add)
         neg_max = keep.tile([P, 1], F32, name="neg_max")
         nc.vector.tensor_reduce(neg_max[:], s_sb[:].rearrange("q h n -> q (h n)"), AX.X, ALU.max, negate=True)
-        prob = [keep.tile([P, 4, P], F32, name=f"prob{h}") for h in range(2)]
-        sums = keep.tile([P, 2], F32, name="sums")
+        prob = [[keep.tile([P, 2, P], F32, name=f"prob{h}{u}") for u in range(2)] for h in range(2)]
+        sums = keep.tile([P, 4], F32, name="sums")
         for h in range(2):
-            nc.scalar.activation(
-                prob[h][:].rearrange("q t p -> q p t"),
-                s_sb[:, h].rearrange("q (p t) -> q p t", t=4),
-                ACT.Exp,
-                bias=neg_max[:],
-                accum_out=sums[:, h : h + 1],
-            )
+            for u in range(2):
+                nc.scalar.activation(
+                    prob[h][u][:].rearrange("q j p -> q p j"),
+                    s_sb[:, h].rearrange("q (p t) -> q p t", t=4)[:, :, 2 * u : 2 * u + 2],
+                    ACT.Exp,
+                    bias=neg_max[:],
+                    accum_out=sums[:, 2 * h + u : 2 * h + u + 1],
+                )
 
         v_g = [[keep.tile([P, HALF], BF16, name=f"v_g{e}{h}", align_bytes=64) for h in range(2)] for e in range(2)]
 
@@ -206,7 +210,7 @@ def tile_attend_x_alibi_gate_srt_kernel(tc, qT, kT, vT, vs, pos, slope, og, offs
         for h in range(2):
             p_ps = banks.tile([P, 4, P], F32, name="p_ps", tag="turn", bufs=4)
             for t in range(4):
-                nc.tensor.transpose(p_ps[:, t, :], prob[h][:, t, :], ident[:])
+                nc.tensor.transpose(p_ps[:, t, :], prob[h][t // 2][:, t % 2, :], ident[:])
             nc.vector.tensor_tensor(
                 w_grp[h].rearrange("p (q t) -> p q t", t=4),
                 p_ps[:].rearrange("p t q -> p q t"),
@@ -214,7 +218,7 @@ def tile_attend_x_alibi_gate_srt_kernel(tc, qT, kT, vT, vs, pos, slope, og, offs
                 ALU.mult,
             )
         total = keep.tile([P, 1], F32, name="total")
-        nc.scalar.activation(total[:], sums[:, 0:1], ACT.Identity, bias=sums[:, 1:2])
+        nc.vector.tensor_reduce(total[:], sums[:], AX.X, ALU.add)
         turn_values(0, 0)
         turn_values(0, 1)
         gather_values(1, V1_SCALAR)

@@ -21,6 +21,10 @@ N = 1024
 HALF = 512
 QUARTER = 256
 FIRST = T - HALF
+K_EARLY = 640
+K_VECTOR = 448
+K_FIRST = T - N + K_VECTOR
+K_SCALAR_CUTS = (K_VECTOR, 576, 768, N)
 V0_SCALAR = 256
 V1_SCALAR = 288
 WHOLE = [slice(0, T)]
@@ -50,6 +54,12 @@ def tile_attend_x_alibi_gate_srt_kernel(tc, qT, kT, vT, vs, pos, slope, og, offs
 
         def listed(lo, hi):
             return offsets[:, lo // 16 : hi // 16]
+
+        def in_runs(row):
+            return row.rearrange("q (b a j) -> q b a j", b=2, a=2)
+
+        def crossed(row):
+            return row.rearrange("q (a b j) -> q b a j", a=2, b=2)
 
         def load(tile, src, cuts):
             for c in cuts:
@@ -93,18 +103,21 @@ def tile_attend_x_alibi_gate_srt_kernel(tc, qT, kT, vT, vs, pos, slope, og, offs
 
         kp.extend(placed(f"k_plane{t}", AT_K[t]) for t in range(2, 4))
         load(kp[2], k_planes[:, 2, :], WHOLE)
-        load(kp[3], k_planes[:, 3, :], HALVES)
+        load(kp[3], k_planes[:, 3, :], [slice(0, K_FIRST), slice(K_FIRST, T)])
 
         slope_col = banks.tile([P, P], F32, name="slope_col", tag="turn", bufs=4)
         nc.tensor.transpose(slope_col[:], slope_row[:], ident[:])
         slope_sb = keep.tile([P, 1], F32, name="slope_sb")
         nc.scalar.copy(slope_sb[:], slope_col[:, 0:1])
 
-        k_grp = [keep.tile([P, HALF, 4], BF16, name=f"k_grp{h}", align_bytes=64) for h in range(2)]
+        k_grp = keep.tile([P, N, 4], BF16, name="k_grp", align_bytes=64)
 
         def gather_keys(t):
-            nc.vector.tensor_copy(k_grp[0][:, :, t], kp[t][:, : FIRST if t == 3 else T].indirect(listed(0, HALF)))
-            nc.scalar.activation(k_grp[1][:, :, t], kp[t][:].indirect(listed(HALF, N)), ACT.Copy)
+            cuts = (K_EARLY, N) if t < 2 else (K_VECTOR, N) if t == 2 else K_SCALAR_CUTS
+            window = kp[t][:, : T - N + cuts[0]]
+            nc.vector.tensor_copy(k_grp[:, : cuts[0], t], window.indirect(listed(0, cuts[0])))
+            for lo, hi in zip(cuts, cuts[1:]):
+                nc.scalar.activation(k_grp[:, lo:hi, t], kp[t][:].indirect(listed(lo, hi)), ACT.Copy)
 
         gather_keys(0)
         gather_keys(1)
@@ -117,7 +130,10 @@ def tile_attend_x_alibi_gate_srt_kernel(tc, qT, kT, vT, vs, pos, slope, og, offs
         for h in range(2):
             c = slice(h * HALF, (h + 1) * HALF)
             nc.vector.tensor_copy(pos_g[:, c], pos_row[:].indirect(listed(c.start, c.stop)))
-            nc.scalar.activation(vs_g[:, c], vs_row[:].indirect(listed(c.start, c.stop)), ACT.Copy)
+        for run in range(4):
+            at = P * (2 * (run % 2) + run // 2)
+            nc.scalar.activation(vs_g[:, at : at + P], vs_row[:].indirect(listed(run * P, (run + 1) * P)), ACT.Copy)
+        nc.scalar.activation(vs_g[:, HALF:], vs_row[:].indirect(listed(HALF, N)), ACT.Copy)
         og_sb = placed("og_sb", AT_POS, (P, DV))
         nc.sync.dma_start(og_sb[:], og[0])
 
@@ -154,7 +170,7 @@ def tile_attend_x_alibi_gate_srt_kernel(tc, qT, kT, vT, vs, pos, slope, og, offs
             for part in range(2):
                 within = slice(part * QUARTER, (part + 1) * QUARTER)
                 c = slice(h * HALF + within.start, h * HALF + within.stop)
-                quantise(k_codes[:, c], k_scales[:, c], k_grp[h][:, within, :].rearrange("p n t -> p (n t)"))
+                quantise(k_codes[:, c], k_scales[:, c], k_grp[:, c, :].rearrange("p n t -> p (n t)"))
                 nc.tensor.matmul_mx(
                     out=s_ps[:, within],
                     lhsT=q_codes[:].bitcast(FP8X4),
@@ -165,8 +181,8 @@ def tile_attend_x_alibi_gate_srt_kernel(tc, qT, kT, vT, vs, pos, slope, og, offs
                     stop=True,
                 )
             score.append(s_ps)
-        for h in range(2):
-            nc.vector.tensor_tensor(s_sb[:, h], score[h][:], bias[:, h], ALU.add)
+        nc.vector.tensor_tensor(crossed(s_sb[:, 0]), in_runs(score[0][:]), in_runs(bias[:, 0]), ALU.add)
+        nc.vector.tensor_tensor(s_sb[:, 1], score[1][:], bias[:, 1], ALU.add)
         neg_max = keep.tile([P, 1], F32, name="neg_max")
         nc.vector.tensor_reduce(neg_max[:], s_sb[:].rearrange("q h n -> q (h n)"), AX.X, ALU.max, negate=True)
         prob = [[keep.tile([P, 2, P], F32, name=f"prob{h}{u}") for u in range(2)] for h in range(2)]
@@ -184,8 +200,7 @@ def tile_attend_x_alibi_gate_srt_kernel(tc, qT, kT, vT, vs, pos, slope, og, offs
         v_g = [[keep.tile([P, HALF], BF16, name=f"v_g{e}{h}", align_bytes=64) for h in range(2)] for e in range(2)]
 
         def gather_values(e, scalar_share):
-            dealt = v_g[e][0][:].rearrange("f (u p j) -> f p u j", u=2, j=2)
-            nc.vector.tensor_copy(dealt, vp[e][:, : FIRST if e == 1 else T].indirect(listed(0, HALF)))
+            nc.vector.tensor_copy(crossed(v_g[e][0][:]), vp[e][:, : FIRST if e == 1 else T].indirect(listed(0, HALF)))
             cut = N - scalar_share
             nc.vector.tensor_copy(v_g[e][1][:, : cut - HALF], vp[e][:].indirect(listed(HALF, cut)))
             nc.scalar.activation(v_g[e][1][:, cut - HALF :], vp[e][:].indirect(listed(cut, N)), ACT.Copy)
@@ -202,8 +217,7 @@ def tile_attend_x_alibi_gate_srt_kernel(tc, qT, kT, vT, vs, pos, slope, og, offs
                 bank = banks.tile([P, 2, P], F32, name="v_ps", tag=f"s_ps{h}")
             words = v_g[e][h][:].bitcast(F32)
             for u in range(2):
-                pairs = words[:, u : 2 * P : 2] if h == 1 else words[:, u * P : (u + 1) * P]
-                nc.tensor.transpose(bank[:, u, :], pairs, ident[:])
+                nc.tensor.transpose(bank[:, u, :], words[:, u : 2 * P : 2], ident[:])
             nc.scalar.copy(v_grp[e][h].bitcast(F32).rearrange("p (f u) -> p f u", u=2), bank[:].rearrange("p u f -> p f u"))
 
         gather_values(0, V0_SCALAR)

@@ -19,12 +19,12 @@ DV = 256
 T = 4096
 N = 1024
 HALF = 512
-QUARTER = 256
 FIRST = T - HALF
 K_EARLY = 640
 K_VECTOR = 448
 K_FIRST = T - N + K_VECTOR
-K_SCALAR_CUTS = (K_VECTOR, 576, 768, N)
+K_SCALAR_CUTS = (K_VECTOR, 576, 768, 896, N)
+SCORE_CUTS = ((0, 256, 512), (512, 768, 896, N))
 V0_SCALAR = 256
 V1_SCALAR = 288
 WHOLE = [slice(0, T)]
@@ -167,9 +167,9 @@ def tile_attend_x_alibi_gate_srt_kernel(tc, qT, kT, vT, vs, pos, slope, og, offs
         score = []
         for h in range(2):
             s_ps = banks.tile([P, HALF], F32, name=f"s_ps{h}")
-            for part in range(2):
-                within = slice(part * QUARTER, (part + 1) * QUARTER)
-                c = slice(h * HALF + within.start, h * HALF + within.stop)
+            for lo, hi in zip(SCORE_CUTS[h], SCORE_CUTS[h][1:]):
+                c = slice(lo, hi)
+                within = slice(lo - h * HALF, hi - h * HALF)
                 quantise(k_codes[:, c], k_scales[:, c], k_grp[:, c, :].rearrange("p n t -> p (n t)"))
                 nc.tensor.matmul_mx(
                     out=s_ps[:, within],
@@ -231,8 +231,6 @@ def tile_attend_x_alibi_gate_srt_kernel(tc, qT, kT, vT, vs, pos, slope, og, offs
                 vs_col[:, h, :4].unsqueeze(1).to_broadcast([P, P, 4]),
                 ALU.mult,
             )
-        total = keep.tile([P, 1], F32, name="total")
-        nc.vector.tensor_reduce(total[:], sums[:], AX.X, ALU.add)
         turn_values(0, 0)
         turn_values(0, 1)
         gather_values(1, V1_SCALAR)
@@ -253,6 +251,8 @@ def tile_attend_x_alibi_gate_srt_kernel(tc, qT, kT, vT, vs, pos, slope, og, offs
         v_codes = [[codes[:, blocks[h]] for h in range(2)] for codes in (early_codes, late_codes)]
         v_scales = [[scales[:, blocks[h]] for h in range(2)] for scales in (early_scales, late_scales)]
         quantise(early_codes[:], early_scales[:], early[:].rearrange("p b n -> p (b n)"))
+        total = placed("total", AT_V[1] + 4352, (P, 1))
+        nc.vector.tensor_reduce(total[:], sums[:], AX.X, ALU.add)
         quantise(v_codes[1][0], v_scales[1][0], v_grp[1][0])
         inv = placed("inv", AT_V[1] + 4096, (P, 1))
         nc.vector.reciprocal(inv[:], total[:])

from contextlib import ExitStack

import concourse.mybir as mybir
from concourse.masks import make_identity

F32 = mybir.dt.float32
BF16 = mybir.dt.bfloat16
U32 = mybir.dt.uint32
U16 = mybir.dt.uint16
U8 = mybir.dt.uint8
FP8X4 = mybir.dt.float8_e4m3fn_x4
ACT = mybir.ActivationFunctionType
ALU = mybir.AluOpType
AX = mybir.AxisListType

P = 128
D = 512
DV = 256
T = 4096
N = 1024
HALF = 512
FIRST = T - HALF
K_EARLY = 640
K_VECTOR = 448
K_FIRST = T - N + K_VECTOR
K_SCALAR_CUTS = (K_VECTOR, 576, 768, 896, N)
SCORE_CUTS = ((0, 256, 512), (512, 768, 896, N))
V0_SCALAR = 256
V1_SCALAR = 288
WHOLE = [slice(0, T)]
HALVES = [slice(0, FIRST), slice(FIRST, T)]
PLANE = 4 * T
AT_POS = 0
AT_VS = PLANE
AT_K = [(2 + t) * PLANE for t in range(4)]
AT_V = AT_K[:2]
FLOPS = 2 * N * D * P + 2 * N * P * DV
BYTES = 4 * (D * P + D * T + DV * T + 2 * T + P + 2 * P * DV) + 2 * P * (N // 16)


def tile_attend_x_alibi_gate_srt_kernel(tc, qT, kT, vT, vs, pos, slope, og, offs, out):
    nc = tc.nc
    with ExitStack() as ctx:
        keep = ctx.enter_context(tc.tile_pool(name="keep", bufs=1))
        banks = ctx.enter_context(tc.psum_pool(name="banks", bufs=1))

        offsets = keep.tile([P, N // 16], U16, name="offsets", align_bytes=256)
        nc.sync.dma_start(offsets[:], offs)

        planes = ctx.enter_context(tc.tile_pool(name="planes", bufs=1))

        def placed(name, at, shape=(P, T), dtype=F32, align=256):
            return planes.tile(list(shape), dtype, name=name, align_bytes=align, offset=at)

        def listed(lo, hi):
            return offsets[:, lo // 16 : hi // 16]

        def in_runs(row):
            return row.rearrange("q (b a j) -> q b a j", b=2, a=2)

        def crossed(row):
            return row.rearrange("q (a b j) -> q b a j", a=2, b=2)

        def load(tile, src, cuts):
            for c in cuts:
                nc.sync.dma_start(tile[:, c], src[:, c])

        def load_row(row, src, first):
            for u in range(2):
                c = slice(u * T // 2, (u + 1) * T // 2)
                at = first + 64 * u
                nc.sync.dma_start(row[at : at + 1, c], src[0:1, c])

        def quantise(codes, scales, grouped):
            nc.vector.quantize_mx(out=codes.bitcast(FP8X4), scales=scales, in_=grouped)

        pos_row = placed("pos_row", AT_POS)
        vs_row = placed("vs_row", AT_VS)
        ident_made = placed("ident_made", AT_K[2], (P, P), BF16)
        make_identity(nc, ident_made[:])
        slope_row = keep.tile([P, P], F32, name="slope_row", align_bytes=256)
        nc.vector.memset(slope_row[:], 0.0)
        nc.vector.memset(pos_row[:], 0.0)
        nc.vector.memset(vs_row[:], 0.0)
        ident = keep.tile([P, P], F32, name="ident", align_bytes=64)
        nc.vector.tensor_copy(ident[:], ident_made[:])

        k_planes = kT.rearrange("(p t) n -> p t n", t=4)
        q_raw = keep.tile([P, 4, P], F32, name="q_raw", align_bytes=256)
        nc.sync.dma_start(q_raw[:], qT[0].rearrange("(p t) q -> p t q", t=4))
        kp = [placed(f"k_plane{t}", AT_K[t]) for t in range(2)]
        for t in range(2):
            load(kp[t], k_planes[:, t, :], WHOLE)
        nc.sync.dma_start(slope_row[0:1, :], slope[0].rearrange("q o -> o q"))
        load_row(pos_row, pos, 0)
        load_row(vs_row, vs, 4)

        q_grp = placed("q_grp", AT_K[3], (P, P, 4), BF16)
        nc.scalar.copy(q_grp[:], q_raw[:].rearrange("p t q -> p q t"))
        q_codes = keep.tile([P, P], U32, name="q_codes", align_bytes=64)
        q_scales = keep.tile([P, P], U8, name="q_scales", align_bytes=64)
        quantise(q_codes[:], q_scales[:], q_grp[:].rearrange("p q t -> p (q t)"))

        kp.extend(placed(f"k_plane{t}", AT_K[t]) for t in range(2, 4))
        load(kp[2], k_planes[:, 2, :], WHOLE)
        load(kp[3], k_planes[:, 3, :], [slice(0, K_FIRST), slice(K_FIRST, T)])

        slope_col = banks.tile([P, P], F32, name="slope_col", tag="turn", bufs=4)
        nc.tensor.transpose(slope_col[:], slope_row[:], ident[:])
        slope_sb = keep.tile([P, 1], F32, name="slope_sb")
        nc.scalar.copy(slope_sb[:], slope_col[:, 0:1])

        k_grp = keep.tile([P, N, 4], BF16, name="k_grp", align_bytes=64)

        def gather_keys(t):
            cuts = (K_EARLY, N) if t < 2 else (K_VECTOR, N) if t == 2 else K_SCALAR_CUTS
            window = kp[t][:, : T - N + cuts[0]]
            nc.vector.tensor_copy(k_grp[:, : cuts[0], t], window.indirect(listed(0, cuts[0])))
            for lo, hi in zip(cuts, cuts[1:]):
                nc.scalar.activation(k_grp[:, lo:hi, t], kp[t][:].indirect(listed(lo, hi)), ACT.Copy)

        gather_keys(0)
        gather_keys(1)
        vp = [placed(f"v_plane{e}", AT_V[e]) for e in range(2)]
        load(vp[0], vT[0:P, :], WHOLE)
        load(vp[1], vT[P : 2 * P, :], HALVES)

        pos_g = keep.tile([P, N], F32, name="pos_g")
        vs_g = keep.tile([P, N], F32, name="vs_g")
        for h in range(2):
            c = slice(h * HALF, (h + 1) * HALF)
            nc.vector.tensor_copy(pos_g[:, c], pos_row[:].indirect(listed(c.start, c.stop)))
        for run in range(4):
            at = P * (2 * (run % 2) + run // 2)
            nc.scalar.activation(vs_g[:, at : at + P], vs_row[:].indirect(listed(run * P, (run + 1) * P)), ACT.Copy)
        nc.scalar.activation(vs_g[:, HALF:], vs_row[:].indirect(listed(HALF, N)), ACT.Copy)
        og_sb = placed("og_sb", AT_POS, (P, DV))
        nc.sync.dma_start(og_sb[:], og[0])

        def columns(gathered, first, col, step):
            for h in range(2):
                turned = banks.tile([P, 4, P], F32, name="turned", tag="turn", bufs=4)
                half = gathered[:, h * HALF : (h + 1) * HALF]
                for j in range(4):
                    nc.tensor.transpose(turned[:, j, :], half[:, j::4] if step else half[:, j * P : (j + 1) * P], ident[:])
                nc.vector.tensor_reduce(col[:, h, :4], turned[:, :, first:P:64], AX.X, ALU.add)

        pos_col = keep.tile([P, 2, 8], F32, name="pos_col")
        columns(pos_g, 0, pos_col, False)
        spreads = []
        for h in range(2):
            spread = banks.tile([P, 4, P], F32, name="spread", tag="head", bufs=2)
            for j in range(4):
                nc.tensor.transpose(spread[:, j, :], pos_col[:, h, j : j + 1].to_broadcast([P, P]), ident[:])
            spreads.append(spread)
        gather_keys(2)
        bias = placed("bias", AT_K[2], (P, 2, HALF))
        for h in range(2):
            nc.scalar.activation(bias[:, h], spreads[h][:].rearrange("q j n -> q (j n)"), ACT.Copy, scale=slope_sb[:])
        vs_col = placed("vs_col", AT_K[2] + 4096, (P, 2, 8))
        columns(vs_g, 4, vs_col, True)

        gather_keys(3)
        k_codes = keep.tile([P, N], U32, name="k_codes", align_bytes=64)
        k_scales = keep.tile([P, N], U8, name="k_scales", align_bytes=64)
        s_sb = keep.tile([P, 2, HALF], F32, name="s_sb")
        score = []
        for h in range(2):
            s_ps = banks.tile([P, HALF], F32, name=f"s_ps{h}")
            for lo, hi in zip(SCORE_CUTS[h], SCORE_CUTS[h][1:]):
                c = slice(lo, hi)
                within = slice(lo - h * HALF, hi - h * HALF)
                quantise(k_codes[:, c], k_scales[:, c], k_grp[:, c, :].rearrange("p n t -> p (n t)"))
                nc.tensor.matmul_mx(
                    out=s_ps[:, within],
                    lhsT=q_codes[:].bitcast(FP8X4),
                    lhsT_scale=q_scales[:],
                    rhs=k_codes[:, c].bitcast(FP8X4),
                    rhs_scale=k_scales[:, c],
                    start=True,
                    stop=True,
                )
            score.append(s_ps)
        nc.vector.tensor_tensor(crossed(s_sb[:, 0]), in_runs(score[0][:]), in_runs(bias[:, 0]), ALU.add)
        nc.vector.tensor_tensor(s_sb[:, 1], score[1][:], bias[:, 1], ALU.add)
        neg_max = keep.tile([P, 1], F32, name="neg_max")
        nc.vector.tensor_reduce(neg_max[:], s_sb[:].rearrange("q h n -> q (h n)"), AX.X, ALU.max, negate=True)
        prob = [[keep.tile([P, 2, P], F32, name=f"prob{h}{u}") for u in range(2)] for h in range(2)]
        sums = keep.tile([P, 4], F32, name="sums")
        for h in range(2):
            for u in range(2):
                nc.scalar.activation(
                    prob[h][u][:].rearrange("q j p -> q p j"),
                    s_sb[:, h].rearrange("q (p t) -> q p t", t=4)[:, :, 2 * u : 2 * u + 2],
                    ACT.Exp,
                    bias=neg_max[:],
                    accum_out=sums[:, 2 * h + u : 2 * h + u + 1],
                )

        v_g = [[keep.tile([P, HALF], BF16, name=f"v_g{e}{h}", align_bytes=64) for h in range(2)] for e in range(2)]

        def gather_values(e, scalar_share):
            nc.vector.tensor_copy(crossed(v_g[e][0][:]), vp[e][:, : FIRST if e == 1 else T].indirect(listed(0, HALF)))
            cut = N - scalar_share
            nc.vector.tensor_copy(v_g[e][1][:, : cut - HALF], vp[e][:].indirect(listed(HALF, cut)))
            nc.scalar.activation(v_g[e][1][:, cut - HALF :], vp[e][:].indirect(listed(cut, N)), ACT.Copy)

        early = keep.tile([P, 4, HALF], BF16, name="early", align_bytes=64)
        late = [keep.tile([P, HALF], BF16, name=f"late{h}", align_bytes=64) for h in range(2)]
        v_grp = [[early[:, h] for h in range(2)], [late[h][:] for h in range(2)]]
        w_grp = [early[:, 2 + h] for h in range(2)]

        def turn_values(e, h):
            if e == 0:
                bank = banks.tile([P, 2, P], F32, name="v_ps", tag="turn", bufs=4)
            else:
                bank = banks.tile([P, 2, P], F32, name="v_ps", tag=f"s_ps{h}")
            words = v_g[e][h][:].bitcast(F32)
            for u in range(2):
                nc.tensor.transpose(bank[:, u, :], words[:, u : 2 * P : 2], ident[:])
            nc.scalar.copy(v_grp[e][h].bitcast(F32).rearrange("p (f u) -> p f u", u=2), bank[:].rearrange("p u f -> p f u"))

        gather_values(0, V0_SCALAR)
        for h in range(2):
            p_ps = banks.tile([P, 4, P], F32, name="p_ps", tag="turn", bufs=4)
            for t in range(4):
                nc.tensor.transpose(p_ps[:, t, :], prob[h][t // 2][:, t % 2, :], ident[:])
            nc.vector.tensor_tensor(
                w_grp[h].rearrange("p (q t) -> p q t", t=4),
                p_ps[:].rearrange("p t q -> p q t"),
                vs_col[:, h, :4].unsqueeze(1).to_broadcast([P, P, 4]),
                ALU.mult,
            )
        turn_values(0, 0)
        turn_values(0, 1)
        gather_values(1, V1_SCALAR)
        turn_values(1, 0)
        half_tanh = keep.tile([P, DV], F32, name="half_tanh")
        nc.scalar.activation(half_tanh[:], og_sb[:], ACT.Tanh, scale=0.5)
        turn_values(1, 1)
        gate = keep.tile([P, DV], F32, name="gate", tag="v_g11", align_bytes=64)
        nc.scalar.activation(gate[:], half_tanh[:], ACT.Identity, scale=0.5, bias=0.5)

        early_codes = placed("early_codes", AT_V[1], (P, 4 * P), U32)
        early_scales = keep.tile([P, 4 * P], U8, name="early_scales", align_bytes=64)
        late_codes = placed("late_codes", AT_V[1] + 2048, (P, 2 * P), U32)
        late_scales = keep.tile([P, 2 * P], U8, name="late_scales", align_bytes=64)
        blocks = [slice(j * P, (j + 1) * P) for j in range(4)]
        w_codes = [early_codes[:, blocks[2 + h]] for h in range(2)]
        w_scales = [early_scales[:, blocks[2 + h]] for h in range(2)]
        v_codes = [[codes[:, blocks[h]] for h in range(2)] for codes in (early_codes, late_codes)]
        v_scales = [[scales[:, blocks[h]] for h in range(2)] for scales in (early_scales, late_scales)]
        quantise(early_codes[:], early_scales[:], early[:].rearrange("p b n -> p (b n)"))
        total = placed("total", AT_V[1] + 4352, (P, 1))
        nc.vector.tensor_reduce(total[:], sums[:], AX.X, ALU.add)
        quantise(v_codes[1][0], v_scales[1][0], v_grp[1][0])
        inv = placed("inv", AT_V[1] + 4096, (P, 1))
        nc.vector.reciprocal(inv[:], total[:])
        quantise(v_codes[1][1], v_scales[1][1], v_grp[1][1])

        for e in range(2):
            y_ps = banks.tile([P, P], F32, name="y_ps", tag="head", bufs=2)
            for h in range(2):
                nc.tensor.matmul_mx(
                    out=y_ps[:],
                    lhsT=w_codes[h].bitcast(FP8X4),
                    lhsT_scale=w_scales[h],
                    rhs=v_codes[e][h].bitcast(FP8X4),
                    rhs_scale=v_scales[e][h],
                    start=(h == 0),
                    stop=(h == 1),
                )
            c = slice(e * P, (e + 1) * P)
            y_sb = keep.tile([P, P], F32, name=f"y_sb{e}", align_bytes=256)
            nc.vector.scalar_tensor_tensor(y_sb[:], y_ps[:], inv[:], gate[:, c], ALU.mult, ALU.mult)
            nc.sync.dma_start(out[0][:, c], y_sb[:])
